import numpy as np
import ml_dtypes


def mxq(x, axis, fmt="e4m3"):
    dtype, down = {"e4m3": (ml_dtypes.float8_e4m3fn, 7), "e5m2": (ml_dtypes.float8_e5m2, 14)}[fmt]
    v = np.moveaxis(np.asarray(x, np.float32).astype(ml_dtypes.bfloat16).astype(np.float64), axis, -1)
    blocks = v.reshape(v.shape[:-1] + (-1, 32))
    amax = np.abs(blocks).max(-1, keepdims=True)
    byte = np.maximum(np.where(amax > 0, np.frexp(amax)[1] - 1 + 127, 0) - down, 1)
    scale = np.exp2(byte - 127.0)
    codes = (blocks / scale).astype(np.float32).astype(dtype).astype(np.float64)
    return np.moveaxis((codes * scale).reshape(v.shape), -1, axis)


WIDE = False


def mx_kscale(k):
    if not WIDE:
        return np.ones(k)
    levels = np.array([10, -10, 5, -5, 0])
    if k % 512:
        return np.exp2(np.random.permutation(np.resize(levels, k // 32))).repeat(32)
    a = np.empty((k // 512, 16))
    for p in range(k // 512):
        a[p, :8] = np.random.permutation(np.resize(levels, 8))
        for g in range(8):
            far = levels[np.abs(levels - a[p, g]) >= 10]
            a[p, g + 8] = far[np.random.randint(len(far))]
    return np.exp2(a.ravel()).repeat(32)


def f64(x):
    return np.asarray(x).astype(np.float64)


def striped(idx):
    return np.tile(idx.reshape(-1, 16).T, (8, 1)).astype(np.uint16)


def unstriped(offs):
    return offs[:16].T.reshape(-1).astype(np.int64)


E2M1 = np.array([0.0, 0.5, 1.0, 1.5, 2.0, 3.0, 4.0, 6.0, -0.0, -0.5, -1.0, -1.5, -2.0, -3.0, -4.0, -6.0])


def pack_weight(w, fmt):
    k, n = w.shape
    w = f64(np.asarray(w, np.float32).astype(ml_dtypes.bfloat16)).reshape(k // 32, 32, n)
    amax = np.abs(w).max(1)
    if fmt == "e4m3":
        byte = np.frexp(amax)[1] - 1 + 127 - 7
    else:
        mant, ex = np.frexp(amax / 6.0)
        byte = np.where(mant > 0.5, ex, ex - 1) + 127
    byte = np.clip(np.where(amax > 0, byte, 1), 1, 254)
    scaled = (w * np.exp2(127.0 - byte)[:, None, :]).reshape(k, n).astype(np.float32)
    by_word = np.ascontiguousarray(scaled.reshape(k // 512, 128, 4, n).transpose(0, 1, 3, 2))
    if fmt == "e4m3":
        words = by_word.astype(ml_dtypes.float8_e4m3fn).view(np.uint8)
    else:
        c = by_word.astype(ml_dtypes.float4_e2m1fn).view(np.uint8) & 0xF
        words = (c[..., 0::2] | (c[..., 1::2] << 4)).reshape(k // 512, 128, 2 * n)
    return np.ascontiguousarray(words), np.ascontiguousarray(byte.astype(np.uint8).reshape(k // 512, 16, n))


def unpack_weight(words, scales, fmt):
    g, _, n = scales.shape
    words = np.ascontiguousarray(words).reshape(g, 128, n, -1)
    if fmt == "e4m3":
        vals = words.view(ml_dtypes.float8_e4m3fn).astype(np.float64)
    else:
        nib = np.empty((g, 128, n, 4), np.uint8)
        nib[..., 0::2] = words & 0xF
        nib[..., 1::2] = words >> 4
        vals = E2M1[nib]
    vals = vals * np.repeat(np.exp2(scales.astype(np.float64) - 127.0), 8, axis=1)[..., None]
    return vals.transpose(0, 1, 3, 2).reshape(g * 512, n)


def d_relu2(v):
    return 2.0 * np.maximum(v, 0.0)


K, T, E, C, H, N = 256, 512, 6, 256, 512, 512
TOP = 3


def by_expert(wq, xq):
    return np.concatenate([wq[e].T @ xq[:, e * C:(e + 1) * C] for e in range(E)], axis=1)


def setup_inputs():
    n = np.random.standard_normal
    s = mx_kscale(N)[:, None]
    u = mx_kscale(H)
    deal = np.repeat(np.arange(E), C).reshape(TOP, T)[:, np.random.permutation(T)]
    deal = np.take_along_axis(deal, np.argsort(np.random.rand(TOP, T), axis=0), axis=0)
    for _ in range(8):
        s_, t_ = np.random.permutation(T).reshape(2, -1); r = np.random.randint(TOP, size=T // 2); x, y = deal[r, s_].copy(), deal[r, t_].copy()
        ok = ~((deal[:, s_] == y).any(0) | (deal[:, t_] == x).any(0)); deal[r[ok], s_[ok]] = y[ok]; deal[r[ok], t_[ok]] = x[ok]
    order = np.lexsort((np.random.rand(TOP * T), deal.reshape(-1)))
    slot_token = order % T; pos = np.empty(TOP * T, np.int64); pos[order] = np.arange(TOP * T); pos = pos.reshape(TOP, T)
    g = np.random.uniform(0.5, 1.5, (TOP, T)); g = g / g.sum(0)
    w_slot = np.empty(E * C)
    for r in range(TOP): w_slot[pos[r]] = g[r]
    w2 = [pack_weight(m, "e2m1") for m in n((E, N, H)) / np.sqrt(N) / s[None] * u[None, None, :]]
    w1 = [pack_weight(m, "e2m1") for m in n((E, H, K)) / np.sqrt(H) / u[None, :, None]]
    return {
        "dyT": (n((N, T)) * s).astype(np.float32),
        "a": n((H, E * C)).astype(np.float32),
        "w2_words": np.stack([m[0] for m in w2]),
        "w2_scales": np.stack([m[1] for m in w2]),
        "w1_words": np.stack([m[0] for m in w1]),
        "w1_scales": np.stack([m[1] for m in w1]),
        "gate": np.tile(w_slot, (N, 1)).astype(np.float32),
        "offs": striped(slot_token),
        "pos1": striped(pos[0]),
        "pos2": striped(pos[1]),
        "pos3": striped(pos[2]),
    }


def reference(dyT, a, w2_words, w2_scales, w1_words, w1_scales, gate, offs, pos1, pos2, pos3):
    idx = unstriped(offs)
    w2 = np.stack([unpack_weight(w2_words[e], w2_scales[e], "e2m1") for e in range(E)])
    w1 = np.stack([unpack_weight(w1_words[e], w1_scales[e], "e2m1") for e in range(E)])
    gq = mxq(f64(gate) * f64(dyT)[:, idx], 0, "e4m3")
    dh = by_expert(w2, gq)
    da = dh * d_relu2(f64(a))
    dx = by_expert(w1, mxq(da, 0, "e4m3"))
    return dx[:, unstriped(pos1)] + dx[:, unstriped(pos2)] + dx[:, unstriped(pos3)]

@@ -1,0 +1,200 @@
+from contextlib import ExitStack
+
+import concourse.mybir as mybir
+from concourse.masks import make_identity
+
+K, T, E, C, H, N = 256, 512, 6, 256, 512, 512
+S = E * C
+P = 128
+PACK = 4
+FLOPS = 2 * S * H * (N + K)
+BYTES = 4 * (N * T + H * S + S + K * T) + E * (N * H + H * K) // 2 + E * (N * H + H * K) // 32 + 2 * (S + 3 * T)
+
+F32 = mybir.dt.float32
+BF16 = mybir.dt.bfloat16
+I32 = mybir.dt.int32
+U32 = mybir.dt.uint32
+U16 = mybir.dt.uint16
+U8 = mybir.dt.uint8
+FP8X4 = mybir.dt.float8_e4m3fn_x4
+FP4X4 = mybir.dt.float4_e2m1fn_x4
+ALU = mybir.AluOpType
+ACT = mybir.ActivationFunctionType
+
+
+def tile_moe_bdx_mlp_relu2_kernel(
+    tc, dyT, a, w2_words, w2_scales, w1_words, w1_scales, gate, offs, pos1, pos2, pos3, out
+):
+    nc = tc.nc
+    with ExitStack() as ctx:
+        keep = ctx.enter_context(tc.tile_pool(name="keep", bufs=1))
+        ps_dh = ctx.enter_context(tc.psum_pool(name="ps_dh", bufs=2))
+        ps_tr = ctx.enter_context(tc.psum_pool(name="ps_tr", bufs=4))
+        ps_dx = ctx.enter_context(tc.psum_pool(name="ps_dx", bufs=2))
+
+        def tile(shape, dtype, name):
+            return keep.tile(shape, dtype, name=name, align_bytes=64)
+
+        offs_sb = keep.tile([P, S // 16], U16, name="offs_sb")
+        pos_sb = [keep.tile([P, T // 16], U16, name="pos_sb%d" % r) for r in range(3)]
+        dy = [tile([P, T], F32, "dy%d" % t) for t in range(PACK)]
+        gate_cuts = [(0, 1), (1, 2), (2, E)]
+        gate_sb = tile([P, S], F32, "gate_sb")
+        w2 = tile([P, E, 2 * H], U8, "w2")
+        w1 = tile([P, E, 2 * K], U8, "w1")
+        s2 = tile([P, E, H], U8, "s2")
+        s1 = tile([P, E, K], U8, "s1")
+        a_sb = [tile([P, PACK, C], F32, "a%d" % e) for e in range(E)]
+        ident = tile([P, P], F32, "ident")
+
+        nc.vector.memset(s2[:].bitcast(I32), 0)
+        nc.vector.memset(s1[:].bitcast(I32), 0)
+        make_identity(nc, ident[:])
+
+        dy_rows = dyT.rearrange("(p t) c -> p t c", t=PACK)
+        a_rows = a.rearrange("(p t) s -> p t s", t=PACK)
+
+        def load_gate(e0, e1):
+            nc.sync.dma_start(out=gate_sb[:, e0 * C : e1 * C], in_=gate[0:P, e0 * C : e1 * C])
+
+        def load_scales(dst, src):
+            for q in range(4):
+                nc.sync.dma_start(
+                    out=dst[32 * q : 32 * q + 4].bitcast(I32),
+                    in_=src[:, 0, 4 * q : 4 * q + 4, :].rearrange("e r n -> r e n").bitcast(I32),
+                )
+
+        def load_words(dst, src, e0, e1):
+            nc.sync.dma_start(
+                out=dst[:, e0:e1].bitcast(I32),
+                in_=src[e0:e1, 0].rearrange("e p n -> p e n").bitcast(I32),
+            )
+
+        def load_a(e):
+            nc.sync.dma_start(out=a_sb[e][:], in_=a_rows[:, :, e * C : (e + 1) * C])
+
+        nc.sync.dma_start(offs_sb[:], offs)
+        load_gate(*gate_cuts[0])
+        for t in range(PACK):
+            nc.sync.dma_start(out=dy[t][:], in_=dy_rows[:, t, :])
+        load_gate(*gate_cuts[1])
+        load_scales(s2, w2_scales)
+        load_words(w2, w2_words, 0, 2)
+        load_gate(*gate_cuts[2])
+        load_words(w2, w2_words, 2, E)
+        load_a(0)
+        load_a(1)
+        load_scales(s1, w1_scales)
+        load_words(w1, w1_words, 0, E)
+        for e in range(2, E):
+            load_a(e)
+        for r, pos in enumerate((pos1, pos2, pos3)):
+            nc.sync.dma_start(pos_sb[r][:], pos)
+
+        g32 = [tile([P, PACK, C], F32, "g32_%d" % e) for e in range(E)]
+        g16 = [tile([P, C, PACK], BF16, "g16_%d" % e) for e in range(E)]
+        gq = [tile([P, C], U32, "gq%d" % e) for e in range(E)]
+        gs = [tile([P, C], U8, "gs%d" % e) for e in range(E)]
+        dhT = [tile([P, PACK, P], F32, "dhT%d" % b) for b in range(2 * E)]
+        da16 = [tile([P, C, PACK], BF16, "da16_%d" % e) for e in range(E)]
+        dq = [tile([P, C], U32, "dq%d" % e) for e in range(E)]
+        ds = [tile([P, C], U8, "ds%d" % e) for e in range(E)]
+        dx = tile([P, 2, S], F32, "dx")
+
+        for e in range(E):
+            for t in range(PACK):
+                nc.vector.tensor_tensor(
+                    g32[e][:, t, :],
+                    dy[t][:].indirect(offs_sb[:, e * C // 16 : (e + 1) * C // 16]),
+                    gate_sb[:, e * C : (e + 1) * C],
+                    ALU.mult,
+                )
+            nc.scalar.copy(
+                out=g16[e][:].rearrange("p (c i) t -> p c t i", i=2),
+                in_=g32[e][:].rearrange("p t (c i) -> p c t i", i=2),
+            )
+            nc.vector.quantize_mx(
+                out=gq[e][:].bitcast(FP8X4), scales=gs[e][:], in_=g16[e][:].rearrange("p c t -> p (c t)")
+            )
+            for j in range(2):
+                acc = ps_dh.tile([P, H], F32, name="acc_dh")
+                nc.tensor.matmul_mx(
+                    out=acc[:],
+                    lhsT=gq[e][:, j * P : (j + 1) * P].bitcast(FP8X4),
+                    lhsT_scale=gs[e][:, j * P : (j + 1) * P],
+                    rhs=w2[:, e, :].bitcast(FP4X4),
+                    rhs_scale=s2[:, e, :],
+                    start=True,
+                    stop=True,
+                )
+                nc.scalar.activation(
+                    out=dhT[2 * e + j][:],
+                    in_=acc[:].rearrange("s (m t) -> s t m", t=PACK),
+                    func=ACT.Copy,
+                    scale=2.0,
+                )
+
+        def make_da(b):
+            e, j = divmod(b, 2)
+            tr = ps_tr.tile([P, PACK, P], F32, name="tr")
+            for t in range(PACK):
+                nc.tensor.transpose(tr[:, t, :], dhT[b][:, t, :], ident[:])
+            nc.vector.scalar_tensor_tensor(
+                out=da16[e][:, j * P : (j + 1) * P, :],
+                in0=a_sb[e][:, :, j * P : (j + 1) * P].rearrange("p t s -> p s t"),
+                scalar=0.0,
+                in1=tr[:].rearrange("p t s -> p s t"),
+                op0=ALU.max,
+                op1=ALU.mult,
+            )
+
+        def second_product(e, c0, c1):
+            nc.vector.quantize_mx(
+                out=dq[e][:, c0:c1].bitcast(FP8X4),
+                scales=ds[e][:, c0:c1],
+                in_=da16[e][:, c0:c1, :].rearrange("p c t -> p (c t)"),
+            )
+            acc = ps_dx.tile([P, 2, C], F32, name="acc_dx")
+            for h in range(2):
+                nc.tensor.matmul_mx(
+                    out=acc[:, h, c0:c1],
+                    lhsT=w1[:, e, 2 * h * P : 2 * (h + 1) * P].bitcast(FP4X4),
+                    lhsT_scale=s1[:, e, h * P : (h + 1) * P],
+                    rhs=dq[e][:, c0:c1].bitcast(FP8X4),
+                    rhs_scale=ds[e][:, c0:c1],
+                    start=True,
+                    stop=True,
+                )
+            nc.scalar.copy(out=dx[:, :, e * C + c0 : e * C + c1], in_=acc[:, :, c0:c1])
+
+        for e in range(E):
+            make_da(2 * e)
+            if e > 0:
+                second_product(e - 1, 0, C)
+            make_da(2 * e + 1)
+        second_product(E - 1, 0, P)
+        second_product(E - 1, P, C)
+
+        got = [[tile([P, T], F32, "got%d_%d" % (h, r)) for r in range(3)] for h in range(2)]
+        part = [tile([P, T], F32, "part%d" % h) for h in range(2)]
+        res = [tile([P, T], F32, "res%d" % h) for h in range(2)]
+
+        def fetch(h, r, c0, c1):
+            nc.vector.tensor_copy(got[h][r][:, c0:c1], dx[:, h, :].indirect(pos_sb[r][:, c0 // 16 : c1 // 16]))
+
+        def finish(h, c0, c1):
+            nc.vector.tensor_tensor(res[h][:, c0:c1], part[h][:, c0:c1], got[h][2][:, c0:c1], ALU.add)
+            nc.sync.dma_start(out=out[h * P : (h + 1) * P, c0:c1], in_=res[h][:, c0:c1])
+
+        fetch(0, 0, 0, T)
+        fetch(0, 1, 0, T)
+        fetch(0, 2, 0, T)
+        nc.vector.tensor_tensor(part[0][:], got[0][0][:], got[0][1][:], ALU.add)
+        fetch(1, 0, 0, T)
+        finish(0, 0, T)
+        fetch(1, 1, 0, T)
+        fetch(1, 2, 0, T // 2)
+        nc.vector.tensor_tensor(part[1][:], got[1][0][:], got[1][1][:], ALU.add)
+        fetch(1, 2, T // 2, T)
+        finish(1, 0, T // 2)
+        finish(1, T // 2, T)

@@ -28,17 +28,16 @@ def tile_moe_bdx_mlp_relu2_kernel(
     nc = tc.nc
     with ExitStack() as ctx:
         keep = ctx.enter_context(tc.tile_pool(name="keep", bufs=1))
-        ps_dh = ctx.enter_context(tc.psum_pool(name="ps_dh", bufs=2))
-        ps_tr = ctx.enter_context(tc.psum_pool(name="ps_tr", bufs=4))
+        ps_dh = ctx.enter_context(tc.psum_pool(name="ps_dh", bufs=1))
+        ps_tr = ctx.enter_context(tc.psum_pool(name="ps_tr", bufs=6))
         ps_dx = ctx.enter_context(tc.psum_pool(name="ps_dx", bufs=2))
 
-        def tile(shape, dtype, name):
-            return keep.tile(shape, dtype, name=name, align_bytes=64)
+        def tile(shape, dtype, name, tag=None):
+            return keep.tile(shape, dtype, name=name, tag=tag or name, align_bytes=64)
 
         offs_sb = keep.tile([P, S // 16], U16, name="offs_sb")
         pos_sb = [keep.tile([P, T // 16], U16, name="pos_sb%d" % r) for r in range(3)]
         dy = [tile([P, T], F32, "dy%d" % t) for t in range(PACK)]
-        gate_cuts = [(0, 1), (1, 2), (2, E)]
         gate_sb = tile([P, S], F32, "gate_sb")
         w2 = tile([P, E, 2 * H], U8, "w2")
         w1 = tile([P, E, 2 * K], U8, "w1")
@@ -46,10 +45,13 @@ def tile_moe_bdx_mlp_relu2_kernel(
         s1 = tile([P, E, K], U8, "s1")
         a_sb = [tile([P, PACK, C], F32, "a%d" % e) for e in range(E)]
         ident = tile([P, P], F32, "ident")
+        ident0 = tile([P, P], F32, "ident0")
+        dx = tile([P, 2, S], F32, "dx")
 
         nc.vector.memset(s2[:].bitcast(I32), 0)
         nc.vector.memset(s1[:].bitcast(I32), 0)
-        make_identity(nc, ident[:])
+        make_identity(nc, ident0[:])
+        nc.scalar.copy(out=ident[:], in_=ident0[:])
 
         dy_rows = dyT.rearrange("(p t) c -> p t c", t=PACK)
         a_rows = a.rearrange("(p t) s -> p t s", t=PACK)
@@ -57,11 +59,11 @@ def tile_moe_bdx_mlp_relu2_kernel(
         def load_gate(e0, e1):
             nc.sync.dma_start(out=gate_sb[:, e0 * C : e1 * C], in_=gate[0:P, e0 * C : e1 * C])
 
-        def load_scales(dst, src):
+        def load_scales(dst, src, e0, e1, queue):
             for q in range(4):
-                nc.sync.dma_start(
-                    out=dst[32 * q : 32 * q + 4].bitcast(I32),
-                    in_=src[:, 0, 4 * q : 4 * q + 4, :].rearrange("e r n -> r e n").bitcast(I32),
+                queue.dma_start(
+                    out=dst[32 * q : 32 * q + 4, e0:e1].bitcast(I32),
+                    in_=src[e0:e1, 0, 4 * q : 4 * q + 4, :].rearrange("e r n -> r e n").bitcast(I32),
                 )
 
         def load_words(dst, src, e0, e1):
@@ -74,49 +76,64 @@ def tile_moe_bdx_mlp_relu2_kernel(
             nc.sync.dma_start(out=a_sb[e][:], in_=a_rows[:, :, e * C : (e + 1) * C])
 
         nc.sync.dma_start(offs_sb[:], offs)
-        load_gate(*gate_cuts[0])
-        for t in range(PACK):
-            nc.sync.dma_start(out=dy[t][:], in_=dy_rows[:, t, :])
-        load_gate(*gate_cuts[1])
-        load_scales(s2, w2_scales)
-        load_words(w2, w2_words, 0, 2)
-        load_gate(*gate_cuts[2])
-        load_words(w2, w2_words, 2, E)
+        load_scales(s1, w1_scales, 0, 6, nc.gpsimd)
+        load_gate(0, 1)
+        nc.sync.dma_start(out=dy[0][:], in_=dy_rows[:, 0, :])
+        nc.sync.dma_start(out=dy[1][:], in_=dy_rows[:, 1, :])
+        nc.sync.dma_start(out=dy[2][:], in_=dy_rows[:, 2, :])
+        nc.sync.dma_start(out=dy[3][:], in_=dy_rows[:, 3, :])
+        load_gate(1, 3)
+        load_scales(s2, w2_scales, 0, 6, nc.sync)
+        load_words(w2, w2_words, 0, 3)
+        load_gate(3, 6)
         load_a(0)
+        load_words(w2, w2_words, 3, 6)
         load_a(1)
-        load_scales(s1, w1_scales)
-        load_words(w1, w1_words, 0, E)
-        for e in range(2, E):
-            load_a(e)
+        load_words(w1, w1_words, 0, 6)
+        load_a(2)
+        load_a(3)
+        load_a(4)
+        load_a(5)
         for r, pos in enumerate((pos1, pos2, pos3)):
             nc.sync.dma_start(pos_sb[r][:], pos)
 
-        g32 = [tile([P, PACK, C], F32, "g32_%d" % e) for e in range(E)]
-        g16 = [tile([P, C, PACK], BF16, "g16_%d" % e) for e in range(E)]
-        gq = [tile([P, C], U32, "gq%d" % e) for e in range(E)]
-        gs = [tile([P, C], U8, "gs%d" % e) for e in range(E)]
-        dhT = [tile([P, PACK, P], F32, "dhT%d" % b) for b in range(2 * E)]
-        da16 = [tile([P, C, PACK], BF16, "da16_%d" % e) for e in range(E)]
-        dq = [tile([P, C], U32, "dq%d" % e) for e in range(E)]
-        ds = [tile([P, C], U8, "ds%d" % e) for e in range(E)]
-        dx = tile([P, 2, S], F32, "dx")
+        g32, g16, gq, gs, dhT, da16, dq, ds, relu2a = {}, {}, {}, {}, {}, {}, {}, {}, {}
+        TAGS = {}
+        REUSE = {2: -1, 3: -2, 4: -3, 5: -4}
 
-        for e in range(E):
+        def made(store, key, shape, dtype, name):
+            if key not in store:
+                store[key] = tile(shape, dtype, name, TAGS.get(name))
+            return store[key]
+
+        def by_fours(ap, order):
+            return ap.rearrange(order + " -> p c t i", i=4)
+
+        def gather(e, c0, c1):
+            if e in REUSE:
+                g32[e] = a_sb[REUSE[e]] if REUSE[e] >= 0 else g32[-1 - REUSE[e]]
+            made(g32, e, [P, PACK, C], F32, "g32_%d" % e)
             for t in range(PACK):
                 nc.vector.tensor_tensor(
-                    g32[e][:, t, :],
-                    dy[t][:].indirect(offs_sb[:, e * C // 16 : (e + 1) * C // 16]),
-                    gate_sb[:, e * C : (e + 1) * C],
+                    g32[e][:, t, c0:c1],
+                    dy[t][:].indirect(offs_sb[:, (e * C + c0) // 16 : (e * C + c1) // 16]),
+                    gate_sb[:, e * C + c0 : e * C + c1],
                     ALU.mult,
                 )
+            made(g16, e, [P, C, PACK], BF16, "g16_%d" % e)
             nc.scalar.copy(
-                out=g16[e][:].rearrange("p (c i) t -> p c t i", i=2),
-                in_=g32[e][:].rearrange("p t (c i) -> p c t i", i=2),
+                out=by_fours(g16[e][:, c0:c1, :], "p (c i) t"), in_=by_fours(g32[e][:, :, c0:c1], "p t (c i)")
             )
+
+        def first_product(e, c0, c1):
+            made(gq, e, [P, C], U32, "gq%d" % e)
+            made(gs, e, [P, C], U8, "gs%d" % e)
             nc.vector.quantize_mx(
-                out=gq[e][:].bitcast(FP8X4), scales=gs[e][:], in_=g16[e][:].rearrange("p c t -> p (c t)")
+                out=gq[e][:, c0:c1].bitcast(FP8X4),
+                scales=gs[e][:, c0:c1],
+                in_=g16[e][:, c0:c1, :].rearrange("p c t -> p (c t)"),
             )
-            for j in range(2):
+            for j in range(c0 // P, c1 // P):
                 acc = ps_dh.tile([P, H], F32, name="acc_dh")
                 nc.tensor.matmul_mx(
                     out=acc[:],
@@ -127,28 +144,81 @@ def tile_moe_bdx_mlp_relu2_kernel(
                     start=True,
                     stop=True,
                 )
+                made(dhT, (e, j), [P, PACK, P], F32, "dhT%d_%d" % (e, j))
                 nc.scalar.activation(
-                    out=dhT[2 * e + j][:],
+                    out=dhT[e, j][:],
                     in_=acc[:].rearrange("s (m t) -> s t m", t=PACK),
                     func=ACT.Copy,
                     scale=2.0,
                 )
 
-        def make_da(b):
-            e, j = divmod(b, 2)
-            tr = ps_tr.tile([P, PACK, P], F32, name="tr")
-            for t in range(PACK):
-                nc.tensor.transpose(tr[:, t, :], dhT[b][:, t, :], ident[:])
-            nc.vector.scalar_tensor_tensor(
-                out=da16[e][:, j * P : (j + 1) * P, :],
-                in0=a_sb[e][:, :, j * P : (j + 1) * P].rearrange("p t s -> p s t"),
-                scalar=0.0,
-                in1=tr[:].rearrange("p t s -> p s t"),
-                op0=ALU.max,
-                op1=ALU.mult,
+        w2p = tile([P, E, PACK, P], U16, "w2p")
+        s2p = tile([P, E, PACK, P], U8, "s2p")
+        banks = {}
+
+        def permute_words(e0, e1):
+            nc.vector.tensor_copy(
+                w2p[:, e0:e1], w2[:, e0:e1].bitcast(U16).rearrange("p e (m t) -> p e t m", t=PACK)
             )
 
+        def permute_scales(e0, e1):
+            nc.vector.tensor_copy(s2p[:, e0:e1], s2[:, e0:e1].rearrange("p e (m t) -> p e t m", t=PACK))
+
+        def first_direct(e, c0, c1):
+            made(gq, e, [P, C], U32, "gq%d" % e)
+            made(gs, e, [P, C], U8, "gs%d" % e)
+            nc.vector.quantize_mx(
+                out=gq[e][:, c0:c1].bitcast(FP8X4),
+                scales=gs[e][:, c0:c1],
+                in_=g16[e][:, c0:c1, :].rearrange("p c t -> p (c t)"),
+            )
+            for j in range(c0 // P, c1 // P):
+                banks[e, j] = ps_tr.tile([P, PACK, P], F32, name="tr")
+                for t in range(PACK):
+                    nc.tensor.matmul_mx(
+                        out=banks[e, j][:, t, :],
+                        lhsT=w2p[:, e, t, :].bitcast(FP4X4),
+                        lhsT_scale=s2p[:, e, t, :],
+                        rhs=gq[e][:, j * P : (j + 1) * P].bitcast(FP8X4),
+                        rhs_scale=gs[e][:, j * P : (j + 1) * P],
+                        start=True,
+                        stop=True,
+                    )
+
+        def make_relu(e, j):
+            if e in [0, 1, 2, 3, 4, 5]:
+                made(relu2a, (e, j), [P, PACK, P], F32, "relu%d_%d" % (e, j))
+                nc.scalar.activation(out=relu2a[e, j][:], in_=a_sb[e][:, :, j * P : (j + 1) * P], func=ACT.Relu, scale=2.0 if e in [0, 1, 2, 3, 4, 5] else 1.0)
+
+        def make_da(e, j):
+            cols = slice(j * P, (j + 1) * P)
+            if (e, j) in banks:
+                tr = banks[e, j]
+            else:
+                tr = ps_tr.tile([P, PACK, P], F32, name="tr")
+                for t in range(PACK):
+                    nc.tensor.transpose(tr[:, t, :], dhT[e, j][:, t, :], ident[:])
+            made(da16, e, [P, C, PACK], BF16, "da16_%d" % e)
+            if e in [0, 1, 2, 3, 4, 5]:
+                nc.vector.tensor_tensor(
+                    by_fours(da16[e][:, cols, :], "p (c i) t"),
+                    by_fours(tr[:], "p t (c i)"),
+                    by_fours(relu2a[e, j][:], "p t (c i)"),
+                    ALU.mult,
+                )
+            else:
+                nc.vector.scalar_tensor_tensor(
+                    out=da16[e][:, cols, :],
+                    in0=a_sb[e][:, :, cols].rearrange("p t s -> p s t"),
+                    scalar=0.0,
+                    in1=tr[:].rearrange("p t s -> p s t"),
+                    op0=ALU.max,
+                    op1=ALU.mult,
+                )
+
         def second_product(e, c0, c1):
+            made(dq, e, [P, C], U32, "dq%d" % e)
+            made(ds, e, [P, C], U8, "ds%d" % e)
             nc.vector.quantize_mx(
                 out=dq[e][:, c0:c1].bitcast(FP8X4),
                 scales=ds[e][:, c0:c1],
@@ -167,34 +237,92 @@ def tile_moe_bdx_mlp_relu2_kernel(
                 )
             nc.scalar.copy(out=dx[:, :, e * C + c0 : e * C + c1], in_=acc[:, :, c0:c1])
 
-        for e in range(E):
-            make_da(2 * e)
-            if e > 0:
-                second_product(e - 1, 0, C)
-            make_da(2 * e + 1)
-        second_product(E - 1, 0, P)
-        second_product(E - 1, P, C)
+        gather(0, 0, C)
+        permute_scales(0, 6)
+        permute_words(0, 2)
+        first_direct(0, 0, C)
+        gather(1, 0, C)
+        first_direct(1, 0, C)
+        gather(2, 0, C)
+        permute_words(2, 4)
+        first_direct(2, 0, C)
+        gather(3, 0, C)
+        make_relu(0, 0)
+        make_relu(0, 1)
+        make_da(0, 0)
+        make_da(0, 1)
+        first_direct(3, 0, C)
+        gather(4, 0, C)
+        permute_words(4, 6)
+        make_relu(1, 0)
+        make_relu(1, 1)
+        make_da(1, 0)
+        second_product(0, 0, C)
+        make_da(1, 1)
+        first_direct(4, 0, C)
+        gather(5, 0, P)
+        gather(5, P, C)
+        make_relu(2, 0)
+        make_relu(2, 1)
+        make_da(2, 0)
+        second_product(1, 0, C)
+        make_da(2, 1)
+        first_direct(5, 0, P)
+        first_direct(5, P, C)
+        make_relu(3, 0)
+        make_relu(3, 1)
+        make_da(3, 0)
+        second_product(2, 0, C)
+        make_da(3, 1)
+        make_relu(4, 0)
+        make_relu(4, 1)
+        make_da(4, 0)
+        second_product(3, 0, C)
+        make_da(4, 1)
+        make_relu(5, 0)
+        make_relu(5, 1)
+        make_da(5, 0)
+        second_product(4, 0, C)
+        make_da(5, 1)
+        second_product(5, 0, P)
+        second_product(5, P, C)
 
-        got = [[tile([P, T], F32, "got%d_%d" % (h, r)) for r in range(3)] for h in range(2)]
-        part = [tile([P, T], F32, "part%d" % h) for h in range(2)]
+        got = [[tile([P, T], F32, "got%d_%d" % (h, r)) for r in range(2)] for h in range(2)]
+        third = tile([P, T], F32, "third")
         res = [tile([P, T], F32, "res%d" % h) for h in range(2)]
+        pair = {}
 
-        def fetch(h, r, c0, c1):
-            nc.vector.tensor_copy(got[h][r][:, c0:c1], dx[:, h, :].indirect(pos_sb[r][:, c0 // 16 : c1 // 16]))
+        def fetch(dst, h, r, c0, c1):
+            nc.vector.tensor_copy(dst[:, c0:c1], dx[:, h, :].indirect(pos_sb[r][:, c0 // 16 : c1 // 16]))
 
-        def finish(h, c0, c1):
-            nc.vector.tensor_tensor(res[h][:, c0:c1], part[h][:, c0:c1], got[h][2][:, c0:c1], ALU.add)
-            nc.sync.dma_start(out=out[h * P : (h + 1) * P, c0:c1], in_=res[h][:, c0:c1])
+        def add_pair(h, u):
+            turned = ps_tr.tile([P, 2, P], F32, name="tr")
+            for b in range(2):
+                cols = slice((2 * u + b) * P, (2 * u + b + 1) * P)
+                for r in range(2):
+                    nc.tensor.matmul(
+                        turned[:, b, :], got[h][r][:, cols], ident[:], start=r == 0, stop=r == 1, is_transpose=True
+                    )
+            turned_sb = tile([P, 2, P], F32, "turned%d_%d" % (h, u))
+            nc.scalar.copy(out=turned_sb[:], in_=turned[:])
+            pair[h, u] = ps_tr.tile([P, 2, P], F32, name="tr")
+            for b in range(2):
+                nc.tensor.transpose(pair[h, u][:, b, :], turned_sb[:, b, :], ident[:])
 
-        fetch(0, 0, 0, T)
-        fetch(0, 1, 0, T)
-        fetch(0, 2, 0, T)
-        nc.vector.tensor_tensor(part[0][:], got[0][0][:], got[0][1][:], ALU.add)
-        fetch(1, 0, 0, T)
-        finish(0, 0, T)
-        fetch(1, 1, 0, T)
-        fetch(1, 2, 0, T // 2)
-        nc.vector.tensor_tensor(part[1][:], got[1][0][:], got[1][1][:], ALU.add)
-        fetch(1, 2, T // 2, T)
-        finish(1, 0, T // 2)
-        finish(1, T // 2, T)
+        def finish(h, u):
+            cols = slice(2 * u * P, 2 * (u + 1) * P)
+            nc.vector.tensor_tensor(
+                res[h][:, cols], pair[h, u][:].rearrange("p b c -> p (b c)"), third[:, cols], ALU.add
+            )
+            nc.sync.dma_start(out=out[h * P : (h + 1) * P, cols], in_=res[h][:, cols])
+
+        for h in range(2):
+            fetch(got[h][0], h, 0, 0, T)
+            fetch(got[h][1], h, 1, 0, T)
+            add_pair(h, 0)
+            add_pair(h, 1)
+        for h in range(2):
+            fetch(third, h, 2, 0, T // 2)
+            fetch(third, h, 2, T // 2, T)
+            finish(h, 0)
+            finish(h, 1)

@@ -28,8 +28,8 @@ def tile_moe_bdx_mlp_relu2_kernel(
     nc = tc.nc
     with ExitStack() as ctx:
         keep = ctx.enter_context(tc.tile_pool(name="keep", bufs=1))
-        ps_dh = ctx.enter_context(tc.psum_pool(name="ps_dh", bufs=1))
-        ps_tr = ctx.enter_context(tc.psum_pool(name="ps_tr", bufs=6))
+        ps_dh = ctx.enter_context(tc.psum_pool(name="ps_dh", bufs=2))
+        ps_tr = ctx.enter_context(tc.psum_pool(name="ps_tr", bufs=4))
         ps_dx = ctx.enter_context(tc.psum_pool(name="ps_dx", bufs=2))
 
         def tile(shape, dtype, name, tag=None):
@@ -37,19 +37,22 @@ def tile_moe_bdx_mlp_relu2_kernel(
 
         offs_sb = keep.tile([P, S // 16], U16, name="offs_sb")
         pos_sb = [keep.tile([P, T // 16], U16, name="pos_sb%d" % r) for r in range(3)]
-        dy = [tile([P, T], F32, "dy%d" % t) for t in range(PACK)]
+        dy = [tile([P, T + 16], F32, "dy%d" % t) for t in range(PACK)]
         gate_sb = tile([P, S], F32, "gate_sb")
         w2 = tile([P, E, 2 * H], U8, "w2")
         w1 = tile([P, E, 2 * K], U8, "w1")
         s2 = tile([P, E, H], U8, "s2")
         s1 = tile([P, E, K], U8, "s1")
-        a_sb = [tile([P, PACK, C], F32, "a%d" % e) for e in range(E)]
+        a_pair = [tile([P, PACK, 2 * C], F32, "a%d" % e) for e in range(E // 2)]
+        a_sb = [a_pair[e // 2][:, :, (e % 2) * C : (e % 2 + 1) * C] for e in range(E)]
         ident = tile([P, P], F32, "ident")
         ident0 = tile([P, P], F32, "ident0")
         dx = tile([P, 2, S], F32, "dx")
 
         nc.vector.memset(s2[:].bitcast(I32), 0)
         nc.vector.memset(s1[:].bitcast(I32), 0)
+        for t in range(PACK):
+            nc.gpsimd.memset(dy[t][:, T:], 0.0)
         make_identity(nc, ident0[:])
         nc.scalar.copy(out=ident[:], in_=ident0[:])
 
@@ -73,15 +76,18 @@ def tile_moe_bdx_mlp_relu2_kernel(
             )
 
         def load_a(e):
-            nc.sync.dma_start(out=a_sb[e][:], in_=a_rows[:, :, e * C : (e + 1) * C])
+            nc.sync.dma_start(out=a_sb[e], in_=a_rows[:, :, e * C : (e + 1) * C])
+
+        def load_a_pair(e):
+            nc.sync.dma_start(out=a_pair[e // 2][:], in_=a_rows[:, :, e * C : (e + 2) * C])
 
         nc.sync.dma_start(offs_sb[:], offs)
         load_scales(s1, w1_scales, 0, 6, nc.gpsimd)
         load_gate(0, 1)
-        nc.sync.dma_start(out=dy[0][:], in_=dy_rows[:, 0, :])
-        nc.sync.dma_start(out=dy[1][:], in_=dy_rows[:, 1, :])
-        nc.sync.dma_start(out=dy[2][:], in_=dy_rows[:, 2, :])
-        nc.sync.dma_start(out=dy[3][:], in_=dy_rows[:, 3, :])
+        nc.sync.dma_start(out=dy[0][:, 0:T], in_=dy_rows[:, 0, :])
+        nc.sync.dma_start(out=dy[1][:, 0:T], in_=dy_rows[:, 1, :])
+        nc.sync.dma_start(out=dy[2][:, 0:T], in_=dy_rows[:, 2, :])
+        nc.sync.dma_start(out=dy[3][:, 0:T], in_=dy_rows[:, 3, :])
         load_gate(1, 3)
         load_scales(s2, w2_scales, 0, 6, nc.sync)
         load_words(w2, w2_words, 0, 3)
@@ -99,7 +105,7 @@ def tile_moe_bdx_mlp_relu2_kernel(
 
         g32, g16, gq, gs, dhT, da16, dq, ds, relu2a = {}, {}, {}, {}, {}, {}, {}, {}, {}
         TAGS = {}
-        REUSE = {2: -1, 3: -2, 4: -3, 5: -4}
+        REUSE = {0: (0, 0), 1: (1, 0), 2: (0, 0), 4: (1, 0)}
 
         def made(store, key, shape, dtype, name):
             if key not in store:
@@ -110,20 +116,23 @@ def tile_moe_bdx_mlp_relu2_kernel(
             return ap.rearrange(order + " -> p c t i", i=4)
 
         def gather(e, c0, c1):
-            if e in REUSE:
-                g32[e] = a_sb[REUSE[e]] if REUSE[e] >= 0 else g32[-1 - REUSE[e]]
-            made(g32, e, [P, PACK, C], F32, "g32_%d" % e)
+            b, off = REUSE[e]
+            buf = made(g32, b, [P, PACK, 2 * C], F32, "g32_%d" % b)
             for t in range(PACK):
                 nc.vector.tensor_tensor(
-                    g32[e][:, t, c0:c1],
+                    buf[:, t, off + c0 : off + c1],
                     dy[t][:].indirect(offs_sb[:, (e * C + c0) // 16 : (e * C + c1) // 16]),
                     gate_sb[:, e * C + c0 : e * C + c1],
                     ALU.mult,
                 )
-            made(g16, e, [P, C, PACK], BF16, "g16_%d" % e)
-            nc.scalar.copy(
-                out=by_fours(g16[e][:, c0:c1, :], "p (c i) t"), in_=by_fours(g32[e][:, :, c0:c1], "p t (c i)")
-            )
+            for d0 in range(c0, c1, C):
+                d1 = min(c1, d0 + C)
+                x = e + d0 // C
+                made(g16, x, [P, C, PACK], BF16, "g16_%d" % x)
+                nc.scalar.copy(
+                    out=by_fours(g16[x][:, d0 % C : (d1 - 1) % C + 1, :], "p (c i) t"),
+                    in_=by_fours(buf[:, :, off + d0 : off + d1], "p t (c i)"),
+                )
 
         def first_product(e, c0, c1):
             made(gq, e, [P, C], U32, "gq%d" % e)
@@ -186,9 +195,9 @@ def tile_moe_bdx_mlp_relu2_kernel(
                     )
 
         def make_relu(e, j):
-            if e in [0, 1, 2, 3, 4, 5]:
+            if e in [4, 5]:
                 made(relu2a, (e, j), [P, PACK, P], F32, "relu%d_%d" % (e, j))
-                nc.scalar.activation(out=relu2a[e, j][:], in_=a_sb[e][:, :, j * P : (j + 1) * P], func=ACT.Relu, scale=2.0 if e in [0, 1, 2, 3, 4, 5] else 1.0)
+                nc.scalar.activation(out=relu2a[e, j][:], in_=a_sb[e][:, :, j * P : (j + 1) * P], func=ACT.Relu, scale=2.0 if e in [4, 5] else 1.0)
 
         def make_da(e, j):
             cols = slice(j * P, (j + 1) * P)
@@ -199,7 +208,7 @@ def tile_moe_bdx_mlp_relu2_kernel(
                 for t in range(PACK):
                     nc.tensor.transpose(tr[:, t, :], dhT[e, j][:, t, :], ident[:])
             made(da16, e, [P, C, PACK], BF16, "da16_%d" % e)
-            if e in [0, 1, 2, 3, 4, 5]:
+            if e in [4, 5]:
                 nc.vector.tensor_tensor(
                     by_fours(da16[e][:, cols, :], "p (c i) t"),
                     by_fours(tr[:], "p t (c i)"),
@@ -238,42 +247,36 @@ def tile_moe_bdx_mlp_relu2_kernel(
             nc.scalar.copy(out=dx[:, :, e * C + c0 : e * C + c1], in_=acc[:, :, c0:c1])
 
         gather(0, 0, C)
-        permute_scales(0, 6)
-        permute_words(0, 2)
-        first_direct(0, 0, C)
+        first_product(0, 0, C)
         gather(1, 0, C)
-        first_direct(1, 0, C)
-        gather(2, 0, C)
-        permute_words(2, 4)
-        first_direct(2, 0, C)
-        gather(3, 0, C)
+        first_product(1, 0, C)
+        gather(2, 0, 2 * C)
         make_relu(0, 0)
         make_relu(0, 1)
         make_da(0, 0)
         make_da(0, 1)
-        first_direct(3, 0, C)
-        gather(4, 0, C)
+        first_product(2, 0, C)
+        first_product(3, 0, C)
+        gather(4, 0, 2 * C)
+        permute_scales(4, 6)
         permute_words(4, 6)
         make_relu(1, 0)
         make_relu(1, 1)
         make_da(1, 0)
         second_product(0, 0, C)
         make_da(1, 1)
-        first_direct(4, 0, C)
-        gather(5, 0, P)
-        gather(5, P, C)
         make_relu(2, 0)
         make_relu(2, 1)
         make_da(2, 0)
         second_product(1, 0, C)
         make_da(2, 1)
-        first_direct(5, 0, P)
-        first_direct(5, P, C)
         make_relu(3, 0)
         make_relu(3, 1)
         make_da(3, 0)
         second_product(2, 0, C)
         make_da(3, 1)
+        first_direct(4, 0, C)
+        first_direct(5, 0, C)
         make_relu(4, 0)
         make_relu(4, 1)
         make_da(4, 0)

@@ -50,10 +50,10 @@ def tile_moe_bdx_mlp_relu2_kernel(
         dx = tile([P, 2, S], F32, "dx")
 
         nc.vector.memset(s2[:].bitcast(I32), 0)
-        nc.vector.memset(s1[:].bitcast(I32), 0)
         for t in range(PACK):
             nc.gpsimd.memset(dy[t][:, T:], 0.0)
         make_identity(nc, ident0[:])
+        nc.gpsimd.memset(s1[:], 0)
         nc.scalar.copy(out=ident[:], in_=ident0[:])
 
         dy_rows = dyT.rearrange("(p t) c -> p t c", t=PACK)
@@ -90,22 +90,21 @@ def tile_moe_bdx_mlp_relu2_kernel(
         nc.sync.dma_start(out=dy[3][:, 0:T], in_=dy_rows[:, 3, :])
         load_gate(1, 3)
         load_scales(s2, w2_scales, 0, 6, nc.sync)
-        load_words(w2, w2_words, 0, 3)
-        load_gate(3, 6)
+        load_gate(3, 5)
+        load_words(w2, w2_words, 0, 2)
         load_a(0)
-        load_words(w2, w2_words, 3, 6)
+        load_gate(5, 6)
+        load_words(w2, w2_words, 2, 6)
+        load_a_pair(2)
         load_a(1)
         load_words(w1, w1_words, 0, 6)
-        load_a(2)
-        load_a(3)
-        load_a(4)
-        load_a(5)
+        load_a_pair(4)
         for r, pos in enumerate((pos1, pos2, pos3)):
             nc.sync.dma_start(pos_sb[r][:], pos)
 
         g32, g16, gq, gs, dhT, da16, dq, ds, relu2a = {}, {}, {}, {}, {}, {}, {}, {}, {}
         TAGS = {}
-        REUSE = {0: (0, 0), 1: (1, 0), 2: (0, 0), 4: (1, 0)}
+        REUSE = {0: (2, 0), 1: (3, 0), 3: (0, 0), 5: (1, 0)}
 
         def made(store, key, shape, dtype, name):
             if key not in store:
@@ -195,9 +194,9 @@ def tile_moe_bdx_mlp_relu2_kernel(
                     )
 
         def make_relu(e, j):
-            if e in [4, 5]:
+            if e in [0, 1, 3, 4, 5]:
                 made(relu2a, (e, j), [P, PACK, P], F32, "relu%d_%d" % (e, j))
-                nc.scalar.activation(out=relu2a[e, j][:], in_=a_sb[e][:, :, j * P : (j + 1) * P], func=ACT.Relu, scale=2.0 if e in [4, 5] else 1.0)
+                nc.scalar.activation(out=relu2a[e, j][:], in_=a_sb[e][:, :, j * P : (j + 1) * P], func=ACT.Relu, scale=2.0 if e in [3, 4, 5] else 1.0)
 
         def make_da(e, j):
             cols = slice(j * P, (j + 1) * P)
@@ -208,7 +207,7 @@ def tile_moe_bdx_mlp_relu2_kernel(
                 for t in range(PACK):
                     nc.tensor.transpose(tr[:, t, :], dhT[e, j][:, t, :], ident[:])
             made(da16, e, [P, C, PACK], BF16, "da16_%d" % e)
-            if e in [4, 5]:
+            if e in [0, 1, 3, 4, 5]:
                 nc.vector.tensor_tensor(
                     by_fours(da16[e][:, cols, :], "p (c i) t"),
                     by_fours(tr[:], "p t (c i)"),
@@ -224,6 +223,25 @@ def tile_moe_bdx_mlp_relu2_kernel(
                     op0=ALU.max,
                     op1=ALU.mult,
                 )
+
+        def last_product(e, c0, c1):
+            nc.vector.quantize_mx(
+                out=dq[e][:, c0:c1].bitcast(FP8X4),
+                scales=ds[e][:, c0:c1],
+                in_=da16[e][:, c0:c1, :].rearrange("p c t -> p (c t)"),
+            )
+            for h in range(2):
+                acc = ps_tr.tile([P, c1 - c0], F32, name="tr")
+                nc.tensor.matmul_mx(
+                    out=acc[:],
+                    lhsT=w1[:, e, 2 * h * P : 2 * (h + 1) * P].bitcast(FP4X4),
+                    lhsT_scale=s1[:, e, h * P : (h + 1) * P],
+                    rhs=dq[e][:, c0:c1].bitcast(FP8X4),
+                    rhs_scale=ds[e][:, c0:c1],
+                    start=True,
+                    stop=True,
+                )
+                nc.scalar.copy(out=dx[:, h, e * C + c0 : e * C + c1], in_=acc[:])
 
         def second_product(e, c0, c1):
             made(dq, e, [P, C], U32, "dq%d" % e)
@@ -246,86 +264,74 @@ def tile_moe_bdx_mlp_relu2_kernel(
                 )
             nc.scalar.copy(out=dx[:, :, e * C + c0 : e * C + c1], in_=acc[:, :, c0:c1])
 
+        permute_scales(3, 4)
         gather(0, 0, C)
         first_product(0, 0, C)
-        gather(1, 0, C)
+        gather(1, 0, 2 * C)
         first_product(1, 0, C)
-        gather(2, 0, 2 * C)
-        make_relu(0, 0)
-        make_relu(0, 1)
-        make_da(0, 0)
-        make_da(0, 1)
-        first_product(2, 0, C)
-        first_product(3, 0, C)
-        gather(4, 0, 2 * C)
-        permute_scales(4, 6)
-        permute_words(4, 6)
         make_relu(1, 0)
-        make_relu(1, 1)
-        make_da(1, 0)
-        second_product(0, 0, C)
-        make_da(1, 1)
         make_relu(2, 0)
-        make_relu(2, 1)
-        make_da(2, 0)
-        second_product(1, 0, C)
-        make_da(2, 1)
-        make_relu(3, 0)
-        make_relu(3, 1)
-        make_da(3, 0)
-        second_product(2, 0, C)
-        make_da(3, 1)
-        first_direct(4, 0, C)
-        first_direct(5, 0, C)
+        gather(3, 0, 2 * C)
+        make_relu(0, 1)
+        permute_words(3, 4)
+        first_product(2, 0, C)
+        permute_scales(4, 6)
+        make_relu(0, 0)
+        permute_words(4, 6)
+        make_da(0, 1)
+        make_da(1, 0)
+        make_relu(1, 1)
+        make_da(0, 0)
         make_relu(4, 0)
         make_relu(4, 1)
+        make_da(1, 1)
+        gather(5, 0, C)
+        first_direct(3, 0, C)
+        second_product(1, 0, C)
+        second_product(0, 0, C)
+        make_relu(2, 1)
+        make_relu(3, 0)
+        make_relu(3, 1)
+        make_da(2, 0)
+        make_da(2, 1)
+        first_direct(4, 0, C)
         make_da(4, 0)
+        make_da(3, 1)
+        first_direct(5, 0, C)
+        make_da(3, 0)
+        second_product(2, 0, C)
+        make_relu(5, 0)
         second_product(3, 0, C)
         make_da(4, 1)
-        make_relu(5, 0)
-        make_relu(5, 1)
-        make_da(5, 0)
         second_product(4, 0, C)
+        make_da(5, 0)
+        make_relu(5, 1)
         make_da(5, 1)
         second_product(5, 0, P)
-        second_product(5, P, C)
+        last_product(5, P, C)
 
         got = [[tile([P, T], F32, "got%d_%d" % (h, r)) for r in range(2)] for h in range(2)]
-        third = tile([P, T], F32, "third")
+        third = [tile([P, T], F32, "third%d" % h) for h in range(2)]
+        pair = [tile([P, T], F32, "pair%d" % h) for h in range(2)]
         res = [tile([P, T], F32, "res%d" % h) for h in range(2)]
-        pair = {}
+        halves = [slice(0, T // 2), slice(T // 2, T)]
 
-        def fetch(dst, h, r, c0, c1):
-            nc.vector.tensor_copy(dst[:, c0:c1], dx[:, h, :].indirect(pos_sb[r][:, c0 // 16 : c1 // 16]))
+        def fetch(dst, h, r, cols):
+            nc.vector.tensor_copy(dst[:, cols], dx[:, h, :].indirect(pos_sb[r][:, cols.start // 16 : cols.stop // 16]))
 
-        def add_pair(h, u):
-            turned = ps_tr.tile([P, 2, P], F32, name="tr")
-            for b in range(2):
-                cols = slice((2 * u + b) * P, (2 * u + b + 1) * P)
-                for r in range(2):
-                    nc.tensor.matmul(
-                        turned[:, b, :], got[h][r][:, cols], ident[:], start=r == 0, stop=r == 1, is_transpose=True
-                    )
-            turned_sb = tile([P, 2, P], F32, "turned%d_%d" % (h, u))
-            nc.scalar.copy(out=turned_sb[:], in_=turned[:])
-            pair[h, u] = ps_tr.tile([P, 2, P], F32, name="tr")
-            for b in range(2):
-                nc.tensor.transpose(pair[h, u][:, b, :], turned_sb[:, b, :], ident[:])
+        for h in range(2):
+            fetch(got[h][0], h, 0, slice(0, T))
+            fetch(got[h][1], h, 1, slice(0, T))
+            for cols in halves:
+                nc.gpsimd.tensor_tensor(pair[h][:, cols], got[h][0][:, cols], got[h][1][:, cols], ALU.add)
 
-        def finish(h, u):
-            cols = slice(2 * u * P, 2 * (u + 1) * P)
-            nc.vector.tensor_tensor(
-                res[h][:, cols], pair[h, u][:].rearrange("p b c -> p (b c)"), third[:, cols], ALU.add
-            )
+        def finish(h, cols):
+            nc.vector.tensor_tensor(res[h][:, cols], pair[h][:, cols], third[h][:, cols], ALU.add)
             nc.sync.dma_start(out=out[h * P : (h + 1) * P, cols], in_=res[h][:, cols])
 
-        for h in range(2):
-            fetch(got[h][0], h, 0, 0, T)
-            fetch(got[h][1], h, 1, 0, T)
-            add_pair(h, 0)
-            add_pair(h, 1)
-        for h in range(2):
-            fetch(third, h, 2, 0, T // 2)
-            fetch(third, h, 2, T // 2, T)
-            finish(h, 0)
-            finish(h, 1)
+        fetch(third[0], 0, 2, slice(0, T))
+        fetch(third[1], 1, 2, halves[0])
+        finish(0, slice(0, T))
+        fetch(third[1], 1, 2, halves[1])
+        finish(1, halves[0])
+        finish(1, halves[1])

@@ -7,8 +7,13 @@ K, T, E, C, H, N = 256, 512, 6, 256, 512, 512
 S = E * C
 P = 128
 PACK = 4
+TOP = 3
+PER_COLUMN = 16
 FLOPS = 2 * S * H * (N + K)
-BYTES = 4 * (N * T + H * S + S + K * T) + E * (N * H + H * K) // 2 + E * (N * H + H * K) // 32 + 2 * (S + 3 * T)
+BYTES = 4 * (N * T + H * S + S + K * T) + E * H * (N + K) // 2 + E * H * (N + K) // 32 + 2 * (S + TOP * T)
+
+PAD = 16
+FIRST_PERMUTED = 3
 
 F32 = mybir.dt.float32
 BF16 = mybir.dt.bfloat16
@@ -28,46 +33,48 @@ def tile_moe_bdx_mlp_relu2_kernel(
     nc = tc.nc
     with ExitStack() as ctx:
         keep = ctx.enter_context(tc.tile_pool(name="keep", bufs=1))
-        ps_dh = ctx.enter_context(tc.psum_pool(name="ps_dh", bufs=2))
-        ps_tr = ctx.enter_context(tc.psum_pool(name="ps_tr", bufs=4))
-        ps_dx = ctx.enter_context(tc.psum_pool(name="ps_dx", bufs=2))
+        psum_rows = ctx.enter_context(tc.psum_pool(name="psum_rows", bufs=2))
+        psum_planes = ctx.enter_context(tc.psum_pool(name="psum_planes", bufs=4))
+        psum_dx = ctx.enter_context(tc.psum_pool(name="psum_dx", bufs=2))
 
-        def tile(shape, dtype, name, tag=None):
-            return keep.tile(shape, dtype, name=name, tag=tag or name, align_bytes=64)
+        def tile(shape, dtype, name):
+            return keep.tile(shape, dtype, name=name, align_bytes=64)
 
-        offs_sb = keep.tile([P, S // 16], U16, name="offs_sb")
-        pos_sb = [keep.tile([P, T // 16], U16, name="pos_sb%d" % r) for r in range(3)]
-        dy = [tile([P, T + 16], F32, "dy%d" % t) for t in range(PACK)]
+        def tiles(count, shape, dtype, name):
+            return [tile(shape, dtype, "%s%d" % (name, x)) for x in range(count)]
+
+        offs_sb = keep.tile([P, S // PER_COLUMN], U16, name="offs_sb")
+        pos_sb = [keep.tile([P, T // PER_COLUMN], U16, name="pos_sb%d" % r) for r in range(TOP)]
+        dy = tiles(PACK, [P, T + PAD], F32, "dy")
         gate_sb = tile([P, S], F32, "gate_sb")
         w2 = tile([P, E, 2 * H], U8, "w2")
         w1 = tile([P, E, 2 * K], U8, "w1")
         s2 = tile([P, E, H], U8, "s2")
         s1 = tile([P, E, K], U8, "s1")
-        a_pair = [tile([P, PACK, 2 * C], F32, "a%d" % e) for e in range(E // 2)]
-        a_sb = [a_pair[e // 2][:, :, (e % 2) * C : (e % 2 + 1) * C] for e in range(E)]
+        a_pair = tiles(E // 2, [P, PACK, 2 * C], F32, "a_pair")
+        ident_made = tile([P, P], F32, "ident_made")
         ident = tile([P, P], F32, "ident")
-        ident0 = tile([P, P], F32, "ident0")
-        dx = tile([P, 2, S], F32, "dx")
+        dx = tile([P, K // P, S], F32, "dx")
 
         nc.vector.memset(s2[:].bitcast(I32), 0)
-        for t in range(PACK):
-            nc.gpsimd.memset(dy[t][:, T:], 0.0)
-        make_identity(nc, ident0[:])
+        for d in range(PACK):
+            nc.gpsimd.memset(dy[d][:, T:], 0.0)
+        make_identity(nc, ident_made[:])
         nc.gpsimd.memset(s1[:], 0)
-        nc.scalar.copy(out=ident[:], in_=ident0[:])
+        nc.scalar.copy(out=ident[:], in_=ident_made[:])
 
-        dy_rows = dyT.rearrange("(p t) c -> p t c", t=PACK)
-        a_rows = a.rearrange("(p t) s -> p t s", t=PACK)
+        dy_planes = dyT.rearrange("(p d) c -> p d c", d=PACK)
+        a_planes = a.rearrange("(p d) s -> p d s", d=PACK)
 
         def load_gate(e0, e1):
             nc.sync.dma_start(out=gate_sb[:, e0 * C : e1 * C], in_=gate[0:P, e0 * C : e1 * C])
 
-        def load_scales(dst, src, e0, e1, queue):
-            for q in range(4):
-                queue.dma_start(
-                    out=dst[32 * q : 32 * q + 4, e0:e1].bitcast(I32),
-                    in_=src[e0:e1, 0, 4 * q : 4 * q + 4, :].rearrange("e r n -> r e n").bitcast(I32),
-                )
+        def a_slots(first, count):
+            start = first % (2 * C)
+            return a_pair[first // (2 * C)][:, :, start : start + count]
+
+        def load_a(e0, e1):
+            nc.sync.dma_start(out=a_slots(e0 * C, (e1 - e0) * C), in_=a_planes[:, :, e0 * C : e1 * C])
 
         def load_words(dst, src, e0, e1):
             nc.sync.dma_start(
@@ -75,263 +82,227 @@ def tile_moe_bdx_mlp_relu2_kernel(
                 in_=src[e0:e1, 0].rearrange("e p n -> p e n").bitcast(I32),
             )
 
-        def load_a(e):
-            nc.sync.dma_start(out=a_sb[e], in_=a_rows[:, :, e * C : (e + 1) * C])
-
-        def load_a_pair(e):
-            nc.sync.dma_start(out=a_pair[e // 2][:], in_=a_rows[:, :, e * C : (e + 2) * C])
+        def load_scales(queue, dst, src):
+            for q in range(4):
+                queue.dma_start(
+                    out=dst[32 * q : 32 * q + 4].bitcast(I32),
+                    in_=src[:, 0, 4 * q : 4 * q + 4, :].rearrange("e r n -> r e n").bitcast(I32),
+                )
 
         nc.sync.dma_start(offs_sb[:], offs)
-        load_scales(s1, w1_scales, 0, 6, nc.gpsimd)
+        load_scales(nc.gpsimd, s1, w1_scales)
         load_gate(0, 1)
-        nc.sync.dma_start(out=dy[0][:, 0:T], in_=dy_rows[:, 0, :])
-        nc.sync.dma_start(out=dy[1][:, 0:T], in_=dy_rows[:, 1, :])
-        nc.sync.dma_start(out=dy[2][:, 0:T], in_=dy_rows[:, 2, :])
-        nc.sync.dma_start(out=dy[3][:, 0:T], in_=dy_rows[:, 3, :])
+        for d in range(PACK):
+            nc.sync.dma_start(out=dy[d][:, 0:T], in_=dy_planes[:, d, :])
         load_gate(1, 3)
-        load_scales(s2, w2_scales, 0, 6, nc.sync)
+        load_scales(nc.sync, s2, w2_scales)
         load_gate(3, 5)
-        load_words(w2, w2_words, 0, 2)
-        load_a(0)
         load_gate(5, 6)
-        load_words(w2, w2_words, 2, 6)
-        load_a_pair(2)
-        load_a(1)
-        load_words(w1, w1_words, 0, 6)
-        load_a_pair(4)
+        load_words(w2, w2_words, 0, 2)
+        load_a(0, 1)
+        load_a(1, 2)
+        load_words(w2, w2_words, 2, E)
+        load_words(w1, w1_words, 0, E)
+        load_a(2, 4)
+        load_a(4, 6)
         for r, pos in enumerate((pos1, pos2, pos3)):
             nc.sync.dma_start(pos_sb[r][:], pos)
 
-        g32, g16, gq, gs, dhT, da16, dq, ds, relu2a = {}, {}, {}, {}, {}, {}, {}, {}, {}
-        TAGS = {}
-        REUSE = {0: (2, 0), 1: (3, 0), 3: (0, 0), 5: (1, 0)}
+        g_single = tile([P, PACK, C], F32, "g_single")
+        g16 = tiles(E, [P, C, PACK], BF16, "g16_")
+        g_codes = tiles(E, [P, C], U32, "g_codes")
+        g_scales = tiles(E, [P, C], U8, "g_scales")
+        dh_rows = tiles(2 * FIRST_PERMUTED, [P, PACK, P], F32, "dh_rows")
+        w2_regrouped = tile([P, E - FIRST_PERMUTED, PACK, P], U16, "w2_regrouped")
+        s2_regrouped = tile([P, E - FIRST_PERMUTED, PACK, P], U8, "s2_regrouped")
+        slope = tiles(2 * E, [P, PACK, P], F32, "slope")
+        da16 = tiles(E, [P, C, PACK], BF16, "da16_")
+        da_codes = tiles(E, [P, C], U32, "da_codes")
+        da_scales = tiles(E, [P, C], U8, "da_scales")
+        dh_planes = {}
 
-        def made(store, key, shape, dtype, name):
-            if key not in store:
-                store[key] = tile(shape, dtype, name, TAGS.get(name))
-            return store[key]
+        def from_planes(ap):
+            return ap.rearrange("p d (c i) -> p c d i", i=4)
 
-        def by_fours(ap, order):
-            return ap.rearrange(order + " -> p c t i", i=4)
+        def side_by_side(ap):
+            return ap.rearrange("p (c i) d -> p c d i", i=4)
 
-        def gather(e, c0, c1):
-            b, off = REUSE[e]
-            buf = made(g32, b, [P, PACK, 2 * C], F32, "g32_%d" % b)
-            for t in range(PACK):
+        def quantize(codes, scales, values):
+            nc.vector.quantize_mx(out=codes.bitcast(FP8X4), scales=scales, in_=values.rearrange("p c d -> p (c d)"))
+
+        def one_pass(acc, stationary, stationary_scales, moving, moving_scales):
+            nc.tensor.matmul_mx(
+                out=acc,
+                lhsT=stationary,
+                lhsT_scale=stationary_scales,
+                rhs=moving,
+                rhs_scale=moving_scales,
+                start=True,
+                stop=True,
+            )
+
+        def gather(e0, e1):
+            g32 = g_single if e1 - e0 == 1 else tile([P, PACK, (e1 - e0) * C], F32, "g_double%d" % e0)
+            entries = offs_sb[:, e0 * C // PER_COLUMN : e1 * C // PER_COLUMN]
+            for d in range(PACK):
                 nc.vector.tensor_tensor(
-                    buf[:, t, off + c0 : off + c1],
-                    dy[t][:].indirect(offs_sb[:, (e * C + c0) // 16 : (e * C + c1) // 16]),
-                    gate_sb[:, e * C + c0 : e * C + c1],
-                    ALU.mult,
+                    g32[:, d, :], dy[d][:].indirect(entries), gate_sb[:, e0 * C : e1 * C], ALU.mult
                 )
-            for d0 in range(c0, c1, C):
-                d1 = min(c1, d0 + C)
-                x = e + d0 // C
-                made(g16, x, [P, C, PACK], BF16, "g16_%d" % x)
+            for e in range(e0, e1):
                 nc.scalar.copy(
-                    out=by_fours(g16[x][:, d0 % C : (d1 - 1) % C + 1, :], "p (c i) t"),
-                    in_=by_fours(buf[:, :, off + d0 : off + d1], "p t (c i)"),
+                    out=side_by_side(g16[e][:]), in_=from_planes(g32[:, :, (e - e0) * C : (e - e0 + 1) * C])
                 )
 
-        def first_product(e, c0, c1):
-            made(gq, e, [P, C], U32, "gq%d" % e)
-            made(gs, e, [P, C], U8, "gs%d" % e)
-            nc.vector.quantize_mx(
-                out=gq[e][:, c0:c1].bitcast(FP8X4),
-                scales=gs[e][:, c0:c1],
-                in_=g16[e][:, c0:c1, :].rearrange("p c t -> p (c t)"),
-            )
-            for j in range(c0 // P, c1 // P):
-                acc = ps_dh.tile([P, H], F32, name="acc_dh")
-                nc.tensor.matmul_mx(
-                    out=acc[:],
-                    lhsT=gq[e][:, j * P : (j + 1) * P].bitcast(FP8X4),
-                    lhsT_scale=gs[e][:, j * P : (j + 1) * P],
-                    rhs=w2[:, e, :].bitcast(FP4X4),
-                    rhs_scale=s2[:, e, :],
-                    start=True,
-                    stop=True,
-                )
-                made(dhT, (e, j), [P, PACK, P], F32, "dhT%d_%d" % (e, j))
-                nc.scalar.activation(
-                    out=dhT[e, j][:],
-                    in_=acc[:].rearrange("s (m t) -> s t m", t=PACK),
-                    func=ACT.Copy,
-                    scale=2.0,
-                )
-
-        w2p = tile([P, E, PACK, P], U16, "w2p")
-        s2p = tile([P, E, PACK, P], U8, "s2p")
-        banks = {}
-
-        def permute_words(e0, e1):
+        def regroup_words(e0, e1):
             nc.vector.tensor_copy(
-                w2p[:, e0:e1], w2[:, e0:e1].bitcast(U16).rearrange("p e (m t) -> p e t m", t=PACK)
+                w2_regrouped[:, e0 - FIRST_PERMUTED : e1 - FIRST_PERMUTED],
+                w2[:, e0:e1].bitcast(U16).rearrange("p e (m d) -> p e d m", d=PACK),
             )
 
-        def permute_scales(e0, e1):
-            nc.vector.tensor_copy(s2p[:, e0:e1], s2[:, e0:e1].rearrange("p e (m t) -> p e t m", t=PACK))
-
-        def first_direct(e, c0, c1):
-            made(gq, e, [P, C], U32, "gq%d" % e)
-            made(gs, e, [P, C], U8, "gs%d" % e)
-            nc.vector.quantize_mx(
-                out=gq[e][:, c0:c1].bitcast(FP8X4),
-                scales=gs[e][:, c0:c1],
-                in_=g16[e][:, c0:c1, :].rearrange("p c t -> p (c t)"),
+        def regroup_scales(e0, e1):
+            nc.vector.tensor_copy(
+                s2_regrouped[:, e0 - FIRST_PERMUTED : e1 - FIRST_PERMUTED],
+                s2[:, e0:e1].rearrange("p e (m d) -> p e d m", d=PACK),
             )
-            for j in range(c0 // P, c1 // P):
-                banks[e, j] = ps_tr.tile([P, PACK, P], F32, name="tr")
-                for t in range(PACK):
-                    nc.tensor.matmul_mx(
-                        out=banks[e, j][:, t, :],
-                        lhsT=w2p[:, e, t, :].bitcast(FP4X4),
-                        lhsT_scale=s2p[:, e, t, :],
-                        rhs=gq[e][:, j * P : (j + 1) * P].bitcast(FP8X4),
-                        rhs_scale=gs[e][:, j * P : (j + 1) * P],
-                        start=True,
-                        stop=True,
-                    )
 
-        def make_relu(e, j):
-            if e in [0, 1, 3, 4, 5]:
-                made(relu2a, (e, j), [P, PACK, P], F32, "relu%d_%d" % (e, j))
-                nc.scalar.activation(out=relu2a[e, j][:], in_=a_sb[e][:, :, j * P : (j + 1) * P], func=ACT.Relu, scale=2.0 if e in [3, 4, 5] else 1.0)
+        def first_product(e):
+            quantize(g_codes[e][:], g_scales[e][:], g16[e][:])
+            for half in range(2):
+                codes = g_codes[e][:, half * P : (half + 1) * P].bitcast(FP8X4)
+                scales = g_scales[e][:, half * P : (half + 1) * P]
+                if e < FIRST_PERMUTED:
+                    acc = psum_rows.tile([P, H], F32, name="rows")
+                    one_pass(acc[:], codes, scales, w2[:, e, :].bitcast(FP4X4), s2[:, e, :])
+                    nc.scalar.copy(out=dh_rows[2 * e + half][:], in_=acc[:].rearrange("s (m d) -> s d m", d=PACK))
+                else:
+                    dh_planes[e, half] = psum_planes.tile([P, PACK, P], F32, name="planes")
+                    for d in range(PACK):
+                        one_pass(
+                            dh_planes[e, half][:, d, :],
+                            w2_regrouped[:, e - FIRST_PERMUTED, d, :].bitcast(FP4X4),
+                            s2_regrouped[:, e - FIRST_PERMUTED, d, :],
+                            codes,
+                            scales,
+                        )
 
-        def make_da(e, j):
-            cols = slice(j * P, (j + 1) * P)
-            if (e, j) in banks:
-                tr = banks[e, j]
+        def make_slope(e, half):
+            nc.scalar.activation(
+                out=slope[2 * e + half][:], in_=a_slots(e * C + half * P, P), func=ACT.Relu, scale=2.0
+            )
+
+        def make_da(e, half):
+            if e < FIRST_PERMUTED:
+                planes = psum_planes.tile([P, PACK, P], F32, name="planes")
+                for d in range(PACK):
+                    nc.tensor.transpose(planes[:, d, :], dh_rows[2 * e + half][:, d, :], ident[:])
             else:
-                tr = ps_tr.tile([P, PACK, P], F32, name="tr")
-                for t in range(PACK):
-                    nc.tensor.transpose(tr[:, t, :], dhT[e, j][:, t, :], ident[:])
-            made(da16, e, [P, C, PACK], BF16, "da16_%d" % e)
-            if e in [0, 1, 3, 4, 5]:
-                nc.vector.tensor_tensor(
-                    by_fours(da16[e][:, cols, :], "p (c i) t"),
-                    by_fours(tr[:], "p t (c i)"),
-                    by_fours(relu2a[e, j][:], "p t (c i)"),
-                    ALU.mult,
-                )
-            else:
-                nc.vector.scalar_tensor_tensor(
-                    out=da16[e][:, cols, :],
-                    in0=a_sb[e][:, :, cols].rearrange("p t s -> p s t"),
-                    scalar=0.0,
-                    in1=tr[:].rearrange("p t s -> p s t"),
-                    op0=ALU.max,
-                    op1=ALU.mult,
-                )
-
-        def last_product(e, c0, c1):
-            nc.vector.quantize_mx(
-                out=dq[e][:, c0:c1].bitcast(FP8X4),
-                scales=ds[e][:, c0:c1],
-                in_=da16[e][:, c0:c1, :].rearrange("p c t -> p (c t)"),
+                planes = dh_planes[e, half]
+            nc.vector.tensor_tensor(
+                side_by_side(da16[e][:, half * P : (half + 1) * P, :]),
+                from_planes(planes[:]),
+                from_planes(slope[2 * e + half][:]),
+                ALU.mult,
             )
-            for h in range(2):
-                acc = ps_tr.tile([P, c1 - c0], F32, name="tr")
-                nc.tensor.matmul_mx(
-                    out=acc[:],
-                    lhsT=w1[:, e, 2 * h * P : 2 * (h + 1) * P].bitcast(FP4X4),
-                    lhsT_scale=s1[:, e, h * P : (h + 1) * P],
-                    rhs=dq[e][:, c0:c1].bitcast(FP8X4),
-                    rhs_scale=ds[e][:, c0:c1],
-                    start=True,
-                    stop=True,
-                )
-                nc.scalar.copy(out=dx[:, h, e * C + c0 : e * C + c1], in_=acc[:])
 
-        def second_product(e, c0, c1):
-            made(dq, e, [P, C], U32, "dq%d" % e)
-            made(ds, e, [P, C], U8, "ds%d" % e)
-            nc.vector.quantize_mx(
-                out=dq[e][:, c0:c1].bitcast(FP8X4),
-                scales=ds[e][:, c0:c1],
-                in_=da16[e][:, c0:c1, :].rearrange("p c t -> p (c t)"),
+        def times_w1(acc, e, kh, c0, c1):
+            one_pass(
+                acc,
+                w1[:, e, 2 * kh * P : 2 * (kh + 1) * P].bitcast(FP4X4),
+                s1[:, e, kh * P : (kh + 1) * P],
+                da_codes[e][:, c0:c1].bitcast(FP8X4),
+                da_scales[e][:, c0:c1],
             )
-            acc = ps_dx.tile([P, 2, C], F32, name="acc_dx")
-            for h in range(2):
-                nc.tensor.matmul_mx(
-                    out=acc[:, h, c0:c1],
-                    lhsT=w1[:, e, 2 * h * P : 2 * (h + 1) * P].bitcast(FP4X4),
-                    lhsT_scale=s1[:, e, h * P : (h + 1) * P],
-                    rhs=dq[e][:, c0:c1].bitcast(FP8X4),
-                    rhs_scale=ds[e][:, c0:c1],
-                    start=True,
-                    stop=True,
-                )
+
+        def second_product(e, c0=0, c1=C):
+            quantize(da_codes[e][:, c0:c1], da_scales[e][:, c0:c1], da16[e][:, c0:c1, :])
+            acc = psum_dx.tile([P, K // P, C], F32, name="dx_sums")
+            for kh in range(K // P):
+                times_w1(acc[:, kh, c0:c1], e, kh, c0, c1)
             nc.scalar.copy(out=dx[:, :, e * C + c0 : e * C + c1], in_=acc[:, :, c0:c1])
 
-        permute_scales(3, 4)
-        gather(0, 0, C)
-        first_product(0, 0, C)
-        gather(1, 0, 2 * C)
-        first_product(1, 0, C)
-        make_relu(1, 0)
-        make_relu(2, 0)
-        gather(3, 0, 2 * C)
-        make_relu(0, 1)
-        permute_words(3, 4)
-        first_product(2, 0, C)
-        permute_scales(4, 6)
-        make_relu(0, 0)
-        permute_words(4, 6)
+        def last_second_product(e, c0, c1):
+            quantize(da_codes[e][:, c0:c1], da_scales[e][:, c0:c1], da16[e][:, c0:c1, :])
+            for kh in range(K // P):
+                acc = psum_planes.tile([P, c1 - c0], F32, name="planes")
+                times_w1(acc[:], e, kh, c0, c1)
+                nc.scalar.copy(out=dx[:, kh, e * C + c0 : e * C + c1], in_=acc[:])
+
+        gather(0, 1)
+        first_product(0)
+        gather(1, 3)
+        regroup_scales(3, 4)
+        make_slope(0, 1)
+        first_product(1)
+        make_slope(1, 0)
+        first_product(2)
+        gather(3, 5)
+        make_slope(3, 0)
         make_da(0, 1)
-        make_da(1, 0)
-        make_relu(1, 1)
+        regroup_scales(4, 6)
+        make_slope(0, 0)
+        regroup_words(3, 4)
         make_da(0, 0)
-        make_relu(4, 0)
-        make_relu(4, 1)
+        make_slope(1, 1)
+        make_slope(4, 1)
+        regroup_words(4, 6)
+        make_slope(2, 1)
+        make_da(1, 0)
+        make_slope(3, 1)
         make_da(1, 1)
-        gather(5, 0, C)
-        first_direct(3, 0, C)
-        second_product(1, 0, C)
-        second_product(0, 0, C)
-        make_relu(2, 1)
-        make_relu(3, 0)
-        make_relu(3, 1)
-        make_da(2, 0)
+        first_product(3)
         make_da(2, 1)
-        first_direct(4, 0, C)
-        make_da(4, 0)
-        make_da(3, 1)
-        first_direct(5, 0, C)
+        make_slope(4, 0)
+        gather(5, 6)
+        make_slope(2, 0)
+        second_product(1)
+        make_da(2, 0)
+        first_product(4)
+        second_product(0)
         make_da(3, 0)
-        second_product(2, 0, C)
-        make_relu(5, 0)
-        second_product(3, 0, C)
+        first_product(5)
         make_da(4, 1)
-        second_product(4, 0, C)
+        make_da(3, 1)
+        second_product(3)
+        make_slope(5, 0)
         make_da(5, 0)
-        make_relu(5, 1)
+        make_slope(5, 1)
         make_da(5, 1)
+        make_da(4, 0)
+        second_product(4)
         second_product(5, 0, P)
-        last_product(5, P, C)
+        last_second_product(5, P, C)
+        second_product(2)
 
-        got = [[tile([P, T], F32, "got%d_%d" % (h, r)) for r in range(2)] for h in range(2)]
-        third = [tile([P, T], F32, "third%d" % h) for h in range(2)]
-        pair = [tile([P, T], F32, "pair%d" % h) for h in range(2)]
-        res = [tile([P, T], F32, "res%d" % h) for h in range(2)]
-        halves = [slice(0, T // 2), slice(T // 2, T)]
+        fetched = [tiles(TOP, [P, T], F32, "fetched%d_" % kh) for kh in range(K // P)]
+        pair_sum = tiles(K // P, [P, T], F32, "pair_sum")
+        total = tiles(K // P, [P, T], F32, "total")
+        all_tokens = slice(0, T)
+        token_halves = [slice(0, T // 2), slice(T // 2, T)]
 
-        def fetch(dst, h, r, cols):
-            nc.vector.tensor_copy(dst[:, cols], dx[:, h, :].indirect(pos_sb[r][:, cols.start // 16 : cols.stop // 16]))
+        def fetch(kh, r, tokens):
+            entries = pos_sb[r][:, tokens.start // PER_COLUMN : tokens.stop // PER_COLUMN]
+            nc.vector.tensor_copy(fetched[kh][r][:, tokens], dx[:, kh, :].indirect(entries))
 
-        for h in range(2):
-            fetch(got[h][0], h, 0, slice(0, T))
-            fetch(got[h][1], h, 1, slice(0, T))
-            for cols in halves:
-                nc.gpsimd.tensor_tensor(pair[h][:, cols], got[h][0][:, cols], got[h][1][:, cols], ALU.add)
+        def add_pair(kh, tokens):
+            nc.gpsimd.tensor_tensor(
+                pair_sum[kh][:, tokens], fetched[kh][0][:, tokens], fetched[kh][1][:, tokens], ALU.add
+            )
 
-        def finish(h, cols):
-            nc.vector.tensor_tensor(res[h][:, cols], pair[h][:, cols], third[h][:, cols], ALU.add)
-            nc.sync.dma_start(out=out[h * P : (h + 1) * P, cols], in_=res[h][:, cols])
+        def finish(engine, kh, tokens):
+            engine.tensor_tensor(total[kh][:, tokens], pair_sum[kh][:, tokens], fetched[kh][2][:, tokens], ALU.add)
+            nc.sync.dma_start(out=out[kh * P : (kh + 1) * P, tokens], in_=total[kh][:, tokens])
 
-        fetch(third[0], 0, 2, slice(0, T))
-        fetch(third[1], 1, 2, halves[0])
-        finish(0, slice(0, T))
-        fetch(third[1], 1, 2, halves[1])
-        finish(1, halves[0])
-        finish(1, halves[1])
+        for r in range(TOP):
+            fetch(0, r, all_tokens)
+        for tokens in token_halves:
+            add_pair(0, tokens)
+        for tokens in token_halves:
+            finish(nc.gpsimd, 0, tokens)
+        fetch(1, 0, all_tokens)
+        for tokens in token_halves:
+            fetch(1, 1, tokens)
+            add_pair(1, tokens)
+        for tokens in token_halves:
+            fetch(1, 2, tokens)
+        for tokens in token_halves:
+            finish(nc.vector, 1, tokens)

@@ -12,8 +12,7 @@ PER_COLUMN = 16
 FLOPS = 2 * S * H * (N + K)
 BYTES = 4 * (N * T + H * S + S + K * T) + E * H * (N + K) // 2 + E * H * (N + K) // 32 + 2 * (S + TOP * T)
 
-PAD = 16
-FIRST_PERMUTED = 3
+FUSED = 3
 
 F32 = mybir.dt.float32
 BF16 = mybir.dt.bfloat16
@@ -33,6 +32,7 @@ def tile_moe_bdx_mlp_relu2_kernel(
     nc = tc.nc
     with ExitStack() as ctx:
         keep = ctx.enter_context(tc.tile_pool(name="keep", bufs=1))
+        reuse = ctx.enter_context(tc.tile_pool(name="reuse", bufs=1))
         psum_rows = ctx.enter_context(tc.psum_pool(name="psum_rows", bufs=2))
         psum_planes = ctx.enter_context(tc.psum_pool(name="psum_planes", bufs=4))
         psum_dx = ctx.enter_context(tc.psum_pool(name="psum_dx", bufs=2))
@@ -43,9 +43,12 @@ def tile_moe_bdx_mlp_relu2_kernel(
         def tiles(count, shape, dtype, name):
             return [tile(shape, dtype, "%s%d" % (name, x)) for x in range(count)]
 
+        def shared(tag, shape, dtype, name):
+            return reuse.tile(shape, dtype, name=name, tag=tag, align_bytes=64)
+
         offs_sb = keep.tile([P, S // PER_COLUMN], U16, name="offs_sb")
         pos_sb = [keep.tile([P, T // PER_COLUMN], U16, name="pos_sb%d" % r) for r in range(TOP)]
-        dy = tiles(PACK, [P, T + PAD], F32, "dy")
+        dy = tiles(PACK, [P, T], F32, "dy")
         gate_sb = tile([P, S], F32, "gate_sb")
         w2 = tile([P, E, 2 * H], U8, "w2")
         w1 = tile([P, E, 2 * K], U8, "w1")
@@ -54,13 +57,11 @@ def tile_moe_bdx_mlp_relu2_kernel(
         a_pair = tiles(E // 2, [P, PACK, 2 * C], F32, "a_pair")
         ident_made = tile([P, P], F32, "ident_made")
         ident = tile([P, P], F32, "ident")
-        dx = tile([P, K // P, S], F32, "dx")
+        dx = tiles(K // P, [P, S], F32, "dx")
 
         nc.vector.memset(s2[:].bitcast(I32), 0)
-        for d in range(PACK):
-            nc.gpsimd.memset(dy[d][:, T:], 0.0)
+        nc.vector.memset(s1[:].bitcast(I32), 0)
         make_identity(nc, ident_made[:])
-        nc.gpsimd.memset(s1[:], 0)
         nc.scalar.copy(out=ident[:], in_=ident_made[:])
 
         dy_planes = dyT.rearrange("(p d) c -> p d c", d=PACK)
@@ -90,36 +91,30 @@ def tile_moe_bdx_mlp_relu2_kernel(
                 )
 
         nc.sync.dma_start(offs_sb[:], offs)
+        load_scales(nc.scalar, s2, w2_scales)
         load_scales(nc.gpsimd, s1, w1_scales)
         load_gate(0, 1)
         for d in range(PACK):
             nc.sync.dma_start(out=dy[d][:, 0:T], in_=dy_planes[:, d, :])
         load_gate(1, 3)
-        load_scales(nc.sync, s2, w2_scales)
-        load_gate(3, 5)
-        load_gate(5, 6)
-        load_words(w2, w2_words, 0, 2)
         load_a(0, 1)
+        load_words(w2, w2_words, 0, 2)
         load_a(1, 2)
+        load_gate(3, E)
         load_words(w2, w2_words, 2, E)
-        load_words(w1, w1_words, 0, E)
         load_a(2, 4)
+        load_words(w1, w1_words, 0, E)
         load_a(4, 6)
         for r, pos in enumerate((pos1, pos2, pos3)):
             nc.sync.dma_start(pos_sb[r][:], pos)
 
-        g_single = tile([P, PACK, C], F32, "g_single")
-        g16 = tiles(E, [P, C, PACK], BF16, "g16_")
+        g16 = [shared("half%d" % e, [P, C, PACK], BF16, "g16_%d" % e) for e in range(E)]
         g_codes = tiles(E, [P, C], U32, "g_codes")
         g_scales = tiles(E, [P, C], U8, "g_scales")
-        dh_rows = tiles(2 * FIRST_PERMUTED, [P, PACK, P], F32, "dh_rows")
-        w2_regrouped = tile([P, E - FIRST_PERMUTED, PACK, P], U16, "w2_regrouped")
-        s2_regrouped = tile([P, E - FIRST_PERMUTED, PACK, P], U8, "s2_regrouped")
-        slope = tiles(2 * E, [P, PACK, P], F32, "slope")
-        da16 = tiles(E, [P, C, PACK], BF16, "da16_")
-        da_codes = tiles(E, [P, C], U32, "da_codes")
-        da_scales = tiles(E, [P, C], U8, "da_scales")
-        dh_planes = {}
+        dh_rows = tiles(2 * E, [P, PACK, P], F32, "dh_rows")
+        slope = [shared("slope%d" % e, [P, 2, PACK, P], F32, "slope%d" % e) for e in range(FUSED)]
+        da_codes = tile([P, S], U32, "da_codes")
+        da_scales = tile([P, S], U8, "da_scales")
 
         def from_planes(ap):
             return ap.rearrange("p d (c i) -> p c d i", i=4)
@@ -141,168 +136,117 @@ def tile_moe_bdx_mlp_relu2_kernel(
                 stop=True,
             )
 
-        def gather(e0, e1):
-            g32 = g_single if e1 - e0 == 1 else tile([P, PACK, (e1 - e0) * C], F32, "g_double%d" % e0)
-            entries = offs_sb[:, e0 * C // PER_COLUMN : e1 * C // PER_COLUMN]
+        def entries_of(e0, e1):
+            return offs_sb[:, e0 * C // PER_COLUMN : e1 * C // PER_COLUMN]
+
+        def gather(e):
+            g32 = shared("ab"[e % 2] if e < 4 else "slope%d" % (e - 4), [P, PACK, C], F32, "g32_%d" % e)
             for d in range(PACK):
                 nc.vector.tensor_tensor(
-                    g32[:, d, :], dy[d][:].indirect(entries), gate_sb[:, e0 * C : e1 * C], ALU.mult
+                    g32[:, d, :], dy[d][:].indirect(entries_of(e, e + 1)), gate_sb[:, e * C : (e + 1) * C], ALU.mult
                 )
-            for e in range(e0, e1):
-                nc.scalar.copy(
-                    out=side_by_side(g16[e][:]), in_=from_planes(g32[:, :, (e - e0) * C : (e - e0 + 1) * C])
-                )
+            return g32
 
-        def regroup_words(e0, e1):
-            nc.vector.tensor_copy(
-                w2_regrouped[:, e0 - FIRST_PERMUTED : e1 - FIRST_PERMUTED],
-                w2[:, e0:e1].bitcast(U16).rearrange("p e (m d) -> p e d m", d=PACK),
-            )
-
-        def regroup_scales(e0, e1):
-            nc.vector.tensor_copy(
-                s2_regrouped[:, e0 - FIRST_PERMUTED : e1 - FIRST_PERMUTED],
-                s2[:, e0:e1].rearrange("p e (m d) -> p e d m", d=PACK),
-            )
+        def interleave(e, g32):
+            nc.scalar.copy(out=side_by_side(g16[e][:]), in_=from_planes(g32[:]))
 
         def first_product(e):
             quantize(g_codes[e][:], g_scales[e][:], g16[e][:])
             for half in range(2):
                 codes = g_codes[e][:, half * P : (half + 1) * P].bitcast(FP8X4)
                 scales = g_scales[e][:, half * P : (half + 1) * P]
-                if e < FIRST_PERMUTED:
-                    acc = psum_rows.tile([P, H], F32, name="rows")
-                    one_pass(acc[:], codes, scales, w2[:, e, :].bitcast(FP4X4), s2[:, e, :])
-                    nc.scalar.copy(out=dh_rows[2 * e + half][:], in_=acc[:].rearrange("s (m d) -> s d m", d=PACK))
-                else:
-                    dh_planes[e, half] = psum_planes.tile([P, PACK, P], F32, name="planes")
-                    for d in range(PACK):
-                        one_pass(
-                            dh_planes[e, half][:, d, :],
-                            w2_regrouped[:, e - FIRST_PERMUTED, d, :].bitcast(FP4X4),
-                            s2_regrouped[:, e - FIRST_PERMUTED, d, :],
-                            codes,
-                            scales,
-                        )
+                acc = psum_rows.tile([P, H], F32, name="rows")
+                one_pass(acc[:], codes, scales, w2[:, e, :].bitcast(FP4X4), s2[:, e, :])
+                nc.scalar.copy(out=dh_rows[2 * e + half][:], in_=acc[:].rearrange("s (m d) -> s d m", d=PACK))
 
-        def make_slope(e, half):
-            nc.scalar.activation(
-                out=slope[2 * e + half][:], in_=a_slots(e * C + half * P, P), func=ACT.Relu, scale=2.0
-            )
+        def make_slope(e):
+            for half in range(2):
+                nc.scalar.activation(
+                    out=slope[e][:, half], in_=a_slots(e * C + half * P, P), func=ACT.Relu
+                )
 
-        def make_da(e, half):
-            if e < FIRST_PERMUTED:
+        def make_da(e, da16, first):
+            for half in range(2):
                 planes = psum_planes.tile([P, PACK, P], F32, name="planes")
                 for d in range(PACK):
                     nc.tensor.transpose(planes[:, d, :], dh_rows[2 * e + half][:, d, :], ident[:])
+                dst = da16[:, first + half * P : first + (half + 1) * P, :]
+                if e < FUSED:
+                    nc.vector.tensor_tensor(
+                        side_by_side(dst), from_planes(planes[:]), from_planes(slope[e][:, half]), ALU.mult
+                    )
+                else:
+                    nc.vector.scalar_tensor_tensor(
+                        dst,
+                        a_slots(e * C + half * P, P).rearrange("p d c -> p c d"),
+                        0.0,
+                        planes[:].rearrange("p d c -> p c d"),
+                        ALU.max,
+                        ALU.mult,
+                    )
+
+        def quantize_da(da16, j0, j1):
+            quantize(da_codes[:, j0:j1], da_scales[:, j0:j1], da16)
+
+        def second_product(j0, j1):
+            for kh in range(K // P):
+                acc = psum_dx.tile([P, j1 - j0], F32, name="dx_sums")
+                for c0 in range(j0, j1, C):
+                    c1 = min(c0 + C, j1)
+                    e = c0 // C
+                    one_pass(
+                        acc[:, c0 - j0 : c1 - j0],
+                        w1[:, e, 2 * kh * P : 2 * (kh + 1) * P].bitcast(FP4X4),
+                        s1[:, e, kh * P : (kh + 1) * P],
+                        da_codes[:, c0:c1].bitcast(FP8X4),
+                        da_scales[:, c0:c1],
+                    )
+                nc.scalar.activation(out=dx[kh][:, j0:j1], in_=acc[:], func=ACT.Copy, scale=2.0)
+
+        da16 = {}
+
+        def back(e):
+            da16[e] = shared("half%d" % (e + 2), [P, C, PACK], BF16, "da16_%d" % e)
+            make_da(e, da16[e], 0)
+
+        g32 = [gather(0), gather(1)]
+        interleave(0, g32[0])
+        for e in range(E):
+            if e < FUSED:
+                make_slope(e)
+            if e + 1 < E:
+                interleave(e + 1, g32[e + 1])
+            first_product(e)
+            if e >= 2:
+                back(e - 2)
+            if e + 2 < E:
+                g32.append(gather(e + 2))
+            if e >= 2:
+                quantize_da(da16[e - 2][:], (e - 2) * C, (e - 1) * C)
+            if e in (3, 5):
+                second_product((e - 3) * C, (e - 1) * C)
+        back(4)
+        back(5)
+        quantize_da(da16[4][:], 4 * C, 5 * C)
+        second_product(4 * C, 5 * C)
+        for half in range(2):
+            quantize_da(da16[5][:, half * P : (half + 1) * P, :], 5 * C + half * P, 5 * C + (half + 1) * P)
+            second_product(5 * C + half * P, 5 * C + (half + 1) * P)
+
+        sums = [tiles(TOP, [P, T], F32, "sums%d_" % kh) for kh in range(K // P)]
+
+        def fetch(kh, r, t0, t1):
+            window = dx[kh][:].indirect(pos_sb[r][:, t0 // PER_COLUMN : t1 // PER_COLUMN])
+            if r == 0:
+                nc.vector.tensor_copy(sums[kh][r][:, t0:t1], window)
             else:
-                planes = dh_planes[e, half]
-            nc.vector.tensor_tensor(
-                side_by_side(da16[e][:, half * P : (half + 1) * P, :]),
-                from_planes(planes[:]),
-                from_planes(slope[2 * e + half][:]),
-                ALU.mult,
-            )
+                nc.vector.tensor_tensor(sums[kh][r][:, t0:t1], window, sums[kh][r - 1][:, t0:t1], ALU.add)
+            if r == TOP - 1:
+                nc.sync.dma_start(out=out[kh * P : (kh + 1) * P, t0:t1], in_=sums[kh][r][:, t0:t1])
 
-        def times_w1(acc, e, kh, c0, c1):
-            one_pass(
-                acc,
-                w1[:, e, 2 * kh * P : 2 * (kh + 1) * P].bitcast(FP4X4),
-                s1[:, e, kh * P : (kh + 1) * P],
-                da_codes[e][:, c0:c1].bitcast(FP8X4),
-                da_scales[e][:, c0:c1],
-            )
-
-        def second_product(e, c0=0, c1=C):
-            quantize(da_codes[e][:, c0:c1], da_scales[e][:, c0:c1], da16[e][:, c0:c1, :])
-            acc = psum_dx.tile([P, K // P, C], F32, name="dx_sums")
+        for r in range(TOP - 1):
             for kh in range(K // P):
-                times_w1(acc[:, kh, c0:c1], e, kh, c0, c1)
-            nc.scalar.copy(out=dx[:, :, e * C + c0 : e * C + c1], in_=acc[:, :, c0:c1])
-
-        def last_second_product(e, c0, c1):
-            quantize(da_codes[e][:, c0:c1], da_scales[e][:, c0:c1], da16[e][:, c0:c1, :])
-            for kh in range(K // P):
-                acc = psum_planes.tile([P, c1 - c0], F32, name="planes")
-                times_w1(acc[:], e, kh, c0, c1)
-                nc.scalar.copy(out=dx[:, kh, e * C + c0 : e * C + c1], in_=acc[:])
-
-        gather(0, 1)
-        first_product(0)
-        gather(1, 3)
-        regroup_scales(3, 4)
-        make_slope(0, 1)
-        first_product(1)
-        make_slope(1, 0)
-        first_product(2)
-        gather(3, 5)
-        make_slope(3, 0)
-        make_da(0, 1)
-        regroup_scales(4, 6)
-        make_slope(0, 0)
-        regroup_words(3, 4)
-        make_da(0, 0)
-        make_slope(1, 1)
-        make_slope(4, 1)
-        regroup_words(4, 6)
-        make_slope(2, 1)
-        make_da(1, 0)
-        make_slope(3, 1)
-        make_da(1, 1)
-        first_product(3)
-        make_da(2, 1)
-        make_slope(4, 0)
-        gather(5, 6)
-        make_slope(2, 0)
-        second_product(1)
-        make_da(2, 0)
-        first_product(4)
-        second_product(0)
-        make_da(3, 0)
-        first_product(5)
-        make_da(4, 1)
-        make_da(3, 1)
-        second_product(3)
-        make_slope(5, 0)
-        make_da(5, 0)
-        make_slope(5, 1)
-        make_da(5, 1)
-        make_da(4, 0)
-        second_product(4)
-        second_product(5, 0, P)
-        last_second_product(5, P, C)
-        second_product(2)
-
-        fetched = [tiles(TOP, [P, T], F32, "fetched%d_" % kh) for kh in range(K // P)]
-        pair_sum = tiles(K // P, [P, T], F32, "pair_sum")
-        total = tiles(K // P, [P, T], F32, "total")
-        all_tokens = slice(0, T)
-        token_halves = [slice(0, T // 2), slice(T // 2, T)]
-
-        def fetch(kh, r, tokens):
-            entries = pos_sb[r][:, tokens.start // PER_COLUMN : tokens.stop // PER_COLUMN]
-            nc.vector.tensor_copy(fetched[kh][r][:, tokens], dx[:, kh, :].indirect(entries))
-
-        def add_pair(kh, tokens):
-            nc.gpsimd.tensor_tensor(
-                pair_sum[kh][:, tokens], fetched[kh][0][:, tokens], fetched[kh][1][:, tokens], ALU.add
-            )
-
-        def finish(engine, kh, tokens):
-            engine.tensor_tensor(total[kh][:, tokens], pair_sum[kh][:, tokens], fetched[kh][2][:, tokens], ALU.add)
-            nc.sync.dma_start(out=out[kh * P : (kh + 1) * P, tokens], in_=total[kh][:, tokens])
-
-        for r in range(TOP):
-            fetch(0, r, all_tokens)
-        for tokens in token_halves:
-            add_pair(0, tokens)
-        for tokens in token_halves:
-            finish(nc.gpsimd, 0, tokens)
-        fetch(1, 0, all_tokens)
-        for tokens in token_halves:
-            fetch(1, 1, tokens)
-            add_pair(1, tokens)
-        for tokens in token_halves:
-            fetch(1, 2, tokens)
-        for tokens in token_halves:
-            finish(nc.vector, 1, tokens)
+                fetch(kh, r, 0, T)
+        fetch(0, TOP - 1, 0, T)
+        fetch(1, TOP - 1, 0, T - P)
+        fetch(1, TOP - 1, T - P, T)

@@ -12,7 +12,7 @@ PER_COLUMN = 16
 FLOPS = 2 * S * H * (N + K)
 BYTES = 4 * (N * T + H * S + S + K * T) + E * H * (N + K) // 2 + E * H * (N + K) // 32 + 2 * (S + TOP * T)
 
-FUSED = 3
+FUSED = 6
 
 F32 = mybir.dt.float32
 BF16 = mybir.dt.bfloat16
@@ -60,7 +60,7 @@ def tile_moe_bdx_mlp_relu2_kernel(
         dx = tiles(K // P, [P, S], F32, "dx")
 
         nc.vector.memset(s2[:].bitcast(I32), 0)
-        nc.vector.memset(s1[:].bitcast(I32), 0)
+        nc.gpsimd.memset(s1[:].bitcast(I32), 0)
         make_identity(nc, ident_made[:])
         nc.scalar.copy(out=ident[:], in_=ident_made[:])
 
@@ -92,7 +92,6 @@ def tile_moe_bdx_mlp_relu2_kernel(
 
         nc.sync.dma_start(offs_sb[:], offs)
         load_scales(nc.scalar, s2, w2_scales)
-        load_scales(nc.gpsimd, s1, w1_scales)
         load_gate(0, 1)
         for d in range(PACK):
             nc.sync.dma_start(out=dy[d][:, 0:T], in_=dy_planes[:, d, :])
@@ -104,6 +103,7 @@ def tile_moe_bdx_mlp_relu2_kernel(
         load_words(w2, w2_words, 2, E)
         load_a(2, 4)
         load_words(w1, w1_words, 0, E)
+        load_scales(nc.sync, s1, w1_scales)
         load_a(4, 6)
         for r, pos in enumerate((pos1, pos2, pos3)):
             nc.sync.dma_start(pos_sb[r][:], pos)
@@ -188,20 +188,23 @@ def tile_moe_bdx_mlp_relu2_kernel(
         def quantize_da(da16, j0, j1):
             quantize(da_codes[:, j0:j1], da_scales[:, j0:j1], da16)
 
+        def times_w1(pool, name, kh, j0, j1):
+            acc = pool.tile([P, j1 - j0], F32, name=name)
+            for c0 in range(j0, j1, C):
+                c1 = min(c0 + C, j1)
+                e = c0 // C
+                one_pass(
+                    acc[:, c0 - j0 : c1 - j0],
+                    w1[:, e, 2 * kh * P : 2 * (kh + 1) * P].bitcast(FP4X4),
+                    s1[:, e, kh * P : (kh + 1) * P],
+                    da_codes[:, c0:c1].bitcast(FP8X4),
+                    da_scales[:, c0:c1],
+                )
+            nc.scalar.activation(out=dx[kh][:, j0:j1], in_=acc[:], func=ACT.Copy, scale=2.0)
+
         def second_product(j0, j1):
             for kh in range(K // P):
-                acc = psum_dx.tile([P, j1 - j0], F32, name="dx_sums")
-                for c0 in range(j0, j1, C):
-                    c1 = min(c0 + C, j1)
-                    e = c0 // C
-                    one_pass(
-                        acc[:, c0 - j0 : c1 - j0],
-                        w1[:, e, 2 * kh * P : 2 * (kh + 1) * P].bitcast(FP4X4),
-                        s1[:, e, kh * P : (kh + 1) * P],
-                        da_codes[:, c0:c1].bitcast(FP8X4),
-                        da_scales[:, c0:c1],
-                    )
-                nc.scalar.activation(out=dx[kh][:, j0:j1], in_=acc[:], func=ACT.Copy, scale=2.0)
+                times_w1(psum_dx, "dx_sums", kh, j0, j1)
 
         da16 = {}
 
@@ -223,15 +226,17 @@ def tile_moe_bdx_mlp_relu2_kernel(
                 g32.append(gather(e + 2))
             if e >= 2:
                 quantize_da(da16[e - 2][:], (e - 2) * C, (e - 1) * C)
-            if e in (3, 5):
-                second_product((e - 3) * C, (e - 1) * C)
         back(4)
-        back(5)
         quantize_da(da16[4][:], 4 * C, 5 * C)
-        second_product(4 * C, 5 * C)
+        back(5)
+        second_product(0, 2 * C)
+        times_w1(psum_dx, "dx_sums", 0, 2 * C, 4 * C)
+        times_w1(psum_rows, "rows", 0, 4 * C, 5 * C)
         for half in range(2):
             quantize_da(da16[5][:, half * P : (half + 1) * P, :], 5 * C + half * P, 5 * C + (half + 1) * P)
-            second_product(5 * C + half * P, 5 * C + (half + 1) * P)
+            times_w1(psum_planes, "planes", 0, 5 * C + half * P, 5 * C + (half + 1) * P)
+        times_w1(psum_dx, "dx_sums", 1, 2 * C, 4 * C)
+        times_w1(psum_rows, "rows", 1, 4 * C, 6 * C)
 
         sums = [tiles(TOP, [P, T], F32, "sums%d_" % kh) for kh in range(K // P)]
 

@@ -12,7 +12,7 @@ PER_COLUMN = 16
 FLOPS = 2 * S * H * (N + K)
 BYTES = 4 * (N * T + H * S + S + K * T) + E * H * (N + K) // 2 + E * H * (N + K) // 32 + 2 * (S + TOP * T)
 
-FUSED = 6
+FUSED = 4
 
 F32 = mybir.dt.float32
 BF16 = mybir.dt.bfloat16
@@ -59,9 +59,9 @@ def tile_moe_bdx_mlp_relu2_kernel(
         ident = tile([P, P], F32, "ident")
         dx = tiles(K // P, [P, S], F32, "dx")
 
-        nc.vector.memset(s2[:].bitcast(I32), 0)
-        nc.gpsimd.memset(s1[:].bitcast(I32), 0)
         make_identity(nc, ident_made[:])
+        nc.gpsimd.memset(s2[:].bitcast(I32), 0)
+        nc.gpsimd.memset(s1[:].bitcast(I32), 0)
         nc.scalar.copy(out=ident[:], in_=ident_made[:])
 
         dy_planes = dyT.rearrange("(p d) c -> p d c", d=PACK)
@@ -112,7 +112,7 @@ def tile_moe_bdx_mlp_relu2_kernel(
         g_codes = tiles(E, [P, C], U32, "g_codes")
         g_scales = tiles(E, [P, C], U8, "g_scales")
         dh_rows = tiles(2 * E, [P, PACK, P], F32, "dh_rows")
-        slope = [shared("slope%d" % e, [P, 2, PACK, P], F32, "slope%d" % e) for e in range(FUSED)]
+        slope = [shared("slope%d" % x, [P, PACK, P], F32, "slope%d" % x) for x in range(2 * FUSED)]
         da_codes = tile([P, S], U32, "da_codes")
         da_scales = tile([P, S], U8, "da_scales")
 
@@ -139,8 +139,11 @@ def tile_moe_bdx_mlp_relu2_kernel(
         def entries_of(e0, e1):
             return offs_sb[:, e0 * C // PER_COLUMN : e1 * C // PER_COLUMN]
 
+        def g32_tag(e):
+            return "ab"[e % 2] if e < 4 else "slope%d" % (2 * (e - 4))
+
         def gather(e):
-            g32 = shared("ab"[e % 2] if e < 4 else "slope%d" % (e - 4), [P, PACK, C], F32, "g32_%d" % e)
+            g32 = shared(g32_tag(e), [P, PACK, C], F32, "g32_%d" % e)
             for d in range(PACK):
                 nc.vector.tensor_tensor(
                     g32[:, d, :], dy[d][:].indirect(entries_of(e, e + 1)), gate_sb[:, e * C : (e + 1) * C], ALU.mult
@@ -162,7 +165,7 @@ def tile_moe_bdx_mlp_relu2_kernel(
         def make_slope(e):
             for half in range(2):
                 nc.scalar.activation(
-                    out=slope[e][:, half], in_=a_slots(e * C + half * P, P), func=ACT.Relu
+                    out=slope[2 * e + half][:], in_=a_slots(e * C + half * P, P), func=ACT.Relu
                 )
 
         def make_da(e, da16, first):
@@ -173,7 +176,7 @@ def tile_moe_bdx_mlp_relu2_kernel(
                 dst = da16[:, first + half * P : first + (half + 1) * P, :]
                 if e < FUSED:
                     nc.vector.tensor_tensor(
-                        side_by_side(dst), from_planes(planes[:]), from_planes(slope[e][:, half]), ALU.mult
+                        side_by_side(dst), from_planes(planes[:]), from_planes(slope[2 * e + half][:]), ALU.mult
                     )
                 else:
                     nc.vector.scalar_tensor_tensor(
@@ -209,7 +212,7 @@ def tile_moe_bdx_mlp_relu2_kernel(
         da16 = {}
 
         def back(e):
-            da16[e] = shared("half%d" % (e + 2), [P, C, PACK], BF16, "da16_%d" % e)
+            da16[e] = shared(g32_tag(e + 2) if e < 4 else "da%d" % e, [P, C, PACK], BF16, "da16_%d" % e)
             make_da(e, da16[e], 0)
 
         g32 = [gather(0), gather(1)]
@@ -224,11 +227,13 @@ def tile_moe_bdx_mlp_relu2_kernel(
                 back(e - 2)
             if e + 2 < E:
                 g32.append(gather(e + 2))
-            if e >= 2:
+            if 2 <= e < 4:
                 quantize_da(da16[e - 2][:], (e - 2) * C, (e - 1) * C)
+        quantize_da(da16[2][:], 2 * C, 3 * C)
         back(4)
-        quantize_da(da16[4][:], 4 * C, 5 * C)
+        quantize_da(da16[3][:], 3 * C, 4 * C)
         back(5)
+        quantize_da(da16[4][:], 4 * C, 5 * C)
         second_product(0, 2 * C)
         times_w1(psum_dx, "dx_sums", 0, 2 * C, 4 * C)
         times_w1(psum_rows, "rows", 0, 4 * C, 5 * C)

@@ -12,7 +12,8 @@ PER_COLUMN = 16
 FLOPS = 2 * S * H * (N + K)
 BYTES = 4 * (N * T + H * S + S + K * T) + E * H * (N + K) // 2 + E * H * (N + K) // 32 + 2 * (S + TOP * T)
 
-FUSED = 4
+FUSED = (3, 4, 5)
+SIDE = 1
 
 F32 = mybir.dt.float32
 BF16 = mybir.dt.bfloat16
@@ -35,7 +36,7 @@ def tile_moe_bdx_mlp_relu2_kernel(
         reuse = ctx.enter_context(tc.tile_pool(name="reuse", bufs=1))
         psum_rows = ctx.enter_context(tc.psum_pool(name="psum_rows", bufs=2))
         psum_planes = ctx.enter_context(tc.psum_pool(name="psum_planes", bufs=4))
-        psum_dx = ctx.enter_context(tc.psum_pool(name="psum_dx", bufs=2))
+        psum_dx = ctx.enter_context(tc.psum_pool(name="psum_dx", bufs=1))
 
         def tile(shape, dtype, name):
             return keep.tile(shape, dtype, name=name, align_bytes=64)
@@ -112,7 +113,9 @@ def tile_moe_bdx_mlp_relu2_kernel(
         g_codes = tiles(E, [P, C], U32, "g_codes")
         g_scales = tiles(E, [P, C], U8, "g_scales")
         dh_rows = tiles(2 * E, [P, PACK, P], F32, "dh_rows")
-        slope = [shared("slope%d" % x, [P, PACK, P], F32, "slope%d" % x) for x in range(2 * FUSED)]
+        slope = {
+            x: shared("slope%d" % x, [P, PACK, P], F32, "slope%d" % x) for x in range(2 * E) if x // 2 not in FUSED
+        }
         da_codes = tile([P, S], U32, "da_codes")
         da_scales = tile([P, S], U8, "da_scales")
 
@@ -140,7 +143,7 @@ def tile_moe_bdx_mlp_relu2_kernel(
             return offs_sb[:, e0 * C // PER_COLUMN : e1 * C // PER_COLUMN]
 
         def g32_tag(e):
-            return "ab"[e % 2] if e < 4 else "slope%d" % (2 * (e - 4))
+            return "slope0" if e == 4 else "ab"[e % 2]
 
         def gather(e):
             g32 = shared(g32_tag(e), [P, PACK, C], F32, "g32_%d" % e)
@@ -160,7 +163,45 @@ def tile_moe_bdx_mlp_relu2_kernel(
                 scales = g_scales[e][:, half * P : (half + 1) * P]
                 acc = psum_rows.tile([P, H], F32, name="rows")
                 one_pass(acc[:], codes, scales, w2[:, e, :].bitcast(FP4X4), s2[:, e, :])
-                nc.scalar.copy(out=dh_rows[2 * e + half][:], in_=acc[:].rearrange("s (m d) -> s d m", d=PACK))
+                if e == SIDE:
+                    nc.scalar.copy(
+                        out=dh_rows[2 * e + half][:].rearrange("s d p -> s (d p)").rearrange("s (u p t) -> s u p t", u=2, t=2),
+                        in_=acc[:].rearrange("s (p u t) -> s u p t", u=2, t=2),
+                    )
+                else:
+                    nc.scalar.copy(out=dh_rows[2 * e + half][:], in_=acc[:].rearrange("s (m d) -> s d m", d=PACK))
+
+        def turned_slope(e):
+            for half in range(2):
+                turned = psum_planes.tile([P, PACK, P], F32, name="planes")
+                for d in range(PACK):
+                    nc.tensor.transpose(turned[:, d, :], a_slots(e * C + half * P, P)[:, d, :], ident[:])
+                nc.scalar.activation(
+                    out=slope[2 * e + half][:].rearrange("s d p -> s (d p)").rearrange("s (u p t) -> s u p t", u=2, t=2),
+                    in_=turned[:].rearrange("s (u t) p -> s u p t", t=2),
+                    func=ACT.Relu,
+                )
+
+        pairs = {}
+
+        def side_block(tag, half):
+            pairs[half] = shared(tag, [P, H], BF16, "pairs%d" % half)
+            nc.gpsimd.tensor_tensor(
+                pairs[half][:],
+                dh_rows[2 * SIDE + half][:].rearrange("s d p -> s (d p)"),
+                slope[2 * SIDE + half][:].rearrange("s d p -> s (d p)"),
+                ALU.mult,
+            )
+
+        def turn_pairs(da):
+            words = psum_dx.tile([P, 2, 2, P], F32, name="dx_b")
+            for half in range(2):
+                for u in range(2):
+                    nc.tensor.transpose(words[:, half, u, :], pairs[half][:].bitcast(F32)[:, u * P : (u + 1) * P], ident[:])
+            nc.scalar.copy(
+                out=da.rearrange("p c d -> p (c d)").bitcast(F32).rearrange("p (h s u) -> p h s u", s=P, u=2),
+                in_=words[:].rearrange("p h u s -> p h s u"),
+            )
 
         def make_slope(e):
             for half in range(2):
@@ -174,7 +215,7 @@ def tile_moe_bdx_mlp_relu2_kernel(
                 for d in range(PACK):
                     nc.tensor.transpose(planes[:, d, :], dh_rows[2 * e + half][:, d, :], ident[:])
                 dst = da16[:, first + half * P : first + (half + 1) * P, :]
-                if e < FUSED:
+                if e not in FUSED:
                     nc.vector.tensor_tensor(
                         side_by_side(dst), from_planes(planes[:]), from_planes(slope[2 * e + half][:]), ALU.mult
                     )
@@ -191,57 +232,67 @@ def tile_moe_bdx_mlp_relu2_kernel(
         def quantize_da(da16, j0, j1):
             quantize(da_codes[:, j0:j1], da_scales[:, j0:j1], da16)
 
-        def times_w1(pool, name, kh, j0, j1):
-            acc = pool.tile([P, j1 - j0], F32, name=name)
-            for c0 in range(j0, j1, C):
-                c1 = min(c0 + C, j1)
-                e = c0 // C
+        def times_w1(pool, name, kh, experts, c0=0, c1=C):
+            acc = pool.tile([P, len(experts), c1 - c0], F32, name=name)
+            for x, e in enumerate(experts):
                 one_pass(
-                    acc[:, c0 - j0 : c1 - j0],
+                    acc[:, x, :],
                     w1[:, e, 2 * kh * P : 2 * (kh + 1) * P].bitcast(FP4X4),
                     s1[:, e, kh * P : (kh + 1) * P],
-                    da_codes[:, c0:c1].bitcast(FP8X4),
-                    da_scales[:, c0:c1],
+                    da_codes[:, e * C + c0 : e * C + c1].bitcast(FP8X4),
+                    da_scales[:, e * C + c0 : e * C + c1],
                 )
-            nc.scalar.activation(out=dx[kh][:, j0:j1], in_=acc[:], func=ACT.Copy, scale=2.0)
-
-        def second_product(j0, j1):
-            for kh in range(K // P):
-                times_w1(psum_dx, "dx_sums", kh, j0, j1)
+            by_expert = dx[kh][:].rearrange("p (e c) -> p e c", c=C)
+            step = max(experts[-1] - experts[0], 1)
+            nc.scalar.activation(
+                out=by_expert[:, experts[0] : experts[-1] + 1 : step, c0:c1], in_=acc[:], func=ACT.Copy, scale=2.0
+            )
 
         da16 = {}
 
-        def back(e):
-            da16[e] = shared(g32_tag(e + 2) if e < 4 else "da%d" % e, [P, C, PACK], BF16, "da16_%d" % e)
+        def back(e, tag):
+            da16[e] = shared(tag, [P, C, PACK], BF16, "da16_%d" % e)
             make_da(e, da16[e], 0)
+
+        def quantize_expert(e):
+            quantize_da(da16[e][:], e * C, (e + 1) * C)
 
         g32 = [gather(0), gather(1)]
         interleave(0, g32[0])
         for e in range(E):
-            if e < FUSED:
+            if e == SIDE:
+                turned_slope(e)
+            elif e not in FUSED:
                 make_slope(e)
             if e + 1 < E:
                 interleave(e + 1, g32[e + 1])
             first_product(e)
-            if e >= 2:
-                back(e - 2)
+            if e >= 4:
+                side_block("half%d" % e, e - 4)
+            if e >= 2 and e - 2 != SIDE:
+                back(e - 2, g32_tag(e))
             if e + 2 < E:
                 g32.append(gather(e + 2))
-            if 2 <= e < 4:
-                quantize_da(da16[e - 2][:], (e - 2) * C, (e - 1) * C)
-        quantize_da(da16[2][:], 2 * C, 3 * C)
-        back(4)
-        quantize_da(da16[3][:], 3 * C, 4 * C)
-        back(5)
-        quantize_da(da16[4][:], 4 * C, 5 * C)
-        second_product(0, 2 * C)
-        times_w1(psum_dx, "dx_sums", 0, 2 * C, 4 * C)
-        times_w1(psum_rows, "rows", 0, 4 * C, 5 * C)
-        for half in range(2):
-            quantize_da(da16[5][:, half * P : (half + 1) * P, :], 5 * C + half * P, 5 * C + (half + 1) * P)
-            times_w1(psum_planes, "planes", 0, 5 * C + half * P, 5 * C + (half + 1) * P)
-        times_w1(psum_dx, "dx_sums", 1, 2 * C, 4 * C)
-        times_w1(psum_rows, "rows", 1, 4 * C, 6 * C)
+            if e == 2:
+                quantize_expert(0)
+        da16[SIDE] = tile([P, C, PACK], BF16, "da16_side")
+        turn_pairs(da16[SIDE][:])
+        quantize_expert(2)
+        back(4, "da4")
+        quantize_expert(3)
+        quantize_expert(SIDE)
+        back(5, "da5")
+        quantize_expert(4)
+        times_w1(psum_dx, "dx_a", 0, (0, 2))
+        times_w1(psum_dx, "dx_a", 0, (1, 3))
+        times_w1(psum_rows, "rows", 0, (4,))
+        quantize_da(da16[5][:, 0:P, :], 5 * C, 5 * C + P)
+        quantize_da(da16[5][:, P:C, :], 5 * C + P, 6 * C)
+        times_w1(psum_planes, "planes", 0, (5,), 0, P)
+        times_w1(psum_planes, "planes", 0, (5,), P, C)
+        times_w1(psum_dx, "dx_b", 1, (0, 2))
+        times_w1(psum_dx, "dx_b", 1, (1, 3))
+        times_w1(psum_rows, "rows", 1, (4, 5))
 
         sums = [tiles(TOP, [P, T], F32, "sums%d_" % kh) for kh in range(K // P)]
 

@@ -12,8 +12,8 @@ PER_COLUMN = 16
 FLOPS = 2 * S * H * (N + K)
 BYTES = 4 * (N * T + H * S + S + K * T) + E * H * (N + K) // 2 + E * H * (N + K) // 32 + 2 * (S + TOP * T)
 
-FUSED = (3, 4, 5)
-SIDE = 1
+FUSED = (4, 5)
+ON_GPSIMD = {2: (1, 0), 4: (1, 1), 5: (3, 1)}
 
 F32 = mybir.dt.float32
 BF16 = mybir.dt.bfloat16
@@ -109,7 +109,7 @@ def tile_moe_bdx_mlp_relu2_kernel(
         for r, pos in enumerate((pos1, pos2, pos3)):
             nc.sync.dma_start(pos_sb[r][:], pos)
 
-        g16 = [shared("half%d" % e, [P, C, PACK], BF16, "g16_%d" % e) for e in range(E)]
+        g16 = [shared("g16_%d" % e, [P, C, PACK], BF16, "g16_%d" % e) for e in range(E)]
         g_codes = tiles(E, [P, C], U32, "g_codes")
         g_scales = tiles(E, [P, C], U8, "g_scales")
         dh_rows = tiles(2 * E, [P, PACK, P], F32, "dh_rows")
@@ -118,12 +118,20 @@ def tile_moe_bdx_mlp_relu2_kernel(
         }
         da_codes = tile([P, S], U32, "da_codes")
         da_scales = tile([P, S], U8, "da_scales")
+        da_rows = {}
+        da16 = {}
 
         def from_planes(ap):
             return ap.rearrange("p d (c i) -> p c d i", i=4)
 
         def side_by_side(ap):
             return ap.rearrange("p (c i) d -> p c d i", i=4)
+
+        def flat(ap):
+            return ap.rearrange("s d p -> s (d p)")
+
+        def by_words(ap):
+            return flat(ap).rearrange("s (u p t) -> s u p t", u=2, t=2)
 
         def quantize(codes, scales, values):
             nc.vector.quantize_mx(out=codes.bitcast(FP8X4), scales=scales, in_=values.rearrange("p c d -> p (c d)"))
@@ -139,17 +147,15 @@ def tile_moe_bdx_mlp_relu2_kernel(
                 stop=True,
             )
 
-        def entries_of(e0, e1):
-            return offs_sb[:, e0 * C // PER_COLUMN : e1 * C // PER_COLUMN]
-
         def g32_tag(e):
             return "slope0" if e == 4 else "ab"[e % 2]
 
         def gather(e):
             g32 = shared(g32_tag(e), [P, PACK, C], F32, "g32_%d" % e)
+            entries = offs_sb[:, e * C // PER_COLUMN : (e + 1) * C // PER_COLUMN]
             for d in range(PACK):
                 nc.vector.tensor_tensor(
-                    g32[:, d, :], dy[d][:].indirect(entries_of(e, e + 1)), gate_sb[:, e * C : (e + 1) * C], ALU.mult
+                    g32[:, d, :], dy[d][:].indirect(entries), gate_sb[:, e * C : (e + 1) * C], ALU.mult
                 )
             return g32
 
@@ -163,63 +169,63 @@ def tile_moe_bdx_mlp_relu2_kernel(
                 scales = g_scales[e][:, half * P : (half + 1) * P]
                 acc = psum_rows.tile([P, H], F32, name="rows")
                 one_pass(acc[:], codes, scales, w2[:, e, :].bitcast(FP4X4), s2[:, e, :])
-                if e == SIDE:
+                if (e, half) in ON_GPSIMD.values():
                     nc.scalar.copy(
-                        out=dh_rows[2 * e + half][:].rearrange("s d p -> s (d p)").rearrange("s (u p t) -> s u p t", u=2, t=2),
+                        out=by_words(dh_rows[2 * e + half][:]),
                         in_=acc[:].rearrange("s (p u t) -> s u p t", u=2, t=2),
                     )
                 else:
-                    nc.scalar.copy(out=dh_rows[2 * e + half][:], in_=acc[:].rearrange("s (m d) -> s d m", d=PACK))
-
-        def turned_slope(e):
-            for half in range(2):
-                turned = psum_planes.tile([P, PACK, P], F32, name="planes")
-                for d in range(PACK):
-                    nc.tensor.transpose(turned[:, d, :], a_slots(e * C + half * P, P)[:, d, :], ident[:])
-                nc.scalar.activation(
-                    out=slope[2 * e + half][:].rearrange("s d p -> s (d p)").rearrange("s (u p t) -> s u p t", u=2, t=2),
-                    in_=turned[:].rearrange("s (u t) p -> s u p t", t=2),
-                    func=ACT.Relu,
-                )
-
-        pairs = {}
-
-        def side_block(tag, half):
-            pairs[half] = shared(tag, [P, H], BF16, "pairs%d" % half)
-            nc.gpsimd.tensor_tensor(
-                pairs[half][:],
-                dh_rows[2 * SIDE + half][:].rearrange("s d p -> s (d p)"),
-                slope[2 * SIDE + half][:].rearrange("s d p -> s (d p)"),
-                ALU.mult,
-            )
-
-        def turn_pairs(da):
-            words = psum_dx.tile([P, 2, 2, P], F32, name="dx_b")
-            for half in range(2):
-                for u in range(2):
-                    nc.tensor.transpose(words[:, half, u, :], pairs[half][:].bitcast(F32)[:, u * P : (u + 1) * P], ident[:])
-            nc.scalar.copy(
-                out=da.rearrange("p c d -> p (c d)").bitcast(F32).rearrange("p (h s u) -> p h s u", s=P, u=2),
-                in_=words[:].rearrange("p h u s -> p h s u"),
-            )
+                    nc.scalar.copy(out=dh_rows[2 * e + half][:], in_=acc[:].rearrange("s (p d) -> s d p", d=PACK))
 
         def make_slope(e):
             for half in range(2):
-                nc.scalar.activation(
-                    out=slope[2 * e + half][:], in_=a_slots(e * C + half * P, P), func=ACT.Relu
-                )
+                planes = a_slots(e * C + half * P, P)
+                if (e, half) in ON_GPSIMD.values():
+                    turned = psum_planes.tile([P, PACK, P], F32, name="planes")
+                    for d in range(PACK):
+                        nc.tensor.transpose(turned[:, d, :], planes[:, d, :], ident[:])
+                    nc.scalar.activation(
+                        out=by_words(slope[2 * e + half][:]),
+                        in_=turned[:].rearrange("s (u t) p -> s u p t", t=2),
+                        func=ACT.Relu,
+                    )
+                else:
+                    nc.scalar.activation(out=slope[2 * e + half][:], in_=planes, func=ACT.Relu)
 
-        def make_da(e, da16, first):
+        def da_on_gpsimd(released_by):
+            e, half = ON_GPSIMD[released_by]
+            da_rows[e, half] = shared("g16_%d" % released_by, [P, H], BF16, "da_rows%d%d" % (e, half))
+            nc.gpsimd.tensor_tensor(
+                da_rows[e, half][:], flat(dh_rows[2 * e + half][:]), flat(slope[2 * e + half][:]), ALU.mult
+            )
+
+        def turn_back(pool, name, e, first_half):
+            words = pool.tile([P, 2 - first_half, 2, P], F32, name=name)
+            for half in range(first_half, 2):
+                for u in range(2):
+                    nc.tensor.transpose(
+                        words[:, half - first_half, u, :],
+                        da_rows[e, half][:].bitcast(F32)[:, u * P : (u + 1) * P],
+                        ident[:],
+                    )
+            nc.scalar.copy(
+                out=da16[e][:, first_half * P :, :]
+                .rearrange("p c d -> p (c d)")
+                .bitcast(F32)
+                .rearrange("p (h s u) -> p h s u", s=P, u=2),
+                in_=words[:].rearrange("p h u s -> p h s u"),
+            )
+
+        def da_on_vector(e, tag):
+            da16[e] = shared(tag, [P, C, PACK], BF16, "da16_%d" % e)
             for half in range(2):
+                if (e, half) in ON_GPSIMD.values():
+                    continue
                 planes = psum_planes.tile([P, PACK, P], F32, name="planes")
                 for d in range(PACK):
                     nc.tensor.transpose(planes[:, d, :], dh_rows[2 * e + half][:, d, :], ident[:])
-                dst = da16[:, first + half * P : first + (half + 1) * P, :]
-                if e not in FUSED:
-                    nc.vector.tensor_tensor(
-                        side_by_side(dst), from_planes(planes[:]), from_planes(slope[2 * e + half][:]), ALU.mult
-                    )
-                else:
+                dst = da16[e][:, half * P : (half + 1) * P, :]
+                if e in FUSED:
                     nc.vector.scalar_tensor_tensor(
                         dst,
                         a_slots(e * C + half * P, P).rearrange("p d c -> p c d"),
@@ -228,11 +234,15 @@ def tile_moe_bdx_mlp_relu2_kernel(
                         ALU.max,
                         ALU.mult,
                     )
+                else:
+                    nc.vector.tensor_tensor(
+                        side_by_side(dst), from_planes(planes[:]), from_planes(slope[2 * e + half][:]), ALU.mult
+                    )
 
-        def quantize_da(da16, j0, j1):
-            quantize(da_codes[:, j0:j1], da_scales[:, j0:j1], da16)
+        def quantize_da(e, c0=0, c1=C):
+            quantize(da_codes[:, e * C + c0 : e * C + c1], da_scales[:, e * C + c0 : e * C + c1], da16[e][:, c0:c1, :])
 
-        def times_w1(pool, name, kh, experts, c0=0, c1=C):
+        def second_product(pool, name, kh, experts, c0=0, c1=C):
             acc = pool.tile([P, len(experts), c1 - c0], F32, name=name)
             for x, e in enumerate(experts):
                 one_pass(
@@ -248,51 +258,43 @@ def tile_moe_bdx_mlp_relu2_kernel(
                 out=by_expert[:, experts[0] : experts[-1] + 1 : step, c0:c1], in_=acc[:], func=ACT.Copy, scale=2.0
             )
 
-        da16 = {}
-
-        def back(e, tag):
-            da16[e] = shared(tag, [P, C, PACK], BF16, "da16_%d" % e)
-            make_da(e, da16[e], 0)
-
-        def quantize_expert(e):
-            quantize_da(da16[e][:], e * C, (e + 1) * C)
-
         g32 = [gather(0), gather(1)]
         interleave(0, g32[0])
         for e in range(E):
-            if e == SIDE:
-                turned_slope(e)
-            elif e not in FUSED:
+            if e not in FUSED:
                 make_slope(e)
             if e + 1 < E:
                 interleave(e + 1, g32[e + 1])
             first_product(e)
-            if e >= 4:
-                side_block("half%d" % e, e - 4)
-            if e >= 2 and e - 2 != SIDE:
-                back(e - 2, g32_tag(e))
+            if e in ON_GPSIMD:
+                da_on_gpsimd(e)
+            if e >= 2 and e - 2 != 1:
+                da_on_vector(e - 2, g32_tag(e))
             if e + 2 < E:
                 g32.append(gather(e + 2))
             if e == 2:
-                quantize_expert(0)
-        da16[SIDE] = tile([P, C, PACK], BF16, "da16_side")
-        turn_pairs(da16[SIDE][:])
-        quantize_expert(2)
-        back(4, "da4")
-        quantize_expert(3)
-        quantize_expert(SIDE)
-        back(5, "da5")
-        quantize_expert(4)
-        times_w1(psum_dx, "dx_a", 0, (0, 2))
-        times_w1(psum_dx, "dx_a", 0, (1, 3))
-        times_w1(psum_rows, "rows", 0, (4,))
-        quantize_da(da16[5][:, 0:P, :], 5 * C, 5 * C + P)
-        quantize_da(da16[5][:, P:C, :], 5 * C + P, 6 * C)
-        times_w1(psum_planes, "planes", 0, (5,), 0, P)
-        times_w1(psum_planes, "planes", 0, (5,), P, C)
-        times_w1(psum_dx, "dx_b", 1, (0, 2))
-        times_w1(psum_dx, "dx_b", 1, (1, 3))
-        times_w1(psum_rows, "rows", 1, (4, 5))
+                quantize_da(0)
+
+        da16[1] = tile([P, C, PACK], BF16, "da16_1")
+        turn_back(psum_dx, "dx_b", 1, 0)
+        quantize_da(2)
+        da_on_vector(4, "da4")
+        quantize_da(1)
+        turn_back(psum_planes, "planes", 3, 1)
+        quantize_da(3)
+        da_on_vector(5, "da5")
+        quantize_da(4)
+
+        second_product(psum_dx, "dx_a", 0, (0, 2))
+        second_product(psum_dx, "dx_a", 0, (1, 3))
+        second_product(psum_rows, "rows", 0, (4,))
+        quantize_da(5, 0, P)
+        quantize_da(5, P, C)
+        second_product(psum_planes, "planes", 0, (5,), 0, P)
+        second_product(psum_planes, "planes", 0, (5,), P, C)
+        second_product(psum_dx, "dx_b", 1, (0, 2))
+        second_product(psum_dx, "dx_b", 1, (1, 3))
+        second_product(psum_rows, "rows", 1, (4, 5))
 
         sums = [tiles(TOP, [P, T], F32, "sums%d_" % kh) for kh in range(K // P)]
 

@@ -12,8 +12,9 @@ PER_COLUMN = 16
 FLOPS = 2 * S * H * (N + K)
 BYTES = 4 * (N * T + H * S + S + K * T) + E * H * (N + K) // 2 + E * H * (N + K) // 32 + 2 * (S + TOP * T)
 
-FUSED = (4, 5)
-ON_GPSIMD = {2: (1, 0), 4: (1, 1), 5: (3, 1)}
+LAST = E - 1
+TURNED = 1
+WHOLE = tuple(e for e in range(E) if e != TURNED)
 
 F32 = mybir.dt.float32
 BF16 = mybir.dt.bfloat16
@@ -34,9 +35,11 @@ def tile_moe_bdx_mlp_relu2_kernel(
     with ExitStack() as ctx:
         keep = ctx.enter_context(tc.tile_pool(name="keep", bufs=1))
         reuse = ctx.enter_context(tc.tile_pool(name="reuse", bufs=1))
-        psum_rows = ctx.enter_context(tc.psum_pool(name="psum_rows", bufs=2))
-        psum_planes = ctx.enter_context(tc.psum_pool(name="psum_planes", bufs=4))
-        psum_dx = ctx.enter_context(tc.psum_pool(name="psum_dx", bufs=1))
+        placed = ctx.enter_context(tc.tile_pool(name="placed", bufs=1))
+        psum = ctx.enter_context(tc.psum_pool(name="psum", bufs=1))
+
+        def bank(number, shape, name):
+            return psum.tile(shape, F32, name=name, tag="bank%d" % number)
 
         def tile(shape, dtype, name):
             return keep.tile(shape, dtype, name=name, align_bytes=64)
@@ -49,16 +52,15 @@ def tile_moe_bdx_mlp_relu2_kernel(
 
         offs_sb = keep.tile([P, S // PER_COLUMN], U16, name="offs_sb")
         pos_sb = [keep.tile([P, T // PER_COLUMN], U16, name="pos_sb%d" % r) for r in range(TOP)]
-        dy = tiles(PACK, [P, T], F32, "dy")
+        dy = [shared("dy%d" % d, [P, T], F32, "dy%d" % d) for d in range(PACK)]
         gate_sb = tile([P, S], F32, "gate_sb")
         w2 = tile([P, E, 2 * H], U8, "w2")
         w1 = tile([P, E, 2 * K], U8, "w1")
         s2 = tile([P, E, H], U8, "s2")
         s1 = tile([P, E, K], U8, "s1")
-        a_pair = tiles(E // 2, [P, PACK, 2 * C], F32, "a_pair")
+        a_sb = [shared("a%d" % e, [P, PACK, C], F32, "a_sb%d" % e) for e in range(E)]
         ident_made = tile([P, P], F32, "ident_made")
         ident = tile([P, P], F32, "ident")
-        dx = tiles(K // P, [P, S], F32, "dx")
 
         make_identity(nc, ident_made[:])
         nc.gpsimd.memset(s2[:].bitcast(I32), 0)
@@ -71,12 +73,8 @@ def tile_moe_bdx_mlp_relu2_kernel(
         def load_gate(e0, e1):
             nc.sync.dma_start(out=gate_sb[:, e0 * C : e1 * C], in_=gate[0:P, e0 * C : e1 * C])
 
-        def a_slots(first, count):
-            start = first % (2 * C)
-            return a_pair[first // (2 * C)][:, :, start : start + count]
-
-        def load_a(e0, e1):
-            nc.sync.dma_start(out=a_slots(e0 * C, (e1 - e0) * C), in_=a_planes[:, :, e0 * C : e1 * C])
+        def load_a(e):
+            nc.sync.dma_start(out=a_sb[e][:], in_=a_planes[:, :, e * C : (e + 1) * C])
 
         def load_words(dst, src, e0, e1):
             nc.sync.dma_start(
@@ -84,42 +82,49 @@ def tile_moe_bdx_mlp_relu2_kernel(
                 in_=src[e0:e1, 0].rearrange("e p n -> p e n").bitcast(I32),
             )
 
-        def load_scales(queue, dst, src):
-            for q in range(4):
-                queue.dma_start(
-                    out=dst[32 * q : 32 * q + 4].bitcast(I32),
-                    in_=src[:, 0, 4 * q : 4 * q + 4, :].rearrange("e r n -> r e n").bitcast(I32),
+        def load_scales(dst, src):
+            for r in range(4):
+                nc.sync.dma_start(
+                    out=dst[r:P:32].bitcast(I32),
+                    in_=src[:, 0, r:16:4, :].rearrange("e q n -> q e n").bitcast(I32),
                 )
 
         nc.sync.dma_start(offs_sb[:], offs)
-        load_scales(nc.scalar, s2, w2_scales)
         load_gate(0, 1)
         for d in range(PACK):
-            nc.sync.dma_start(out=dy[d][:, 0:T], in_=dy_planes[:, d, :])
-        load_gate(1, 3)
-        load_a(0, 1)
+            nc.sync.dma_start(out=dy[d][:], in_=dy_planes[:, d, :])
+        load_gate(1, 2)
+        load_a(0)
+        load_gate(2, 4)
+        load_a(2)
+        load_a(3)
+        load_scales(s2, w2_scales)
         load_words(w2, w2_words, 0, 2)
-        load_a(1, 2)
-        load_gate(3, E)
-        load_words(w2, w2_words, 2, E)
-        load_a(2, 4)
+        load_gate(4, E)
+        load_a(TURNED)
+        load_a(4)
+        load_a(5)
+        load_words(w2, w2_words, 2, 4)
+        load_words(w2, w2_words, 4, E)
         load_words(w1, w1_words, 0, E)
-        load_scales(nc.sync, s1, w1_scales)
-        load_a(4, 6)
+        load_scales(s1, w1_scales)
         for r, pos in enumerate((pos1, pos2, pos3)):
             nc.sync.dma_start(pos_sb[r][:], pos)
 
-        g16 = [shared("g16_%d" % e, [P, C, PACK], BF16, "g16_%d" % e) for e in range(E)]
-        g_codes = tiles(E, [P, C], U32, "g_codes")
+        g16 = {}
+        g_codes = {}
         g_scales = tiles(E, [P, C], U8, "g_scales")
-        dh_rows = tiles(2 * E, [P, PACK, P], F32, "dh_rows")
-        slope = {
-            x: shared("slope%d" % x, [P, PACK, P], F32, "slope%d" % x) for x in range(2 * E) if x // 2 not in FUSED
-        }
+        slope = {}
+        da16 = [shared("da16_%d" % e, [P, C, PACK], BF16, "da16_%d" % e) for e in range(E)]
+        dx = [tile([P, S], F32, "dx0")]
         da_codes = tile([P, S], U32, "da_codes")
         da_scales = tile([P, S], U8, "da_scales")
+        dh_rows = tile([P, 2, H], F32, "dh_rows")
+        slope_first = tile([P, 2, H], F32, "slope_first")
+        dh_bank = {}
         da_rows = {}
-        da16 = {}
+        words = {}
+        apart = {}
 
         def from_planes(ap):
             return ap.rearrange("p d (c i) -> p c d i", i=4)
@@ -127,11 +132,11 @@ def tile_moe_bdx_mlp_relu2_kernel(
         def side_by_side(ap):
             return ap.rearrange("p (c i) d -> p c d i", i=4)
 
-        def flat(ap):
-            return ap.rearrange("s d p -> s (d p)")
-
         def by_words(ap):
-            return flat(ap).rearrange("s (u p t) -> s u p t", u=2, t=2)
+            return ap.rearrange("s (u p t) -> s u p t", u=2, t=2)
+
+        def regrouped(bank):
+            return bank.rearrange("s (p u t) -> s u p t", u=2, t=2)
 
         def quantize(codes, scales, values):
             nc.vector.quantize_mx(out=codes.bitcast(FP8X4), scales=scales, in_=values.rearrange("p c d -> p (c d)"))
@@ -147,11 +152,8 @@ def tile_moe_bdx_mlp_relu2_kernel(
                 stop=True,
             )
 
-        def g32_tag(e):
-            return "slope0" if e == 4 else "ab"[e % 2]
-
         def gather(e):
-            g32 = shared(g32_tag(e), [P, PACK, C], F32, "g32_%d" % e)
+            g32 = placed.tile([P, PACK, C], F32, name="g32_%d" % e, offset=e % 2 * 4096, align_bytes=64)
             entries = offs_sb[:, e * C // PER_COLUMN : (e + 1) * C // PER_COLUMN]
             for d in range(PACK):
                 nc.vector.tensor_tensor(
@@ -159,142 +161,212 @@ def tile_moe_bdx_mlp_relu2_kernel(
                 )
             return g32
 
+        def g16_tag(e):
+            return {1: "a0", 2: "a2", 3: "a3", 5: "a4"}.get(e, "g16_%d" % e)
+
         def interleave(e, g32):
+            g16[e] = shared(g16_tag(e), [P, C, PACK], BF16, "g16_%d" % e)
             nc.scalar.copy(out=side_by_side(g16[e][:]), in_=from_planes(g32[:]))
 
-        def first_product(e):
+        def quantize_g(e):
+            g_codes[e] = shared({LAST - 1: "dy0", LAST: "g_codes1"}.get(e, "g_codes%d" % e), [P, C], U32, "g_codes%d" % e)
             quantize(g_codes[e][:], g_scales[e][:], g16[e][:])
-            for half in range(2):
-                codes = g_codes[e][:, half * P : (half + 1) * P].bitcast(FP8X4)
-                scales = g_scales[e][:, half * P : (half + 1) * P]
-                acc = psum_rows.tile([P, H], F32, name="rows")
-                one_pass(acc[:], codes, scales, w2[:, e, :].bitcast(FP4X4), s2[:, e, :])
-                if (e, half) in ON_GPSIMD.values():
-                    nc.scalar.copy(
-                        out=by_words(dh_rows[2 * e + half][:]),
-                        in_=acc[:].rearrange("s (p u t) -> s u p t", u=2, t=2),
-                    )
-                else:
-                    nc.scalar.copy(out=dh_rows[2 * e + half][:], in_=acc[:].rearrange("s (p d) -> s d p", d=PACK))
 
-        def make_slope(e):
-            for half in range(2):
-                planes = a_slots(e * C + half * P, P)
-                if (e, half) in ON_GPSIMD.values():
-                    turned = psum_planes.tile([P, PACK, P], F32, name="planes")
-                    for d in range(PACK):
-                        nc.tensor.transpose(turned[:, d, :], planes[:, d, :], ident[:])
-                    nc.scalar.activation(
-                        out=by_words(slope[2 * e + half][:]),
-                        in_=turned[:].rearrange("s (u t) p -> s u p t", t=2),
-                        func=ACT.Relu,
-                    )
-                else:
-                    nc.scalar.activation(out=slope[2 * e + half][:], in_=planes, func=ACT.Relu)
+        def first_product(number, e, half):
+            acc = bank(number, [P, H], "dh%d%d" % (e, half))
+            codes = g_codes[e][:, half * P : (half + 1) * P].bitcast(FP8X4)
+            scales = g_scales[e][:, half * P : (half + 1) * P]
+            one_pass(acc[:], codes, scales, w2[:, e, :].bitcast(FP4X4), s2[:, e, :])
+            dh_bank[e, half] = acc
 
-        def da_on_gpsimd(released_by):
-            e, half = ON_GPSIMD[released_by]
-            da_rows[e, half] = shared("g16_%d" % released_by, [P, H], BF16, "da_rows%d%d" % (e, half))
-            nc.gpsimd.tensor_tensor(
-                da_rows[e, half][:], flat(dh_rows[2 * e + half][:]), flat(slope[2 * e + half][:]), ALU.mult
+        def make_slope(number, e, half, tag=None):
+            turned = bank(number, [P, PACK, P], "turned%d%d" % (e, half))
+            for d in range(PACK):
+                nc.tensor.transpose(turned[:, d, :], a_sb[e][:, d, half * P : (half + 1) * P], ident[:])
+            if e == 0:
+                slope[e, half] = slope_first[:, half, :]
+            elif isinstance(tag, int):
+                slope[e, half] = placed.tile([P, H], F32, name="slope_placed%d" % half, offset=tag, align_bytes=64)[:]
+            else:
+                slope[e, half] = shared(tag or "slope%d%d" % (e, half), [P, H], F32, "slope%d%d" % (e, half))[:]
+            nc.scalar.activation(
+                out=by_words(slope[e, half]),
+                in_=turned[:].rearrange("s (u t) p -> s u p t", t=2),
+                func=ACT.Relu,
             )
 
-        def turn_back(pool, name, e, first_half):
-            words = pool.tile([P, 2 - first_half, 2, P], F32, name=name)
-            for half in range(first_half, 2):
-                for u in range(2):
-                    nc.tensor.transpose(
-                        words[:, half - first_half, u, :],
-                        da_rows[e, half][:].bitcast(F32)[:, u * P : (u + 1) * P],
-                        ident[:],
-                    )
+        def dh_for_gpsimd(number, half):
+            first_product(number, 0, half)
+            nc.scalar.copy(out=by_words(dh_rows[:, half, :]), in_=regrouped(dh_bank[0, half][:]))
+
+        def da_on_gpsimd(tag):
+            both = shared(tag, [P, 2, H], BF16, "da_rows0")
+            nc.gpsimd.tensor_tensor(both[:], dh_rows[:], slope_first[:], ALU.mult)
+            for half in range(2):
+                da_rows[0, half] = both[:, half, :]
+
+        def da_on_vector(e, half, offset=None):
+            name = "da_rows%d%d" % (e, half)
+            if offset is None:
+                da_rows[e, half] = shared(name, [P, H], BF16, name)[:]
+            else:
+                da_rows[e, half] = placed.tile([P, H], BF16, name=name, offset=offset, align_bytes=64)[:]
+            nc.vector.tensor_tensor(
+                by_words(da_rows[e, half]), regrouped(dh_bank[e, half][:]), by_words(slope[e, half]), ALU.mult
+            )
+
+        def turn(number, e, half, halves=2):
+            if number is not None:
+                words[e] = bank(number, [P, halves, 2, P], "words%d%d" % (e, half))
+            for u in range(2):
+                nc.tensor.transpose(
+                    words[e][:, half % halves, u, :], da_rows[e, half].bitcast(F32)[:, u * P : (u + 1) * P], ident[:]
+                )
+
+        def words_out(e, c0=0, c1=C):
             nc.scalar.copy(
-                out=da16[e][:, first_half * P :, :]
+                out=da16[e][:, c0:c1, :]
                 .rearrange("p c d -> p (c d)")
                 .bitcast(F32)
                 .rearrange("p (h s u) -> p h s u", s=P, u=2),
-                in_=words[:].rearrange("p h u s -> p h s u"),
+                in_=words[e][:].rearrange("p h u s -> p h s u"),
             )
 
-        def da_on_vector(e, tag):
-            da16[e] = shared(tag, [P, C, PACK], BF16, "da16_%d" % e)
-            for half in range(2):
-                if (e, half) in ON_GPSIMD.values():
-                    continue
-                planes = psum_planes.tile([P, PACK, P], F32, name="planes")
-                for d in range(PACK):
-                    nc.tensor.transpose(planes[:, d, :], dh_rows[2 * e + half][:, d, :], ident[:])
-                dst = da16[e][:, half * P : (half + 1) * P, :]
-                if e in FUSED:
-                    nc.vector.scalar_tensor_tensor(
-                        dst,
-                        a_slots(e * C + half * P, P).rearrange("p d c -> p c d"),
-                        0.0,
-                        planes[:].rearrange("p d c -> p c d"),
-                        ALU.max,
-                        ALU.mult,
-                    )
-                else:
-                    nc.vector.tensor_tensor(
-                        side_by_side(dst), from_planes(planes[:]), from_planes(slope[2 * e + half][:]), ALU.mult
-                    )
+        def rows_of_turned(rows):
+            nc.scalar.copy(out=rows[:], in_=dh_bank[TURNED, 1][:].rearrange("s (p d) -> s d p", d=PACK))
 
-        def quantize_da(e, c0=0, c1=C):
-            quantize(da_codes[:, e * C + c0 : e * C + c1], da_scales[:, e * C + c0 : e * C + c1], da16[e][:, c0:c1, :])
+        def planes_of_turned(number, rows):
+            planes = bank(number, [P, PACK, P], "planes")
+            for d in range(PACK):
+                nc.tensor.transpose(planes[:, d, :], rows[:, d, :], ident[:])
+            return planes
 
-        def second_product(pool, name, kh, experts, c0=0, c1=C):
-            acc = pool.tile([P, len(experts), c1 - c0], F32, name=name)
+        def da_of_turned(planes):
+            da_last = placed.tile([P, P, PACK], BF16, name="da_last", offset=4096, align_bytes=64)
+            nc.vector.scalar_tensor_tensor(
+                da_last[:],
+                a_sb[TURNED][:, :, P:].rearrange("p d c -> p c d"),
+                0.0,
+                planes[:].rearrange("p d c -> p c d"),
+                ALU.max,
+                ALU.mult,
+            )
+            return da_last
+
+        def da_operand(e, c0, c1):
+            if (e, c0) in apart:
+                return apart[e, c0][:], da_scales[:, e * C + c0 : e * C + c1]
+            return da_codes[:, e * C + c0 : e * C + c1], da_scales[:, e * C + c0 : e * C + c1]
+
+        def quantize_da(e, c0=0, c1=C, values=None):
+            quantize(*da_operand(e, c0, c1), da16[e][:, c0:c1, :] if values is None else values)
+
+        def second_product(number, kh, experts):
+            acc = bank(number, [P, len(experts), C], "dx%d_%d" % (kh, experts[0]))
             for x, e in enumerate(experts):
-                one_pass(
-                    acc[:, x, :],
-                    w1[:, e, 2 * kh * P : 2 * (kh + 1) * P].bitcast(FP4X4),
-                    s1[:, e, kh * P : (kh + 1) * P],
-                    da_codes[:, e * C + c0 : e * C + c1].bitcast(FP8X4),
-                    da_scales[:, e * C + c0 : e * C + c1],
-                )
+                width = P if e in (TURNED, LAST) else C
+                for c0 in range(0, C, width):
+                    codes, scales = da_operand(e, c0, c0 + width)
+                    one_pass(
+                        acc[:, x, c0 : c0 + width],
+                        w1[:, e, 2 * kh * P : 2 * (kh + 1) * P].bitcast(FP4X4),
+                        s1[:, e, kh * P : (kh + 1) * P],
+                        codes.bitcast(FP8X4),
+                        scales,
+                    )
+            return acc
+
+        def dx_out(kh, experts, acc, on_vector=False):
             by_expert = dx[kh][:].rearrange("p (e c) -> p e c", c=C)
             step = max(experts[-1] - experts[0], 1)
-            nc.scalar.activation(
-                out=by_expert[:, experts[0] : experts[-1] + 1 : step, c0:c1], in_=acc[:], func=ACT.Copy, scale=2.0
-            )
+            dst = by_expert[:, experts[0] : experts[-1] + 1 : step, :]
+            if on_vector:
+                nc.vector.tensor_scalar_mul(dst, acc[:], 2.0)
+            else:
+                nc.scalar.activation(out=dst, in_=acc[:], func=ACT.Copy, scale=2.0)
 
-        g32 = [gather(0), gather(1)]
-        interleave(0, g32[0])
-        for e in range(E):
-            if e not in FUSED:
-                make_slope(e)
-            if e + 1 < E:
-                interleave(e + 1, g32[e + 1])
-            first_product(e)
-            if e in ON_GPSIMD:
-                da_on_gpsimd(e)
-            if e >= 2 and e - 2 != 1:
-                da_on_vector(e - 2, g32_tag(e))
-            if e + 2 < E:
-                g32.append(gather(e + 2))
-            if e == 2:
-                quantize_da(0)
+        rows = tile([P, PACK, P], F32, "rows")
+        g32 = [gather(0)]
+        for e in range(4):
+            interleave(e, g32[e])
+            g32.append(gather(e + 1))
+            if e < 3:
+                for half in range(2):
+                    make_slope(2 * e % 4 + half, WHOLE[e], half)
+            quantize_g(e)
+        dh_for_gpsimd(6, 0)
+        dh_for_gpsimd(7, 1)
+        first_product(5, TURNED, 1)
+        rows_of_turned(rows)
+        interleave(4, g32[4])
+        g32.append(gather(LAST))
+        make_slope(2, TURNED, 0)
+        make_slope(3, 4, 0)
+        make_slope(4, 4, 1)
+        interleave(LAST, g32[LAST])
+        make_slope(5, LAST, 0, 6144)
+        first_product(0, 2, 0)
+        first_product(1, 2, 1)
+        first_product(6, 3, 0)
 
-        da16[1] = tile([P, C, PACK], BF16, "da16_1")
-        turn_back(psum_dx, "dx_b", 1, 0)
+        quantize_g(4)
+        da_on_gpsimd(g16_tag(4))
+        da_on_vector(2, 0, 0)
+        first_product(0, 3, 1)
+        turn(7, 2, 0)
+        da_on_vector(2, 1, 3072)
+        turn(None, 2, 1)
+        words_out(2)
+        first_product(1, TURNED, 0)
+        da_on_vector(3, 0, 1024)
+        first_product(6, 4, 0)
+        make_slope(2, LAST, 1, 4096 - 64)
+        turn(3, 3, 0)
+        da_on_vector(3, 1)
+        turn(None, 3, 1)
+        words_out(3)
+        da_on_vector(TURNED, 0)
+        first_product(1, 4, 1)
+        turn(0, 0, 0)
+        turn(None, 0, 1)
+        words_out(0)
+        turn(4, TURNED, 0, 1)
+        words_out(TURNED, 0, P)
+        quantize_g(LAST)
+        da_on_vector(4, 0)
+        first_product(6, LAST, 0)
+        turn(7, 4, 0)
         quantize_da(2)
-        da_on_vector(4, "da4")
-        quantize_da(1)
-        turn_back(psum_planes, "planes", 3, 1)
+        da_on_vector(4, 1)
+        turn(None, 4, 1)
+        words_out(4)
+        first_product(1, LAST, 1)
         quantize_da(3)
-        da_on_vector(5, "da5")
+        planes = planes_of_turned(5, rows)
+        dx_out(0, (2, 3), second_product(2, 0, (2, 3)))
+        late = [((2, 3), second_product(0, 1, (2, 3)))]
+        da_on_vector(LAST, 0)
+        turn(3, LAST, 0, 1)
+        words_out(LAST, 0, P)
+        quantize_da(0)
+        da_on_vector(LAST, 1)
+        turn(4, LAST, 1, 1)
+        words_out(LAST, P, C)
         quantize_da(4)
-
-        second_product(psum_dx, "dx_a", 0, (0, 2))
-        second_product(psum_dx, "dx_a", 0, (1, 3))
-        second_product(psum_rows, "rows", 0, (4,))
-        quantize_da(5, 0, P)
-        quantize_da(5, P, C)
-        second_product(psum_planes, "planes", 0, (5,), 0, P)
-        second_product(psum_planes, "planes", 0, (5,), P, C)
-        second_product(psum_dx, "dx_b", 1, (0, 2))
-        second_product(psum_dx, "dx_b", 1, (1, 3))
-        second_product(psum_rows, "rows", 1, (4, 5))
+        quantize_da(TURNED, 0, P)
+        dx_out(0, (0, 4), second_product(6, 0, (0, 4)))
+        late.append(((0, 4), second_product(7, 1, (0, 4))))
+        da_last = da_of_turned(planes)
+        quantize_da(LAST, 0, P)
+        apart[TURNED, P] = shared("da_rows51", [P, P], U32, "last_codes")
+        quantize_da(TURNED, P, C, da_last[:])
+        dx_out(0, (TURNED,), second_product(2, 0, (TURNED,)))
+        quantize_da(LAST, P, C)
+        dx_out(0, (LAST,), second_product(1, 0, (LAST,)), True)
+        late.append(((TURNED, LAST), second_product(2, 1, (TURNED, LAST))))
+        dx.append(shared("da_rows51", [P, S], F32, "dx1"))
+        for experts, acc in late:
+            dx_out(1, experts, acc)
 
         sums = [tiles(TOP, [P, T], F32, "sums%d_" % kh) for kh in range(K // P)]
 
@@ -307,9 +379,7 @@ def tile_moe_bdx_mlp_relu2_kernel(
             if r == TOP - 1:
                 nc.sync.dma_start(out=out[kh * P : (kh + 1) * P, t0:t1], in_=sums[kh][r][:, t0:t1])
 
-        for r in range(TOP - 1):
-            for kh in range(K // P):
-                fetch(kh, r, 0, T)
-        fetch(0, TOP - 1, 0, T)
-        fetch(1, TOP - 1, 0, T - P)
-        fetch(1, TOP - 1, T - P, T)
+        for kh, cut in enumerate((T // 2, T - 192)):
+            for r in range(TOP):
+                fetch(kh, r, 0, cut)
+                fetch(kh, r, cut, T)

@@ -73,8 +73,11 @@ def tile_moe_bdx_mlp_relu2_kernel(
         def load_gate(e0, e1):
             nc.sync.dma_start(out=gate_sb[:, e0 * C : e1 * C], in_=gate[0:P, e0 * C : e1 * C])
 
-        def load_a(e):
-            nc.sync.dma_start(out=a_sb[e][:], in_=a_planes[:, :, e * C : (e + 1) * C])
+        def load_a(e, planes=PACK):
+            for d in range(0, PACK, planes):
+                nc.sync.dma_start(
+                    out=a_sb[e][:, d : d + planes, :], in_=a_planes[:, d : d + planes, e * C : (e + 1) * C]
+                )
 
         def load_words(dst, src, e0, e1):
             nc.sync.dma_start(
@@ -94,16 +97,17 @@ def tile_moe_bdx_mlp_relu2_kernel(
         for d in range(PACK):
             nc.sync.dma_start(out=dy[d][:], in_=dy_planes[:, d, :])
         load_gate(1, 2)
-        load_a(0)
+        load_a(0, 2)
         load_gate(2, 4)
-        load_a(2)
+        load_a(2, 2)
         load_a(3)
+        load_gate(4, 5)
         load_scales(s2, w2_scales)
         load_words(w2, w2_words, 0, 2)
-        load_gate(4, E)
-        load_a(TURNED)
+        load_gate(5, E)
         load_a(4)
         load_a(5)
+        load_a(TURNED)
         load_words(w2, w2_words, 2, 4)
         load_words(w2, w2_words, 4, E)
         load_words(w1, w1_words, 0, E)
@@ -115,7 +119,8 @@ def tile_moe_bdx_mlp_relu2_kernel(
         g_codes = {}
         g_scales = tiles(E, [P, C], U8, "g_scales")
         slope = {}
-        da16 = [shared("da16_%d" % e, [P, C, PACK], BF16, "da16_%d" % e) for e in range(E)]
+        da16 = {e: tile([P, C, PACK], BF16, "da16_%d" % e) for e in range(E) if e != 2}
+        da16[2] = placed.tile([P, C, PACK], BF16, name="da16_2", offset=12288, align_bytes=64)
         dx = [tile([P, S], F32, "dx0")]
         da_codes = tile([P, S], U32, "da_codes")
         da_scales = tile([P, S], U8, "da_scales")
@@ -153,7 +158,7 @@ def tile_moe_bdx_mlp_relu2_kernel(
             )
 
         def gather(e):
-            g32 = placed.tile([P, PACK, C], F32, name="g32_%d" % e, offset=e % 2 * 4096, align_bytes=64)
+            g32 = placed.tile([P, PACK, C], F32, name="g32_%d" % e, offset=4096 + e % 2 * 4096, align_bytes=64)
             entries = offs_sb[:, e * C // PER_COLUMN : (e + 1) * C // PER_COLUMN]
             for d in range(PACK):
                 nc.vector.tensor_tensor(
@@ -162,14 +167,14 @@ def tile_moe_bdx_mlp_relu2_kernel(
             return g32
 
         def g16_tag(e):
-            return {1: "a0", 2: "a2", 3: "a3", 5: "a4"}.get(e, "g16_%d" % e)
+            return {1: "a0", 2: "a2", 3: "a3", 4: "g_codes1", 5: "a4"}.get(e, "g16_%d" % e)
 
         def interleave(e, g32):
             g16[e] = shared(g16_tag(e), [P, C, PACK], BF16, "g16_%d" % e)
             nc.scalar.copy(out=side_by_side(g16[e][:]), in_=from_planes(g32[:]))
 
         def quantize_g(e):
-            g_codes[e] = shared({LAST - 1: "dy0", LAST: "g_codes1"}.get(e, "g_codes%d" % e), [P, C], U32, "g_codes%d" % e)
+            g_codes[e] = shared({LAST - 1: "dy0", LAST: "slope31"}.get(e, "g_codes%d" % e), [P, C], U32, "g_codes%d" % e)
             quantize(g_codes[e][:], g_scales[e][:], g16[e][:])
 
         def first_product(number, e, half):
@@ -179,21 +184,28 @@ def tile_moe_bdx_mlp_relu2_kernel(
             one_pass(acc[:], codes, scales, w2[:, e, :].bitcast(FP4X4), s2[:, e, :])
             dh_bank[e, half] = acc
 
-        def make_slope(number, e, half, tag=None):
+        def turn_a(number, e, half):
             turned = bank(number, [P, PACK, P], "turned%d%d" % (e, half))
             for d in range(PACK):
                 nc.tensor.transpose(turned[:, d, :], a_sb[e][:, d, half * P : (half + 1) * P], ident[:])
+            return turned
+
+        def slope_out(turned, e, half, offset=None):
+            name = "slope%d%d" % (e, half)
             if e == 0:
                 slope[e, half] = slope_first[:, half, :]
-            elif isinstance(tag, int):
-                slope[e, half] = placed.tile([P, H], F32, name="slope_placed%d" % half, offset=tag, align_bytes=64)[:]
+            elif offset is None:
+                slope[e, half] = shared(name, [P, H], F32, name)[:]
             else:
-                slope[e, half] = shared(tag or "slope%d%d" % (e, half), [P, H], F32, "slope%d%d" % (e, half))[:]
+                slope[e, half] = placed.tile([P, H], F32, name=name, offset=offset, align_bytes=64)[:]
             nc.scalar.activation(
                 out=by_words(slope[e, half]),
                 in_=turned[:].rearrange("s (u t) p -> s u p t", t=2),
                 func=ACT.Relu,
             )
+
+        def make_slope(number, e, half):
+            slope_out(turn_a(number, e, half), e, half)
 
         def dh_for_gpsimd(number, half):
             first_product(number, 0, half)
@@ -205,10 +217,14 @@ def tile_moe_bdx_mlp_relu2_kernel(
             for half in range(2):
                 da_rows[0, half] = both[:, half, :]
 
+        def third_on_gpsimd(offset):
+            da_rows[TURNED, 0] = placed.tile([P, H], BF16, name="da_rows10", offset=offset, align_bytes=64)[:]
+            nc.gpsimd.tensor_tensor(da_rows[TURNED, 0], dh_third[:], slope[TURNED, 0], ALU.mult)
+
         def da_on_vector(e, half, offset=None):
             name = "da_rows%d%d" % (e, half)
-            if offset is None:
-                da_rows[e, half] = shared(name, [P, H], BF16, name)[:]
+            if not isinstance(offset, int):
+                da_rows[e, half] = shared(offset or name, [P, H], BF16, name)[:]
             else:
                 da_rows[e, half] = placed.tile([P, H], BF16, name=name, offset=offset, align_bytes=64)[:]
             nc.vector.tensor_tensor(
@@ -242,7 +258,7 @@ def tile_moe_bdx_mlp_relu2_kernel(
             return planes
 
         def da_of_turned(planes):
-            da_last = placed.tile([P, P, PACK], BF16, name="da_last", offset=4096, align_bytes=64)
+            da_last = placed.tile([P, P, PACK], BF16, name="da_last", offset=1152, align_bytes=64)
             nc.vector.scalar_tensor_tensor(
                 da_last[:],
                 a_sb[TURNED][:, :, P:].rearrange("p d c -> p c d"),
@@ -298,72 +314,76 @@ def tile_moe_bdx_mlp_relu2_kernel(
         dh_for_gpsimd(7, 1)
         first_product(5, TURNED, 1)
         rows_of_turned(rows)
+        first_product(1, TURNED, 0)
+        dh_third = tile([P, H], F32, "dh_third")
+        nc.scalar.copy(out=by_words(dh_third[:]), in_=regrouped(dh_bank[TURNED, 0][:]))
         interleave(4, g32[4])
         g32.append(gather(LAST))
-        make_slope(2, TURNED, 0)
         make_slope(3, 4, 0)
         make_slope(4, 4, 1)
         interleave(LAST, g32[LAST])
-        make_slope(5, LAST, 0, 6144)
+        turned_last = [turn_a(2, LAST, 0), turn_a(7, LAST, 1)]
         first_product(0, 2, 0)
         first_product(1, 2, 1)
         first_product(6, 3, 0)
 
         quantize_g(4)
         da_on_gpsimd(g16_tag(4))
-        da_on_vector(2, 0, 0)
+        first_product(3, 4, 0)
+        da_on_vector(2, 0, 5120)
         first_product(0, 3, 1)
-        turn(7, 2, 0)
-        da_on_vector(2, 1, 3072)
+        turn(5, 2, 0)
+        da_on_vector(2, 1, 7168)
         turn(None, 2, 1)
         words_out(2)
-        first_product(1, TURNED, 0)
-        da_on_vector(3, 0, 1024)
-        first_product(6, 4, 0)
-        make_slope(2, LAST, 1, 4096 - 64)
-        turn(3, 3, 0)
+        slope_out(turn_a(1, TURNED, 0), TURNED, 0, 8128)
+        slope_out(turned_last[0], LAST, 0, 10240)
+        da_on_vector(3, 0, 3136)
+        turn(4, 3, 0)
+        slope_out(turned_last[1], LAST, 1, 1152)
         da_on_vector(3, 1)
+        first_product(6, 4, 1)
         turn(None, 3, 1)
         words_out(3)
-        da_on_vector(TURNED, 0)
-        first_product(1, 4, 1)
-        turn(0, 0, 0)
+        da_on_vector(4, 0)
+        quantize_g(LAST)
+        first_product(0, LAST, 0)
+        first_product(1, LAST, 1)
+        turn(5, 0, 0)
         turn(None, 0, 1)
         words_out(0)
-        turn(4, TURNED, 0, 1)
-        words_out(TURNED, 0, P)
-        quantize_g(LAST)
-        da_on_vector(4, 0)
-        first_product(6, LAST, 0)
-        turn(7, 4, 0)
+        turn(3, 4, 0)
         quantize_da(2)
-        da_on_vector(4, 1)
+        third_on_gpsimd(13312)
+        da_on_vector(4, 1, g16_tag(LAST))
         turn(None, 4, 1)
         words_out(4)
-        first_product(1, LAST, 1)
-        quantize_da(3)
-        planes = planes_of_turned(5, rows)
-        dx_out(0, (2, 3), second_product(2, 0, (2, 3)))
-        late = [((2, 3), second_product(0, 1, (2, 3)))]
+        planes = planes_of_turned(2, rows)
         da_on_vector(LAST, 0)
-        turn(3, LAST, 0, 1)
+        turn(7, LAST, 0, 1)
         words_out(LAST, 0, P)
-        quantize_da(0)
+        turn(6, TURNED, 0, 1)
+        words_out(TURNED, 0, P)
         da_on_vector(LAST, 1)
-        turn(4, LAST, 1, 1)
+        turn(0, LAST, 1, 1)
         words_out(LAST, P, C)
-        quantize_da(4)
-        quantize_da(TURNED, 0, P)
-        dx_out(0, (0, 4), second_product(6, 0, (0, 4)))
-        late.append(((0, 4), second_product(7, 1, (0, 4))))
+        apart[3, 0] = placed.tile([P, C], U32, name="codes3", offset=10240, align_bytes=64)
+        quantize_da(3)
+        dx_out(0, (2, 3), second_product(4, 0, (2, 3)))
+        late = [((2, 3), second_product(5, 1, (2, 3)))]
+        quantize_da(0)
         da_last = da_of_turned(planes)
+        quantize_da(4)
+        dx_out(0, (0, 4), second_product(3, 0, (0, 4)))
+        late.append(((0, 4), second_product(7, 1, (0, 4))))
         quantize_da(LAST, 0, P)
+        quantize_da(TURNED, 0, P)
         apart[TURNED, P] = shared("da_rows51", [P, P], U32, "last_codes")
         quantize_da(TURNED, P, C, da_last[:])
-        dx_out(0, (TURNED,), second_product(2, 0, (TURNED,)))
+        dx_out(0, (TURNED,), second_product(6, 0, (TURNED,)))
         quantize_da(LAST, P, C)
         dx_out(0, (LAST,), second_product(1, 0, (LAST,)), True)
-        late.append(((TURNED, LAST), second_product(2, 1, (TURNED, LAST))))
+        late.append(((TURNED, LAST), second_product(6, 1, (TURNED, LAST))))
         dx.append(shared("da_rows51", [P, S], F32, "dx1"))
         for experts, acc in late:
             dx_out(1, experts, acc)

@@ -1,7 +1,6 @@
 from contextlib import ExitStack
 
 import concourse.mybir as mybir
-from concourse.masks import make_identity
 
 K, T, E, C, H, N = 256, 512, 6, 256, 512, 512
 S = E * C
@@ -11,10 +10,7 @@ TOP = 3
 PER_COLUMN = 16
 FLOPS = 2 * S * H * (N + K)
 BYTES = 4 * (N * T + H * S + S + K * T) + E * H * (N + K) // 2 + E * H * (N + K) // 32 + 2 * (S + TOP * T)
-
-LAST = E - 1
-TURNED = 1
-WHOLE = tuple(e for e in range(E) if e != TURNED)
+LAP = 64
 
 F32 = mybir.dt.float32
 BF16 = mybir.dt.bfloat16
@@ -34,7 +30,6 @@ def tile_moe_bdx_mlp_relu2_kernel(
     nc = tc.nc
     with ExitStack() as ctx:
         keep = ctx.enter_context(tc.tile_pool(name="keep", bufs=1))
-        reuse = ctx.enter_context(tc.tile_pool(name="reuse", bufs=1))
         placed = ctx.enter_context(tc.tile_pool(name="placed", bufs=1))
         psum = ctx.enter_context(tc.psum_pool(name="psum", bufs=1))
 
@@ -47,25 +42,49 @@ def tile_moe_bdx_mlp_relu2_kernel(
         def tiles(count, shape, dtype, name):
             return [tile(shape, dtype, "%s%d" % (name, x)) for x in range(count)]
 
-        def shared(tag, shape, dtype, name):
-            return reuse.tile(shape, dtype, name=name, tag=tag, align_bytes=64)
+        def at(offset, shape, dtype, name):
+            return placed.tile(shape, dtype, name=name, offset=offset, align_bytes=64)
+
+        WIDE = PACK * C * 4
+        NARROW = PACK * C * 2
+        at_dh1 = 0
+        at_a3 = at_dh1 + WIDE - LAP
+        at_mixed = at_a3 + WIDE - LAP
+        at_da4 = at_mixed + LAP - NARROW
+        at_da1 = at_mixed + WIDE - LAP
+        at_da23 = at_da1 + NARROW - LAP
+        at_g32 = [at_da23, at_da23 + WIDE]
+        at_a0 = at_da23 + 2 * WIDE
+        at_g2 = at_a0 + WIDE
+        at_raw23 = at_g2 + NARROW - LAP
+        at_w45 = at_raw23 + NARROW - LAP
+        at_g3 = at_w45 + NARROW
+        at_raw45 = at_g3 + NARROW - LAP
+        at_dh0 = at_raw45 + NARROW - LAP
 
         offs_sb = keep.tile([P, S // PER_COLUMN], U16, name="offs_sb")
         pos_sb = [keep.tile([P, T // PER_COLUMN], U16, name="pos_sb%d" % r) for r in range(TOP)]
-        dy = [shared("dy%d" % d, [P, T], F32, "dy%d" % d) for d in range(PACK)]
+        dy = tiles(PACK, [P, T], F32, "dy")
         gate_sb = tile([P, S], F32, "gate_sb")
-        w2 = tile([P, E, 2 * H], U8, "w2")
+        raw = [
+            tile([P, 2, 2 * H], U8, "raw01"),
+            at(at_raw23, [P, 2, 2 * H], U8, "raw23"),
+            at(at_raw45, [P, 2, 2 * H], U8, "raw45"),
+        ]
+        w2 = {}
         w1 = tile([P, E, 2 * K], U8, "w1")
+        s2_raw = tile([P, 3 * H], U8, "s2_raw")
+        s2_rows = tile([P, 3 * H], U8, "s2_rows")
         s2 = tile([P, E, H], U8, "s2")
         s1 = tile([P, E, K], U8, "s1")
-        a_sb = [shared("a%d" % e, [P, PACK, C], F32, "a_sb%d" % e) for e in range(E)]
-        ident_made = tile([P, P], F32, "ident_made")
-        ident = tile([P, P], F32, "ident")
+        a_sb = {e: tile([P, PACK, C], F32, "a_sb%d" % e) for e in (1, 2, 4, 5)}
+        a_sb[3] = at(at_a3, [P, PACK, C], F32, "a_sb3")
+        a_sb[0] = at(at_a0, [P, PACK, C], F32, "a_sb0")
 
-        make_identity(nc, ident_made[:])
+        nc.vector.memset(s2_raw[32:64, :].bitcast(I32), 0)
+        nc.vector.memset(s2_raw[64:P, :].bitcast(I32), 0)
         nc.gpsimd.memset(s2[:].bitcast(I32), 0)
         nc.gpsimd.memset(s1[:].bitcast(I32), 0)
-        nc.scalar.copy(out=ident[:], in_=ident_made[:])
 
         dy_planes = dyT.rearrange("(p d) c -> p d c", d=PACK)
         a_planes = a.rearrange("(p d) s -> p d s", d=PACK)
@@ -73,75 +92,69 @@ def tile_moe_bdx_mlp_relu2_kernel(
         def load_gate(e0, e1):
             nc.sync.dma_start(out=gate_sb[:, e0 * C : e1 * C], in_=gate[0:P, e0 * C : e1 * C])
 
-        def load_a(e, planes=PACK):
-            for d in range(0, PACK, planes):
-                nc.sync.dma_start(
-                    out=a_sb[e][:, d : d + planes, :], in_=a_planes[:, d : d + planes, e * C : (e + 1) * C]
-                )
+        def load_a(e):
+            nc.sync.dma_start(out=a_sb[e][:], in_=a_planes[:, :, e * C : (e + 1) * C])
 
         def load_words(dst, src, e0, e1):
             nc.sync.dma_start(
-                out=dst[:, e0:e1].bitcast(I32),
+                out=dst[:].bitcast(I32),
                 in_=src[e0:e1, 0].rearrange("e p n -> p e n").bitcast(I32),
             )
 
-        def load_scales(dst, src):
-            for r in range(4):
-                nc.sync.dma_start(
-                    out=dst[r:P:32].bitcast(I32),
-                    in_=src[:, 0, r:16:4, :].rearrange("e q n -> q e n").bitcast(I32),
-                )
-
+        nc.sync.dma_start(
+            out=s2_raw[0:32, :].rearrange("p (b n) -> p b n", b=3).bitcast(I32),
+            in_=w2_scales.rearrange("(b x) s f n -> (x s f) b n", x=2).bitcast(I32),
+        )
         nc.sync.dma_start(offs_sb[:], offs)
         load_gate(0, 1)
         for d in range(PACK):
             nc.sync.dma_start(out=dy[d][:], in_=dy_planes[:, d, :])
+        nc.vector.tensor_copy(
+            out=s2_rows[:].rearrange("p (b d c i) -> p c b d i", b=3, d=PACK, i=16),
+            in_=s2_raw[:].rearrange("p (b c i d) -> p c b d i", b=3, d=PACK, i=16),
+        )
+        load_words(raw[0], w2_words, 0, 2)
         load_gate(1, 2)
-        load_a(0, 2)
+        load_a(0)
         load_gate(2, 4)
-        load_a(2, 2)
-        load_a(3)
-        load_gate(4, 5)
-        load_scales(s2, w2_scales)
-        load_words(w2, w2_words, 0, 2)
-        load_gate(5, E)
-        load_a(4)
-        load_a(5)
-        load_a(TURNED)
-        load_words(w2, w2_words, 2, 4)
-        load_words(w2, w2_words, 4, E)
+        load_words(raw[1], w2_words, 2, 4)
+        load_words(raw[2], w2_words, 4, E)
+        load_gate(4, E)
+        for x in range(2):
+            for q in range(4):
+                nc.sync.dma_start(
+                    out=s2[32 * q : 32 * q + 4, x:E:2, :].bitcast(I32),
+                    in_=s2_rows[16 * x + 4 * q : 16 * x + 4 * q + 4, :].rearrange("p (b n) -> p b n", b=3).bitcast(I32),
+                )
+        for e in (3, 2, 1, 5, 4):
+            load_a(e)
         load_words(w1, w1_words, 0, E)
-        load_scales(s1, w1_scales)
+        for r in range(4):
+            nc.sync.dma_start(
+                out=s1[r:P:32].bitcast(I32),
+                in_=w1_scales[:, 0, r:16:4, :].rearrange("e q n -> q e n").bitcast(I32),
+            )
         for r, pos in enumerate((pos1, pos2, pos3)):
             nc.sync.dma_start(pos_sb[r][:], pos)
 
+        g32 = {}
         g16 = {}
-        g_codes = {}
-        g_scales = tiles(E, [P, C], U8, "g_scales")
+        g_codes = tiles(E - 1, [P, C], U32, "g_codes")
+        g_scales = tiles(E - 1, [P, C], U8, "g_scales")
         slope = {}
-        da16 = {e: tile([P, C, PACK], BF16, "da16_%d" % e) for e in range(E) if e != 2}
-        da16[2] = placed.tile([P, C, PACK], BF16, name="da16_2", offset=12288, align_bytes=64)
-        dx = [tile([P, S], F32, "dx0")]
-        da_codes = tile([P, S], U32, "da_codes")
-        da_scales = tile([P, S], U8, "da_scales")
-        dh_rows = tile([P, 2, H], F32, "dh_rows")
-        slope_first = tile([P, 2, H], F32, "slope_first")
+        dh_rows = {}
         dh_bank = {}
-        da_rows = {}
-        words = {}
-        apart = {}
+        da16 = {}
+        da_codes = {}
+        da_scales = tile([P, S], U8, "da_scales")
+        scales_of = {e: da_scales[:, e * C : (e + 1) * C] for e in range(1, E)}
+        dx = tiles(2, [P, S], F32, "dx")
 
-        def from_planes(ap):
-            return ap.rearrange("p d (c i) -> p c d i", i=4)
+        def from_planes(ap, run):
+            return ap.rearrange("p d (c i) -> p c d i", i=run)
 
-        def side_by_side(ap):
-            return ap.rearrange("p (c i) d -> p c d i", i=4)
-
-        def by_words(ap):
-            return ap.rearrange("s (u p t) -> s u p t", u=2, t=2)
-
-        def regrouped(bank):
-            return bank.rearrange("s (p u t) -> s u p t", u=2, t=2)
+        def side_by_side(ap, run):
+            return ap.rearrange("p (c i) d -> p c d i", i=run)
 
         def quantize(codes, scales, values):
             nc.vector.quantize_mx(out=codes.bitcast(FP8X4), scales=scales, in_=values.rearrange("p c d -> p (c d)"))
@@ -157,236 +170,200 @@ def tile_moe_bdx_mlp_relu2_kernel(
                 stop=True,
             )
 
+        def regroup(pair, offset=None):
+            if offset is None:
+                w2[pair] = tile([P, 2, 2 * H], U8, "w2_%d" % pair)
+            else:
+                w2[pair] = at(offset, [P, 2, 2 * H], U8, "w2_%d" % pair)
+            nc.scalar.copy(
+                out=w2[pair][:].bitcast(U16).rearrange("p e (d c i) -> p e c d i", d=PACK, i=8),
+                in_=raw[pair][:].bitcast(U16).rearrange("p e (c i d) -> p e c d i", d=PACK, i=8),
+            )
+
         def gather(e):
-            g32 = placed.tile([P, PACK, C], F32, name="g32_%d" % e, offset=4096 + e % 2 * 4096, align_bytes=64)
+            g32[e] = at(at_g32[e % 2], [P, PACK, C], F32, "g32_%d" % e)
             entries = offs_sb[:, e * C // PER_COLUMN : (e + 1) * C // PER_COLUMN]
             for d in range(PACK):
                 nc.vector.tensor_tensor(
-                    g32[:, d, :], dy[d][:].indirect(entries), gate_sb[:, e * C : (e + 1) * C], ALU.mult
+                    g32[e][:, d, :], dy[d][:].indirect(entries), gate_sb[:, e * C : (e + 1) * C], ALU.mult
                 )
-            return g32
 
-        def g16_tag(e):
-            return {1: "a0", 2: "a2", 3: "a3", 4: "g_codes1", 5: "a4"}.get(e, "g16_%d" % e)
-
-        def interleave(e, g32):
-            g16[e] = shared(g16_tag(e), [P, C, PACK], BF16, "g16_%d" % e)
-            nc.scalar.copy(out=side_by_side(g16[e][:]), in_=from_planes(g32[:]))
+        def interleave(e, offset=None):
+            if offset is None:
+                g16[e] = tile([P, C, PACK], BF16, "g16_%d" % e)
+            else:
+                g16[e] = at(offset, [P, C, PACK], BF16, "g16_%d" % e)
+            nc.scalar.copy(out=side_by_side(g16[e][:], 4), in_=from_planes(g32[e][:], 4))
 
         def quantize_g(e):
-            g_codes[e] = shared({LAST - 1: "dy0", LAST: "slope31"}.get(e, "g_codes%d" % e), [P, C], U32, "g_codes%d" % e)
             quantize(g_codes[e][:], g_scales[e][:], g16[e][:])
 
-        def first_product(number, e, half):
-            acc = bank(number, [P, H], "dh%d%d" % (e, half))
-            codes = g_codes[e][:, half * P : (half + 1) * P].bitcast(FP8X4)
-            scales = g_scales[e][:, half * P : (half + 1) * P]
-            one_pass(acc[:], codes, scales, w2[:, e, :].bitcast(FP4X4), s2[:, e, :])
-            dh_bank[e, half] = acc
-
-        def turn_a(number, e, half):
-            turned = bank(number, [P, PACK, P], "turned%d%d" % (e, half))
-            for d in range(PACK):
-                nc.tensor.transpose(turned[:, d, :], a_sb[e][:, d, half * P : (half + 1) * P], ident[:])
-            return turned
-
-        def slope_out(turned, e, half, offset=None):
-            name = "slope%d%d" % (e, half)
-            if e == 0:
-                slope[e, half] = slope_first[:, half, :]
-            elif offset is None:
-                slope[e, half] = shared(name, [P, H], F32, name)[:]
-            else:
-                slope[e, half] = placed.tile([P, H], F32, name=name, offset=offset, align_bytes=64)[:]
-            nc.scalar.activation(
-                out=by_words(slope[e, half]),
-                in_=turned[:].rearrange("s (u t) p -> s u p t", t=2),
-                func=ACT.Relu,
-            )
-
-        def make_slope(number, e, half):
-            slope_out(turn_a(number, e, half), e, half)
-
-        def dh_for_gpsimd(number, half):
-            first_product(number, 0, half)
-            nc.scalar.copy(out=by_words(dh_rows[:, half, :]), in_=regrouped(dh_bank[0, half][:]))
-
-        def da_on_gpsimd(tag):
-            both = shared(tag, [P, 2, H], BF16, "da_rows0")
-            nc.gpsimd.tensor_tensor(both[:], dh_rows[:], slope_first[:], ALU.mult)
+        def first_products(number, e):
             for half in range(2):
-                da_rows[0, half] = both[:, half, :]
+                acc = bank(number + half, [P, PACK, P], "dh%d%d" % (e, half))
+                for d in range(PACK):
+                    one_pass(
+                        acc[:, d, :],
+                        w2[e // 2][:, e % 2, 2 * d * P : 2 * (d + 1) * P].bitcast(FP4X4),
+                        s2[:, e, d * P : (d + 1) * P],
+                        g_codes[e][:, half * P : (half + 1) * P].bitcast(FP8X4),
+                        g_scales[e][:, half * P : (half + 1) * P],
+                    )
+                dh_bank[e, half] = acc
 
-        def third_on_gpsimd(offset):
-            da_rows[TURNED, 0] = placed.tile([P, H], BF16, name="da_rows10", offset=offset, align_bytes=64)[:]
-            nc.gpsimd.tensor_tensor(da_rows[TURNED, 0], dh_third[:], slope[TURNED, 0], ALU.mult)
-
-        def da_on_vector(e, half, offset=None):
-            name = "da_rows%d%d" % (e, half)
-            if not isinstance(offset, int):
-                da_rows[e, half] = shared(offset or name, [P, H], BF16, name)[:]
+        def relu_planes(e, offset=None):
+            if offset is None:
+                slope[e] = tile([P, PACK, C], F32, "slope%d" % e)
             else:
-                da_rows[e, half] = placed.tile([P, H], BF16, name=name, offset=offset, align_bytes=64)[:]
-            nc.vector.tensor_tensor(
-                by_words(da_rows[e, half]), regrouped(dh_bank[e, half][:]), by_words(slope[e, half]), ALU.mult
-            )
+                slope[e] = at(offset, [P, PACK, C], F32, "slope%d" % e)
+            nc.scalar.activation(out=slope[e][:], in_=a_sb[e][:], func=ACT.Relu)
 
-        def turn(number, e, half, halves=2):
-            if number is not None:
-                words[e] = bank(number, [P, halves, 2, P], "words%d%d" % (e, half))
-            for u in range(2):
-                nc.tensor.transpose(
-                    words[e][:, half % halves, u, :], da_rows[e, half].bitcast(F32)[:, u * P : (u + 1) * P], ident[:]
+        def relu_side_by_side(e):
+            slope[e] = tile([P, C, PACK], F32, "slope%d" % e)
+            nc.scalar.activation(out=side_by_side(slope[e][:], 2), in_=from_planes(a_sb[e][:], 2), func=ACT.Relu)
+
+        def dh_out(e, offset):
+            dh_rows[e] = at(offset, [P, C, PACK], F32, "dh_rows%d" % e)
+            for half in range(2):
+                nc.scalar.copy(
+                    out=dh_rows[e][:, half * P : (half + 1) * P, :], in_=dh_bank[e, half][:].rearrange("p d c -> p c d")
                 )
 
-        def words_out(e, c0=0, c1=C):
-            nc.scalar.copy(
-                out=da16[e][:, c0:c1, :]
-                .rearrange("p c d -> p (c d)")
-                .bitcast(F32)
-                .rearrange("p (h s u) -> p h s u", s=P, u=2),
-                in_=words[e][:].rearrange("p h u s -> p h s u"),
-            )
-
-        def rows_of_turned(rows):
-            nc.scalar.copy(out=rows[:], in_=dh_bank[TURNED, 1][:].rearrange("s (p d) -> s d p", d=PACK))
-
-        def planes_of_turned(number, rows):
-            planes = bank(number, [P, PACK, P], "planes")
-            for d in range(PACK):
-                nc.tensor.transpose(planes[:, d, :], rows[:, d, :], ident[:])
-            return planes
-
-        def da_of_turned(planes):
-            da_last = placed.tile([P, P, PACK], BF16, name="da_last", offset=1152, align_bytes=64)
-            nc.vector.scalar_tensor_tensor(
-                da_last[:],
-                a_sb[TURNED][:, :, P:].rearrange("p d c -> p c d"),
-                0.0,
-                planes[:].rearrange("p d c -> p c d"),
-                ALU.max,
+        def da_on_gpsimd(e):
+            nc.gpsimd.tensor_tensor(
+                da16[e].rearrange("p c d -> p (c d)"),
+                dh_rows[e][:].rearrange("p c d -> p (c d)"),
+                slope[e][:].rearrange("p c d -> p (c d)"),
                 ALU.mult,
             )
-            return da_last
 
-        def da_operand(e, c0, c1):
-            if (e, c0) in apart:
-                return apart[e, c0][:], da_scales[:, e * C + c0 : e * C + c1]
-            return da_codes[:, e * C + c0 : e * C + c1], da_scales[:, e * C + c0 : e * C + c1]
+        def da_on_vector(e):
+            for half in range(2):
+                nc.vector.tensor_tensor(
+                    side_by_side(da16[e][:, half * P : (half + 1) * P, :], 2),
+                    from_planes(dh_bank[e, half][:], 2),
+                    from_planes(slope[e][:, :, half * P : (half + 1) * P], 2),
+                    ALU.mult,
+                )
 
-        def quantize_da(e, c0=0, c1=C, values=None):
-            quantize(*da_operand(e, c0, c1), da16[e][:, c0:c1, :] if values is None else values)
+        def da_with_relu(e):
+            for half in range(2):
+                nc.vector.scalar_tensor_tensor(
+                    da16[e][:, half * P : (half + 1) * P, :],
+                    a_sb[e][:, :, half * P : (half + 1) * P].rearrange("p d c -> p c d"),
+                    0.0,
+                    dh_bank[e, half][:].rearrange("p d c -> p c d"),
+                    ALU.max,
+                    ALU.mult,
+                )
+
+        def quantize_da(e):
+            quantize(da_codes[e], scales_of[e], da16[e])
 
         def second_product(number, kh, experts):
             acc = bank(number, [P, len(experts), C], "dx%d_%d" % (kh, experts[0]))
             for x, e in enumerate(experts):
-                width = P if e in (TURNED, LAST) else C
-                for c0 in range(0, C, width):
-                    codes, scales = da_operand(e, c0, c0 + width)
-                    one_pass(
-                        acc[:, x, c0 : c0 + width],
-                        w1[:, e, 2 * kh * P : 2 * (kh + 1) * P].bitcast(FP4X4),
-                        s1[:, e, kh * P : (kh + 1) * P],
-                        codes.bitcast(FP8X4),
-                        scales,
-                    )
+                one_pass(
+                    acc[:, x, :],
+                    w1[:, e, 2 * kh * P : 2 * (kh + 1) * P].bitcast(FP4X4),
+                    s1[:, e, kh * P : (kh + 1) * P],
+                    da_codes[e].bitcast(FP8X4),
+                    scales_of[e],
+                )
             return acc
 
         def dx_out(kh, experts, acc, on_vector=False):
-            by_expert = dx[kh][:].rearrange("p (e c) -> p e c", c=C)
-            step = max(experts[-1] - experts[0], 1)
-            dst = by_expert[:, experts[0] : experts[-1] + 1 : step, :]
+            dst = dx[kh][:, experts[0] * C : (experts[-1] + 1) * C].rearrange("p (e c) -> p e c", c=C)
             if on_vector:
                 nc.vector.tensor_scalar_mul(dst, acc[:], 2.0)
             else:
                 nc.scalar.activation(out=dst, in_=acc[:], func=ACT.Copy, scale=2.0)
 
-        rows = tile([P, PACK, P], F32, "rows")
-        g32 = [gather(0)]
-        for e in range(4):
-            interleave(e, g32[e])
-            g32.append(gather(e + 1))
-            if e < 3:
-                for half in range(2):
-                    make_slope(2 * e % 4 + half, WHOLE[e], half)
-            quantize_g(e)
-        dh_for_gpsimd(6, 0)
-        dh_for_gpsimd(7, 1)
-        first_product(5, TURNED, 1)
-        rows_of_turned(rows)
-        first_product(1, TURNED, 0)
-        dh_third = tile([P, H], F32, "dh_third")
-        nc.scalar.copy(out=by_words(dh_third[:]), in_=regrouped(dh_bank[TURNED, 0][:]))
-        interleave(4, g32[4])
-        g32.append(gather(LAST))
-        make_slope(3, 4, 0)
-        make_slope(4, 4, 1)
-        interleave(LAST, g32[LAST])
-        turned_last = [turn_a(2, LAST, 0), turn_a(7, LAST, 1)]
-        first_product(0, 2, 0)
-        first_product(1, 2, 1)
-        first_product(6, 3, 0)
-
+        regroup(0)
+        gather(0)
+        interleave(0)
+        gather(1)
+        relu_side_by_side(0)
+        quantize_g(0)
+        first_products(0, 0)
+        interleave(1, at_a0)
+        gather(2)
+        regroup(1, at_a0 + NARROW)
+        quantize_g(1)
+        first_products(2, 1)
+        interleave(2, at_g2)
+        gather(3)
+        regroup(2, at_w45)
+        quantize_g(2)
+        first_products(4, 2)
+        interleave(3, at_g3)
+        gather(4)
+        dh_out(0, at_dh0)
+        relu_planes(3)
+        quantize_g(3)
+        first_products(6, 3)
+        interleave(4, at_mixed)
+        gather(5)
+        dh_out(1, at_dh1)
         quantize_g(4)
-        da_on_gpsimd(g16_tag(4))
-        first_product(3, 4, 0)
-        da_on_vector(2, 0, 5120)
-        first_product(0, 3, 1)
-        turn(5, 2, 0)
-        da_on_vector(2, 1, 7168)
-        turn(None, 2, 1)
-        words_out(2)
-        slope_out(turn_a(1, TURNED, 0), TURNED, 0, 8128)
-        slope_out(turned_last[0], LAST, 0, 10240)
-        da_on_vector(3, 0, 3136)
-        turn(4, 3, 0)
-        slope_out(turned_last[1], LAST, 1, 1152)
-        da_on_vector(3, 1)
-        first_product(6, 4, 1)
-        turn(None, 3, 1)
-        words_out(3)
-        da_on_vector(4, 0)
-        quantize_g(LAST)
-        first_product(0, LAST, 0)
-        first_product(1, LAST, 1)
-        turn(5, 0, 0)
-        turn(None, 0, 1)
-        words_out(0)
-        turn(3, 4, 0)
-        quantize_da(2)
-        third_on_gpsimd(13312)
-        da_on_vector(4, 1, g16_tag(LAST))
-        turn(None, 4, 1)
-        words_out(4)
-        planes = planes_of_turned(2, rows)
-        da_on_vector(LAST, 0)
-        turn(7, LAST, 0, 1)
-        words_out(LAST, 0, P)
-        turn(6, TURNED, 0, 1)
-        words_out(TURNED, 0, P)
-        da_on_vector(LAST, 1)
-        turn(0, LAST, 1, 1)
-        words_out(LAST, P, C)
-        apart[3, 0] = placed.tile([P, C], U32, name="codes3", offset=10240, align_bytes=64)
-        quantize_da(3)
-        dx_out(0, (2, 3), second_product(4, 0, (2, 3)))
-        late = [((2, 3), second_product(5, 1, (2, 3)))]
-        quantize_da(0)
-        da_last = da_of_turned(planes)
+        first_products(0, 4)
+        mixed = at(at_mixed, [P, 2 * C, PACK], BF16, "mixed")
+        nc.scalar.copy(out=side_by_side(mixed[:, :C, :], 4), in_=from_planes(g32[5][:], 4))
+        relu_side_by_side(1)
+        relu_planes(5)
+
+        da16[0] = mixed[:, C:, :]
+        da_on_gpsimd(0)
+        da23 = at(at_da23, [P, 2 * C, PACK], BF16, "da23")
+        da16[2] = da23[:, :C, :]
+        da16[3] = da23[:, C:, :]
+        da_with_relu(2)
+        da_on_vector(3)
+        mixed_codes = tile([P, 2 * C], U32, "mixed_codes")
+        mixed_scales = tile([P, 2 * C], U8, "mixed_scales")
+        quantize(mixed_codes[:], mixed_scales[:], mixed[:])
+        g_codes.append(mixed_codes[:, :C])
+        g_scales.append(mixed_scales[:, :C])
+        da_codes[0] = mixed_codes[:, C:]
+        scales_of[0] = mixed_scales[:, C:]
+        first_products(2, 5)
+        codes23 = at(at_dh0 + NARROW, [P, 2 * C], U32, "codes23")
+        da_codes[2] = codes23[:, :C]
+        da_codes[3] = codes23[:, C:]
+        quantize(codes23[:], da_scales[:, 2 * C : 4 * C], da23[:])
+        da16[1] = at(at_da1, [P, C, PACK], BF16, "da16_1")[:]
+        da_on_gpsimd(1)
+        da16[4] = at(at_da4, [P, C, PACK], BF16, "da16_4")[:]
+        da_with_relu(4)
+        da16[5] = tile([P, C, PACK], BF16, "da16_5")[:]
+        da_on_vector(5)
+        dx_out(0, (0,), second_product(4, 0, (0,)))
+        dx_out(0, (2, 3), second_product(5, 0, (2, 3)))
+        dx_out(1, (0,), second_product(6, 1, (0,)))
+        dx_out(1, (2, 3), second_product(7, 1, (2, 3)))
+        da_codes[5] = at(at_dh1, [P, C], U32, "da_codes5")[:]
+        quantize_da(5)
+        dx_out(0, (5,), second_product(0, 0, (5,)))
+        da_codes[4] = at(at_dh1 + 4 * C, [P, C], U32, "da_codes4")[:]
         quantize_da(4)
-        dx_out(0, (0, 4), second_product(3, 0, (0, 4)))
-        late.append(((0, 4), second_product(7, 1, (0, 4))))
-        quantize_da(LAST, 0, P)
-        quantize_da(TURNED, 0, P)
-        apart[TURNED, P] = shared("da_rows51", [P, P], U32, "last_codes")
-        quantize_da(TURNED, P, C, da_last[:])
-        dx_out(0, (TURNED,), second_product(6, 0, (TURNED,)))
-        quantize_da(LAST, P, C)
-        dx_out(0, (LAST,), second_product(1, 0, (LAST,)), True)
-        late.append(((TURNED, LAST), second_product(6, 1, (TURNED, LAST))))
-        dx.append(shared("da_rows51", [P, S], F32, "dx1"))
-        for experts, acc in late:
-            dx_out(1, experts, acc)
+        dx_out(0, (4,), second_product(1, 0, (4,)))
+        da_codes[1] = tile([P, C], U32, "da_codes1")[:]
+        for half in range(2):
+            slots = slice(half * P, (half + 1) * P)
+            quantize(da_codes[1][:, slots], scales_of[1][:, slots], da16[1][:, slots, :])
+        for half in range(2):
+            slots = slice(half * P, (half + 1) * P)
+            acc = bank(2 + half, [P, P], "dx_last%d" % half)
+            one_pass(
+                acc[:],
+                w1[:, 1, 0 : 2 * P].bitcast(FP4X4),
+                s1[:, 1, 0:P],
+                da_codes[1][:, slots].bitcast(FP8X4),
+                scales_of[1][:, slots],
+            )
+            nc.vector.tensor_scalar_mul(dx[0][:, C + half * P : C + (half + 1) * P], acc[:], 2.0)
+        dx_out(1, (1,), second_product(1, 1, (1,)))
+        dx_out(1, (4, 5), second_product(3, 1, (4, 5)))
 
         sums = [tiles(TOP, [P, T], F32, "sums%d_" % kh) for kh in range(K // P)]
 

@@ -11,6 +11,7 @@ PER_COLUMN = 16
 FLOPS = 2 * S * H * (N + K)
 BYTES = 4 * (N * T + H * S + S + K * T) + E * H * (N + K) // 2 + E * H * (N + K) // 32 + 2 * (S + TOP * T)
 LAP = 64
+SPARE = 32
 
 F32 = mybir.dt.float32
 BF16 = mybir.dt.bfloat16
@@ -53,36 +54,35 @@ def tile_moe_bdx_mlp_relu2_kernel(
         at_da4 = at_mixed + LAP - NARROW
         at_da1 = at_mixed + WIDE - LAP
         at_da23 = at_da1 + NARROW - LAP
-        at_g32 = [at_da23, at_da23 + WIDE]
-        at_a0 = at_da23 + 2 * WIDE
-        at_g2 = at_a0 + WIDE
-        at_raw23 = at_g2 + NARROW - LAP
-        at_w45 = at_raw23 + NARROW - LAP
-        at_g3 = at_w45 + NARROW
-        at_raw45 = at_g3 + NARROW - LAP
+        at_g32 = {0: at_da23, 3: at_da23, 1: at_da23 + 2 * WIDE, 5: at_da23 + 2 * WIDE}
+        at_g12 = at_da23 + 4 * WIDE
+        at_raw45 = at_g12 + WIDE - LAP
         at_dh0 = at_raw45 + NARROW - LAP
+        at_raw0 = at_dh0 + WIDE
+        at_g0 = at_raw0 + 2 * H - LAP
 
         offs_sb = keep.tile([P, S // PER_COLUMN], U16, name="offs_sb")
         pos_sb = [keep.tile([P, T // PER_COLUMN], U16, name="pos_sb%d" % r) for r in range(TOP)]
-        dy = tiles(PACK, [P, T], F32, "dy")
+        dy = tiles(PACK, [P, T + SPARE], F32, "dy")
         gate_sb = tile([P, S], F32, "gate_sb")
-        raw = [
-            tile([P, 2, 2 * H], U8, "raw01"),
-            at(at_raw23, [P, 2, 2 * H], U8, "raw23"),
-            at(at_raw45, [P, 2, 2 * H], U8, "raw45"),
-        ]
+        raw = {
+            0: at(at_raw0, [P, 1, 2 * H], U8, "raw0"),
+            1: tile([P, 3, 2 * H], U8, "raw123"),
+            4: at(at_raw45, [P, 2, 2 * H], U8, "raw45"),
+        }
         w2 = {}
         w1 = tile([P, E, 2 * K], U8, "w1")
         s2_raw = tile([P, 3 * H], U8, "s2_raw")
         s2_rows = tile([P, 3 * H], U8, "s2_rows")
         s2 = tile([P, E, H], U8, "s2")
         s1 = tile([P, E, K], U8, "s1")
-        a_sb = {e: tile([P, PACK, C], F32, "a_sb%d" % e) for e in (1, 2, 4, 5)}
+        a_sb = {e: tile([P, PACK, C], F32, "a_sb%d" % e) for e in (0, 1, 2, 4, 5)}
         a_sb[3] = at(at_a3, [P, PACK, C], F32, "a_sb3")
-        a_sb[0] = at(at_a0, [P, PACK, C], F32, "a_sb0")
 
         nc.vector.memset(s2_raw[32:64, :].bitcast(I32), 0)
         nc.vector.memset(s2_raw[64:P, :].bitcast(I32), 0)
+        for d in range(PACK):
+            nc.gpsimd.memset(dy[d][:, T:], 0.0)
         nc.gpsimd.memset(s2[:].bitcast(I32), 0)
         nc.gpsimd.memset(s1[:].bitcast(I32), 0)
 
@@ -108,25 +108,24 @@ def tile_moe_bdx_mlp_relu2_kernel(
         nc.sync.dma_start(offs_sb[:], offs)
         load_gate(0, 1)
         for d in range(PACK):
-            nc.sync.dma_start(out=dy[d][:], in_=dy_planes[:, d, :])
+            nc.sync.dma_start(out=dy[d][:, :T], in_=dy_planes[:, d, :])
         nc.vector.tensor_copy(
             out=s2_rows[:].rearrange("p (b d c i) -> p c b d i", b=3, d=PACK, i=16),
             in_=s2_raw[:].rearrange("p (b c i d) -> p c b d i", b=3, d=PACK, i=16),
         )
-        load_words(raw[0], w2_words, 0, 2)
-        load_gate(1, 2)
+        load_gate(1, 3)
+        load_words(raw[0], w2_words, 0, 1)
+        load_words(raw[1], w2_words, 1, 4)
         load_a(0)
-        load_gate(2, 4)
-        load_words(raw[1], w2_words, 2, 4)
-        load_words(raw[2], w2_words, 4, E)
-        load_gate(4, E)
         for x in range(2):
             for q in range(4):
                 nc.sync.dma_start(
                     out=s2[32 * q : 32 * q + 4, x:E:2, :].bitcast(I32),
                     in_=s2_rows[16 * x + 4 * q : 16 * x + 4 * q + 4, :].rearrange("p (b n) -> p b n", b=3).bitcast(I32),
                 )
-        for e in (3, 2, 1, 5, 4):
+        load_words(raw[4], w2_words, 4, E)
+        load_gate(3, E)
+        for e in (3, 2, 4, 1, 5):
             load_a(e)
         load_words(w1, w1_words, 0, E)
         for r in range(4):
@@ -139,8 +138,8 @@ def tile_moe_bdx_mlp_relu2_kernel(
 
         g32 = {}
         g16 = {}
-        g_codes = tiles(E - 1, [P, C], U32, "g_codes")
-        g_scales = tiles(E - 1, [P, C], U8, "g_scales")
+        g_codes = {}
+        g_scales = {}
         slope = {}
         dh_rows = {}
         dh_bank = {}
@@ -170,33 +169,35 @@ def tile_moe_bdx_mlp_relu2_kernel(
                 stop=True,
             )
 
-        def regroup(pair, offset=None):
-            if offset is None:
-                w2[pair] = tile([P, 2, 2 * H], U8, "w2_%d" % pair)
-            else:
-                w2[pair] = at(offset, [P, 2, 2 * H], U8, "w2_%d" % pair)
+        def regroup(first):
+            count = raw[first].shape[1]
+            words = tile([P, count, 2 * H], U8, "w2_%d" % first)
             nc.scalar.copy(
-                out=w2[pair][:].bitcast(U16).rearrange("p e (d c i) -> p e c d i", d=PACK, i=8),
-                in_=raw[pair][:].bitcast(U16).rearrange("p e (c i d) -> p e c d i", d=PACK, i=8),
+                out=words[:].bitcast(U16).rearrange("p e (d c i) -> p e c d i", d=PACK, i=4),
+                in_=raw[first][:].bitcast(U16).rearrange("p e (c i d) -> p e c d i", d=PACK, i=4),
             )
+            for x in range(count):
+                w2[first + x] = words[:, x, :]
 
-        def gather(e):
-            g32[e] = at(at_g32[e % 2], [P, PACK, C], F32, "g32_%d" % e)
-            entries = offs_sb[:, e * C // PER_COLUMN : (e + 1) * C // PER_COLUMN]
+        def gather(e, count):
+            g32[e] = at(at_g32[e], [P, PACK, count * C], F32, "g32_%d" % e)
+            entries = offs_sb[:, e * C // PER_COLUMN : (e + count) * C // PER_COLUMN]
             for d in range(PACK):
                 nc.vector.tensor_tensor(
-                    g32[e][:, d, :], dy[d][:].indirect(entries), gate_sb[:, e * C : (e + 1) * C], ALU.mult
+                    g32[e][:, d, :], dy[d][:].indirect(entries), gate_sb[:, e * C : (e + count) * C], ALU.mult
                 )
 
-        def interleave(e, offset=None):
-            if offset is None:
-                g16[e] = tile([P, C, PACK], BF16, "g16_%d" % e)
-            else:
-                g16[e] = at(offset, [P, C, PACK], BF16, "g16_%d" % e)
-            nc.scalar.copy(out=side_by_side(g16[e][:], 4), in_=from_planes(g32[e][:], 4))
+        def interleave(e, values):
+            g16[e] = values
+            nc.scalar.copy(out=side_by_side(values, 2), in_=from_planes(g32[e][:], 2))
 
-        def quantize_g(e):
-            quantize(g_codes[e][:], g_scales[e][:], g16[e][:])
+        def quantize_g(e, count):
+            codes = tile([P, count * C], U32, "g_codes%d" % e)
+            scales = tile([P, count * C], U8, "g_scales%d" % e)
+            quantize(codes[:], scales[:], g16[e])
+            for x in range(count):
+                g_codes[e + x] = codes[:, x * C : (x + 1) * C]
+                g_scales[e + x] = scales[:, x * C : (x + 1) * C]
 
         def first_products(number, e):
             for half in range(2):
@@ -204,22 +205,18 @@ def tile_moe_bdx_mlp_relu2_kernel(
                 for d in range(PACK):
                     one_pass(
                         acc[:, d, :],
-                        w2[e // 2][:, e % 2, 2 * d * P : 2 * (d + 1) * P].bitcast(FP4X4),
+                        w2[e][:, 2 * d * P : 2 * (d + 1) * P].bitcast(FP4X4),
                         s2[:, e, d * P : (d + 1) * P],
                         g_codes[e][:, half * P : (half + 1) * P].bitcast(FP8X4),
                         g_scales[e][:, half * P : (half + 1) * P],
                     )
                 dh_bank[e, half] = acc
 
-        def relu_planes(e, offset=None):
+        def relu(e, offset=None):
             if offset is None:
-                slope[e] = tile([P, PACK, C], F32, "slope%d" % e)
+                slope[e] = tile([P, C, PACK], F32, "slope%d" % e)
             else:
-                slope[e] = at(offset, [P, PACK, C], F32, "slope%d" % e)
-            nc.scalar.activation(out=slope[e][:], in_=a_sb[e][:], func=ACT.Relu)
-
-        def relu_side_by_side(e):
-            slope[e] = tile([P, C, PACK], F32, "slope%d" % e)
+                slope[e] = at(offset, [P, C, PACK], F32, "slope%d" % e)
             nc.scalar.activation(out=side_by_side(slope[e][:], 2), in_=from_planes(a_sb[e][:], 2), func=ACT.Relu)
 
         def dh_out(e, offset):
@@ -240,9 +237,9 @@ def tile_moe_bdx_mlp_relu2_kernel(
         def da_on_vector(e):
             for half in range(2):
                 nc.vector.tensor_tensor(
-                    side_by_side(da16[e][:, half * P : (half + 1) * P, :], 2),
-                    from_planes(dh_bank[e, half][:], 2),
-                    from_planes(slope[e][:, :, half * P : (half + 1) * P], 2),
+                    da16[e][:, half * P : (half + 1) * P, :],
+                    dh_bank[e, half][:].rearrange("p d c -> p c d"),
+                    slope[e][:, half * P : (half + 1) * P, :],
                     ALU.mult,
                 )
 
@@ -280,37 +277,31 @@ def tile_moe_bdx_mlp_relu2_kernel(
                 nc.scalar.activation(out=dst, in_=acc[:], func=ACT.Copy, scale=2.0)
 
         regroup(0)
-        gather(0)
-        interleave(0)
-        gather(1)
-        relu_side_by_side(0)
-        quantize_g(0)
+        gather(0, 1)
+        interleave(0, at(at_g0, [P, C, PACK], BF16, "g16_0")[:])
+        gather(1, 2)
+        regroup(1)
+        relu(0)
+        regroup(4)
+        quantize_g(0, 1)
         first_products(0, 0)
-        interleave(1, at_a0)
-        gather(2)
-        regroup(1, at_a0 + NARROW)
-        quantize_g(1)
-        first_products(2, 1)
-        interleave(2, at_g2)
-        gather(3)
-        regroup(2, at_w45)
-        quantize_g(2)
-        first_products(4, 2)
-        interleave(3, at_g3)
-        gather(4)
+        interleave(1, at(at_g12, [P, 2 * C, PACK], BF16, "g16_1")[:])
+        gather(3, 2)
         dh_out(0, at_dh0)
-        relu_planes(3)
-        quantize_g(3)
-        first_products(6, 3)
-        interleave(4, at_mixed)
-        gather(5)
+        relu(3)
+        quantize_g(1, 2)
+        first_products(2, 1)
+        first_products(4, 2)
+        interleave(3, at(at_mixed, [P, 2 * C, PACK], BF16, "g16_3")[:])
+        gather(5, 1)
         dh_out(1, at_dh1)
-        quantize_g(4)
+        quantize_g(3, 2)
+        first_products(6, 3)
         first_products(0, 4)
         mixed = at(at_mixed, [P, 2 * C, PACK], BF16, "mixed")
-        nc.scalar.copy(out=side_by_side(mixed[:, :C, :], 4), in_=from_planes(g32[5][:], 4))
-        relu_side_by_side(1)
-        relu_planes(5)
+        interleave(5, mixed[:, :C, :])
+        relu(1)
+        relu(5)
 
         da16[0] = mixed[:, C:, :]
         da_on_gpsimd(0)
@@ -322,8 +313,8 @@ def tile_moe_bdx_mlp_relu2_kernel(
         mixed_codes = tile([P, 2 * C], U32, "mixed_codes")
         mixed_scales = tile([P, 2 * C], U8, "mixed_scales")
         quantize(mixed_codes[:], mixed_scales[:], mixed[:])
-        g_codes.append(mixed_codes[:, :C])
-        g_scales.append(mixed_scales[:, :C])
+        g_codes[5] = mixed_codes[:, :C]
+        g_scales[5] = mixed_scales[:, :C]
         da_codes[0] = mixed_codes[:, C:]
         scales_of[0] = mixed_scales[:, C:]
         first_products(2, 5)
@@ -339,14 +330,14 @@ def tile_moe_bdx_mlp_relu2_kernel(
         da_on_vector(5)
         dx_out(0, (0,), second_product(4, 0, (0,)))
         dx_out(0, (2, 3), second_product(5, 0, (2, 3)))
-        dx_out(1, (0,), second_product(6, 1, (0,)))
-        dx_out(1, (2, 3), second_product(7, 1, (2, 3)))
+        dx_out(1, (0,), second_product(0, 1, (0,)))
+        dx_out(1, (2, 3), second_product(1, 1, (2, 3)))
         da_codes[5] = at(at_dh1, [P, C], U32, "da_codes5")[:]
         quantize_da(5)
-        dx_out(0, (5,), second_product(0, 0, (5,)))
+        dx_out(0, (5,), second_product(6, 0, (5,)))
         da_codes[4] = at(at_dh1 + 4 * C, [P, C], U32, "da_codes4")[:]
         quantize_da(4)
-        dx_out(0, (4,), second_product(1, 0, (4,)))
+        dx_out(0, (4,), second_product(7, 0, (4,)))
         da_codes[1] = tile([P, C], U32, "da_codes1")[:]
         for half in range(2):
             slots = slice(half * P, (half + 1) * P)
@@ -362,8 +353,8 @@ def tile_moe_bdx_mlp_relu2_kernel(
                 scales_of[1][:, slots],
             )
             nc.vector.tensor_scalar_mul(dx[0][:, C + half * P : C + (half + 1) * P], acc[:], 2.0)
-        dx_out(1, (1,), second_product(1, 1, (1,)))
-        dx_out(1, (4, 5), second_product(3, 1, (4, 5)))
+        dx_out(1, (4, 5), second_product(4, 1, (4, 5)))
+        dx_out(1, (1,), second_product(2, 1, (1,)))
 
         sums = [tiles(TOP, [P, T], F32, "sums%d_" % kh) for kh in range(K // P)]
 
@@ -376,7 +367,11 @@ def tile_moe_bdx_mlp_relu2_kernel(
             if r == TOP - 1:
                 nc.sync.dma_start(out=out[kh * P : (kh + 1) * P, t0:t1], in_=sums[kh][r][:, t0:t1])
 
-        for kh, cut in enumerate((T // 2, T - 192)):
-            for r in range(TOP):
-                fetch(kh, r, 0, cut)
-                fetch(kh, r, cut, T)
+        for r in range(TOP - 1):
+            fetch(0, r, 0, T // 2)
+            fetch(0, r, T // 2, T)
+        for r in range(TOP - 1):
+            fetch(1, r, 0, T)
+            fetch(0, TOP - 1, r * T // 2, (r + 1) * T // 2)
+        fetch(1, TOP - 1, 0, T - 192)
+        fetch(1, TOP - 1, T - 192, T)

@@ -50,14 +50,16 @@ def tile_moe_bdx_mlp_relu2_kernel(
         NARROW = PACK * C * 2
         at_dh1 = 0
         at_a3 = at_dh1 + WIDE - LAP
-        at_mixed = at_a3 + WIDE - LAP
+        at_slope3 = at_a3 + WIDE
+        at_a0 = at_slope3 + WIDE - LAP
+        at_mixed = at_a0 + WIDE - LAP
         at_da4 = at_mixed + LAP - NARROW
         at_da1 = at_mixed + WIDE - LAP
         at_da23 = at_da1 + NARROW - LAP
         at_g32 = {0: at_da23, 3: at_da23, 1: at_da23 + 2 * WIDE, 5: at_da23 + 2 * WIDE}
         at_g12 = at_da23 + 4 * WIDE
-        at_raw45 = at_g12 + WIDE - LAP
-        at_dh0 = at_raw45 + NARROW - LAP
+        at_raw3 = at_g12 + WIDE - LAP
+        at_dh0 = at_raw3 + 3 * 2 * H - LAP
         at_raw0 = at_dh0 + WIDE
         at_g0 = at_raw0 + 2 * H - LAP
 
@@ -67,8 +69,8 @@ def tile_moe_bdx_mlp_relu2_kernel(
         gate_sb = tile([P, S], F32, "gate_sb")
         raw = {
             0: at(at_raw0, [P, 1, 2 * H], U8, "raw0"),
-            1: tile([P, 3, 2 * H], U8, "raw123"),
-            4: at(at_raw45, [P, 2, 2 * H], U8, "raw45"),
+            1: tile([P, 2, 2 * H], U8, "raw1"),
+            3: at(at_raw3, [P, 3, 2 * H], U8, "raw3"),
         }
         w2 = {}
         w1 = tile([P, E, 2 * K], U8, "w1")
@@ -76,7 +78,8 @@ def tile_moe_bdx_mlp_relu2_kernel(
         s2_rows = tile([P, 3 * H], U8, "s2_rows")
         s2 = tile([P, E, H], U8, "s2")
         s1 = tile([P, E, K], U8, "s1")
-        a_sb = {e: tile([P, PACK, C], F32, "a_sb%d" % e) for e in (0, 1, 2, 4, 5)}
+        a_sb = {e: tile([P, PACK, C], F32, "a_sb%d" % e) for e in (1, 2, 4, 5)}
+        a_sb[0] = at(at_a0, [P, PACK, C], F32, "a_sb0")
         a_sb[3] = at(at_a3, [P, PACK, C], F32, "a_sb3")
 
         nc.vector.memset(s2_raw[32:64, :].bitcast(I32), 0)
@@ -110,22 +113,21 @@ def tile_moe_bdx_mlp_relu2_kernel(
         for d in range(PACK):
             nc.sync.dma_start(out=dy[d][:, :T], in_=dy_planes[:, d, :])
         nc.vector.tensor_copy(
-            out=s2_rows[:].rearrange("p (b d c i) -> p c b d i", b=3, d=PACK, i=16),
-            in_=s2_raw[:].rearrange("p (b c i d) -> p c b d i", b=3, d=PACK, i=16),
+            out=s2_rows[:].rearrange("p (b d m) -> p d b m", b=3, d=PACK),
+            in_=s2_raw[:].rearrange("p (b m d) -> p d b m", b=3, d=PACK),
         )
         load_gate(1, 3)
         load_words(raw[0], w2_words, 0, 1)
-        load_words(raw[1], w2_words, 1, 4)
-        load_a(0)
+        load_words(raw[1], w2_words, 1, 3)
+        load_words(raw[3], w2_words, 3, E)
+        load_gate(3, E)
         for x in range(2):
             for q in range(4):
                 nc.sync.dma_start(
                     out=s2[32 * q : 32 * q + 4, x:E:2, :].bitcast(I32),
                     in_=s2_rows[16 * x + 4 * q : 16 * x + 4 * q + 4, :].rearrange("p (b n) -> p b n", b=3).bitcast(I32),
                 )
-        load_words(raw[4], w2_words, 4, E)
-        load_gate(3, E)
-        for e in (3, 2, 4, 1, 5):
+        for e in (0, 3, 2, 4, 1, 5):
             load_a(e)
         load_words(w1, w1_words, 0, E)
         for r in range(4):
@@ -173,8 +175,8 @@ def tile_moe_bdx_mlp_relu2_kernel(
             count = raw[first].shape[1]
             words = tile([P, count, 2 * H], U8, "w2_%d" % first)
             nc.scalar.copy(
-                out=words[:].bitcast(U16).rearrange("p e (d c i) -> p e c d i", d=PACK, i=4),
-                in_=raw[first][:].bitcast(U16).rearrange("p e (c i d) -> p e c d i", d=PACK, i=4),
+                out=words[:].bitcast(U16).rearrange("p e (d m) -> p e d m", d=PACK),
+                in_=raw[first][:].bitcast(U16).rearrange("p e (m d) -> p e d m", d=PACK),
             )
             for x in range(count):
                 w2[first + x] = words[:, x, :]
@@ -189,7 +191,7 @@ def tile_moe_bdx_mlp_relu2_kernel(
 
         def interleave(e, values):
             g16[e] = values
-            nc.scalar.copy(out=side_by_side(values, 2), in_=from_planes(g32[e][:], 2))
+            nc.scalar.copy(out=side_by_side(values, 4), in_=from_planes(g32[e][:], 4))
 
         def quantize_g(e, count):
             codes = tile([P, count * C], U32, "g_codes%d" % e)
@@ -217,7 +219,7 @@ def tile_moe_bdx_mlp_relu2_kernel(
                 slope[e] = tile([P, C, PACK], F32, "slope%d" % e)
             else:
                 slope[e] = at(offset, [P, C, PACK], F32, "slope%d" % e)
-            nc.scalar.activation(out=side_by_side(slope[e][:], 2), in_=from_planes(a_sb[e][:], 2), func=ACT.Relu)
+            nc.scalar.activation(out=side_by_side(slope[e][:], 4), in_=from_planes(a_sb[e][:], 4), func=ACT.Relu)
 
         def dh_out(e, offset):
             dh_rows[e] = at(offset, [P, C, PACK], F32, "dh_rows%d" % e)
@@ -238,8 +240,8 @@ def tile_moe_bdx_mlp_relu2_kernel(
             for half in range(2):
                 nc.vector.tensor_tensor(
                     da16[e][:, half * P : (half + 1) * P, :],
-                    dh_bank[e, half][:].rearrange("p d c -> p c d"),
                     slope[e][:, half * P : (half + 1) * P, :],
+                    dh_bank[e, half][:].rearrange("p d c -> p c d"),
                     ALU.mult,
                 )
 
@@ -281,25 +283,25 @@ def tile_moe_bdx_mlp_relu2_kernel(
         interleave(0, at(at_g0, [P, C, PACK], BF16, "g16_0")[:])
         gather(1, 2)
         regroup(1)
-        relu(0)
-        regroup(4)
+        regroup(3)
         quantize_g(0, 1)
         first_products(0, 0)
         interleave(1, at(at_g12, [P, 2 * C, PACK], BF16, "g16_1")[:])
         gather(3, 2)
         dh_out(0, at_dh0)
-        relu(3)
+        relu(0)
         quantize_g(1, 2)
         first_products(2, 1)
         first_products(4, 2)
         interleave(3, at(at_mixed, [P, 2 * C, PACK], BF16, "g16_3")[:])
         gather(5, 1)
-        dh_out(1, at_dh1)
+        relu(3, at_slope3)
         quantize_g(3, 2)
         first_products(6, 3)
         first_products(0, 4)
         mixed = at(at_mixed, [P, 2 * C, PACK], BF16, "mixed")
         interleave(5, mixed[:, :C, :])
+        dh_out(1, at_dh1)
         relu(1)
         relu(5)
 

@@ -50,36 +50,37 @@ def tile_moe_bdx_mlp_relu2_kernel(
         NARROW = PACK * C * 2
         at_dh1 = 0
         at_a3 = at_dh1 + WIDE - LAP
-        at_slope3 = at_a3 + WIDE
-        at_a0 = at_slope3 + WIDE - LAP
-        at_mixed = at_a0 + WIDE - LAP
-        at_da4 = at_mixed + LAP - NARROW
-        at_da1 = at_mixed + WIDE - LAP
-        at_da23 = at_da1 + NARROW - LAP
-        at_g32 = {0: at_da23, 3: at_da23, 1: at_da23 + 2 * WIDE, 5: at_da23 + 2 * WIDE}
-        at_g12 = at_da23 + 4 * WIDE
-        at_raw3 = at_g12 + WIDE - LAP
-        at_dh0 = at_raw3 + 3 * 2 * H - LAP
-        at_raw0 = at_dh0 + WIDE
-        at_g0 = at_raw0 + 2 * H - LAP
+        at_mixed = at_a3 + WIDE
+        at_dy3 = at_mixed + WIDE - LAP
+        at_dh0 = at_dy3 + WIDE
+        at_a1 = at_dh0 + WIDE - LAP
+        at_g23 = at_a1 + WIDE - LAP
+        at_g4 = at_g23 + LAP
+        at_da4 = at_g23 + WIDE
+        at_da3 = at_da4 + NARROW - LAP
+        at_da1 = at_da3 + NARROW - LAP
+        at_da2 = at_da1 + NARROW
+        at_g32 = {0: at_da3, 4: at_da2 - NARROW, 2: at_da3 + 2 * WIDE, 5: at_da3 + 2 * WIDE}
+        at_g01 = at_da3 + 4 * WIDE
+        at_raw4 = at_g01 + WIDE - LAP
+        at_slope3 = at_raw4 + NARROW
+        at_slope5 = at_slope3 + WIDE
 
         offs_sb = keep.tile([P, S // PER_COLUMN], U16, name="offs_sb")
         pos_sb = [keep.tile([P, T // PER_COLUMN], U16, name="pos_sb%d" % r) for r in range(TOP)]
-        dy = tiles(PACK, [P, T + SPARE], F32, "dy")
+        dy = tiles(PACK - 1, [P, T + SPARE], F32, "dy")
+        dy.append(at(at_dy3, [P, T + SPARE], F32, "dy3"))
         gate_sb = tile([P, S], F32, "gate_sb")
-        raw = {
-            0: at(at_raw0, [P, 1, 2 * H], U8, "raw0"),
-            1: tile([P, 2, 2 * H], U8, "raw1"),
-            3: at(at_raw3, [P, 3, 2 * H], U8, "raw3"),
-        }
+        raw = {e: tile([P, 2, 2 * H], U8, "raw%d" % e) for e in (0, 2)}
+        raw[4] = at(at_raw4, [P, 2, 2 * H], U8, "raw4")
         w2 = {}
         w1 = tile([P, E, 2 * K], U8, "w1")
         s2_raw = tile([P, 3 * H], U8, "s2_raw")
         s2_rows = tile([P, 3 * H], U8, "s2_rows")
         s2 = tile([P, E, H], U8, "s2")
         s1 = tile([P, E, K], U8, "s1")
-        a_sb = {e: tile([P, PACK, C], F32, "a_sb%d" % e) for e in (1, 2, 4, 5)}
-        a_sb[0] = at(at_a0, [P, PACK, C], F32, "a_sb0")
+        a_sb = {e: tile([P, PACK, C], F32, "a_sb%d" % e) for e in (0, 2, 4, 5)}
+        a_sb[1] = at(at_a1, [P, PACK, C], F32, "a_sb1")
         a_sb[3] = at(at_a3, [P, PACK, C], F32, "a_sb3")
 
         nc.vector.memset(s2_raw[32:64, :].bitcast(I32), 0)
@@ -96,7 +97,7 @@ def tile_moe_bdx_mlp_relu2_kernel(
             nc.sync.dma_start(out=gate_sb[:, e0 * C : e1 * C], in_=gate[0:P, e0 * C : e1 * C])
 
         def load_a(e):
-            nc.sync.dma_start(out=a_sb[e][:], in_=a_planes[:, :, e * C : (e + 1) * C])
+            nc.sync.dma_start(out=a_sb[e][:], in_=a_planes[:, :, e * C : e * C + a_sb[e].shape[2]])
 
         def load_words(dst, src, e0, e1):
             nc.sync.dma_start(
@@ -112,22 +113,29 @@ def tile_moe_bdx_mlp_relu2_kernel(
         load_gate(0, 1)
         for d in range(PACK):
             nc.sync.dma_start(out=dy[d][:, :T], in_=dy_planes[:, d, :])
+            if d == 0:
+                load_gate(1, 2)
+            else:
+                load_words(raw[2 * d - 2], w2_words, 2 * d - 2, 2 * d)
         nc.vector.tensor_copy(
             out=s2_rows[:].rearrange("p (b d m) -> p d b m", b=3, d=PACK),
             in_=s2_raw[:].rearrange("p (b m d) -> p d b m", b=3, d=PACK),
         )
-        load_gate(1, 3)
-        load_words(raw[0], w2_words, 0, 1)
-        load_words(raw[1], w2_words, 1, 3)
-        load_words(raw[3], w2_words, 3, E)
-        load_gate(3, E)
-        for x in range(2):
+        load_gate(2, 4)
+        def spread_scales(x):
             for q in range(4):
                 nc.sync.dma_start(
                     out=s2[32 * q : 32 * q + 4, x:E:2, :].bitcast(I32),
                     in_=s2_rows[16 * x + 4 * q : 16 * x + 4 * q + 4, :].rearrange("p (b n) -> p b n", b=3).bitcast(I32),
                 )
-        for e in (0, 3, 2, 4, 1, 5):
+
+        load_a(0)
+        spread_scales(0)
+        load_a(1)
+        load_gate(4, E)
+        load_a(3)
+        spread_scales(1)
+        for e in (2, 4, 5):
             load_a(e)
         load_words(w1, w1_words, 0, E)
         for r in range(4):
@@ -183,11 +191,16 @@ def tile_moe_bdx_mlp_relu2_kernel(
 
         def gather(e, count):
             g32[e] = at(at_g32[e], [P, PACK, count * C], F32, "g32_%d" % e)
-            entries = offs_sb[:, e * C // PER_COLUMN : (e + count) * C // PER_COLUMN]
             for d in range(PACK):
-                nc.vector.tensor_tensor(
-                    g32[e][:, d, :], dy[d][:].indirect(entries), gate_sb[:, e * C : (e + count) * C], ALU.mult
-                )
+                step = 1 if (e, d) == (0, 0) else count
+                for x in range(0, count, step):
+                    j0, j1 = (e + x) * C, (e + x + step) * C
+                    nc.vector.tensor_tensor(
+                        g32[e][:, d, x * C : (x + step) * C],
+                        dy[d][:].indirect(offs_sb[:, j0 // PER_COLUMN : j1 // PER_COLUMN]),
+                        gate_sb[:, j0:j1],
+                        ALU.mult,
+                    )
 
         def interleave(e, values):
             g16[e] = values
@@ -215,24 +228,35 @@ def tile_moe_bdx_mlp_relu2_kernel(
                 dh_bank[e, half] = acc
 
         def relu(e, offset=None):
+            slots = a_sb[e].shape[2]
             if offset is None:
-                slope[e] = tile([P, C, PACK], F32, "slope%d" % e)
+                values = tile([P, slots, PACK], F32, "slope%d" % e)
             else:
-                slope[e] = at(offset, [P, C, PACK], F32, "slope%d" % e)
-            nc.scalar.activation(out=side_by_side(slope[e][:], 4), in_=from_planes(a_sb[e][:], 4), func=ACT.Relu)
+                values = at(offset, [P, slots, PACK], F32, "slope%d" % e)
+            nc.scalar.activation(out=side_by_side(values[:], 4), in_=from_planes(a_sb[e][:], 4), func=ACT.Relu)
+            for x in range(slots // C):
+                slope[e + x] = values[:, x * C : (x + 1) * C, :]
 
-        def dh_out(e, offset):
-            dh_rows[e] = at(offset, [P, C, PACK], F32, "dh_rows%d" % e)
+        def relu_by_halves(e, offset):
             for half in range(2):
-                nc.scalar.copy(
-                    out=dh_rows[e][:, half * P : (half + 1) * P, :], in_=dh_bank[e, half][:].rearrange("p d c -> p c d")
+                values = at(offset + half * NARROW, [P, P, PACK], F32, "slope%d%d" % (e, half))
+                nc.scalar.activation(
+                    out=side_by_side(values[:], 4),
+                    in_=from_planes(a_sb[e][:, :, half * P : (half + 1) * P], 4),
+                    func=ACT.Relu,
                 )
+                slope[e, half] = values[:]
+
+        def dh_out(e, half):
+            nc.scalar.copy(
+                out=dh_rows[e][:, half * P : (half + 1) * P, :], in_=dh_bank[e, half][:].rearrange("p d c -> p c d")
+            )
 
         def da_on_gpsimd(e):
             nc.gpsimd.tensor_tensor(
                 da16[e].rearrange("p c d -> p (c d)"),
                 dh_rows[e][:].rearrange("p c d -> p (c d)"),
-                slope[e][:].rearrange("p c d -> p (c d)"),
+                slope[e].rearrange("p c d -> p (c d)"),
                 ALU.mult,
             )
 
@@ -240,7 +264,7 @@ def tile_moe_bdx_mlp_relu2_kernel(
             for half in range(2):
                 nc.vector.tensor_tensor(
                     da16[e][:, half * P : (half + 1) * P, :],
-                    slope[e][:, half * P : (half + 1) * P, :],
+                    slope[e, half] if (e, half) in slope else slope[e][:, half * P : (half + 1) * P, :],
                     dh_bank[e, half][:].rearrange("p d c -> p c d"),
                     ALU.mult,
                 )
@@ -278,41 +302,47 @@ def tile_moe_bdx_mlp_relu2_kernel(
             else:
                 nc.scalar.activation(out=dst, in_=acc[:], func=ACT.Copy, scale=2.0)
 
-        regroup(0)
-        gather(0, 1)
-        interleave(0, at(at_g0, [P, C, PACK], BF16, "g16_0")[:])
-        gather(1, 2)
-        regroup(1)
-        regroup(3)
-        quantize_g(0, 1)
-        first_products(0, 0)
-        interleave(1, at(at_g12, [P, 2 * C, PACK], BF16, "g16_1")[:])
-        gather(3, 2)
-        dh_out(0, at_dh0)
+        for e in (0, 2, 4):
+            regroup(e)
+        gather(0, 2)
+        interleave(0, at(at_g01, [P, 2 * C, PACK], BF16, "g16_0")[:])
+        gather(2, 2)
         relu(0)
-        quantize_g(1, 2)
+        relu(1)
+        quantize_g(0, 2)
+        first_products(0, 0)
         first_products(2, 1)
+        interleave(2, at(at_g23, [P, 2 * C, PACK], BF16, "g16_2")[:])
+        gather(4, 1)
+        dh_rows[0] = at(at_dh0, [P, C, PACK], F32, "dh_rows0")
+        dh_out(0, 0)
+        dh_out(0, 1)
+        quantize_g(2, 2)
         first_products(4, 2)
-        interleave(3, at(at_mixed, [P, 2 * C, PACK], BF16, "g16_3")[:])
-        gather(5, 1)
-        relu(3, at_slope3)
-        quantize_g(3, 2)
         first_products(6, 3)
+        interleave(4, at(at_g4, [P, C, PACK], BF16, "g16_4")[:])
+        gather(5, 1)
+        relu_by_halves(3, at_slope3)
+        dh_rows[1] = at(at_dh1, [P, C, PACK], F32, "dh_rows1")
+        dh_out(1, 0)
+        quantize_g(4, 1)
         first_products(0, 4)
         mixed = at(at_mixed, [P, 2 * C, PACK], BF16, "mixed")
         interleave(5, mixed[:, :C, :])
-        dh_out(1, at_dh1)
-        relu(1)
-        relu(5)
+        dh_out(1, 1)
+        relu_by_halves(5, at_slope5)
 
         da16[0] = mixed[:, C:, :]
         da_on_gpsimd(0)
-        da23 = at(at_da23, [P, 2 * C, PACK], BF16, "da23")
-        da16[2] = da23[:, :C, :]
-        da16[3] = da23[:, C:, :]
+        da16[2] = at(at_da2, [P, C, PACK], BF16, "da16_2")[:]
+        da16[3] = at(at_da3, [P, C, PACK], BF16, "da16_3")[:]
         da_with_relu(2)
         da_on_vector(3)
-        mixed_codes = tile([P, 2 * C], U32, "mixed_codes")
+        da_codes[2] = at(at_slope3, [P, C], U32, "da_codes2")[:]
+        da_codes[3] = tile([P, C], U32, "da_codes3")[:]
+        quantize_da(2)
+        quantize_da(3)
+        mixed_codes = at(at_slope3 + NARROW, [P, 2 * C], U32, "mixed_codes")
         mixed_scales = tile([P, 2 * C], U8, "mixed_scales")
         quantize(mixed_codes[:], mixed_scales[:], mixed[:])
         g_codes[5] = mixed_codes[:, :C]
@@ -320,43 +350,37 @@ def tile_moe_bdx_mlp_relu2_kernel(
         da_codes[0] = mixed_codes[:, C:]
         scales_of[0] = mixed_scales[:, C:]
         first_products(2, 5)
-        codes23 = at(at_dh0 + NARROW, [P, 2 * C], U32, "codes23")
-        da_codes[2] = codes23[:, :C]
-        da_codes[3] = codes23[:, C:]
-        quantize(codes23[:], da_scales[:, 2 * C : 4 * C], da23[:])
         da16[1] = at(at_da1, [P, C, PACK], BF16, "da16_1")[:]
         da_on_gpsimd(1)
         da16[4] = at(at_da4, [P, C, PACK], BF16, "da16_4")[:]
         da_with_relu(4)
         da16[5] = tile([P, C, PACK], BF16, "da16_5")[:]
         da_on_vector(5)
-        dx_out(0, (0,), second_product(4, 0, (0,)))
         dx_out(0, (2, 3), second_product(5, 0, (2, 3)))
+        dx_out(0, (0,), second_product(4, 0, (0,)))
         dx_out(1, (0,), second_product(0, 1, (0,)))
         dx_out(1, (2, 3), second_product(1, 1, (2, 3)))
-        da_codes[5] = at(at_dh1, [P, C], U32, "da_codes5")[:]
-        quantize_da(5)
-        dx_out(0, (5,), second_product(6, 0, (5,)))
-        da_codes[4] = at(at_dh1 + 4 * C, [P, C], U32, "da_codes4")[:]
-        quantize_da(4)
-        dx_out(0, (4,), second_product(7, 0, (4,)))
-        da_codes[1] = tile([P, C], U32, "da_codes1")[:]
+        for x, e in enumerate((4, 1, 5)):
+            da_codes[e] = at(at_slope5 + x * 4 * C, [P, C], U32, "da_codes%d" % e)[:]
+        for x, e in enumerate((4, 1)):
+            quantize_da(e)
+            dx_out(0, (e,), second_product(6 + x, 0, (e,)))
         for half in range(2):
             slots = slice(half * P, (half + 1) * P)
-            quantize(da_codes[1][:, slots], scales_of[1][:, slots], da16[1][:, slots, :])
+            quantize(da_codes[5][:, slots], scales_of[5][:, slots], da16[5][:, slots, :])
         for half in range(2):
             slots = slice(half * P, (half + 1) * P)
             acc = bank(2 + half, [P, P], "dx_last%d" % half)
             one_pass(
                 acc[:],
-                w1[:, 1, 0 : 2 * P].bitcast(FP4X4),
-                s1[:, 1, 0:P],
-                da_codes[1][:, slots].bitcast(FP8X4),
-                scales_of[1][:, slots],
+                w1[:, 5, 0 : 2 * P].bitcast(FP4X4),
+                s1[:, 5, 0:P],
+                da_codes[5][:, slots].bitcast(FP8X4),
+                scales_of[5][:, slots],
             )
-            nc.vector.tensor_scalar_mul(dx[0][:, C + half * P : C + (half + 1) * P], acc[:], 2.0)
-        dx_out(1, (4, 5), second_product(4, 1, (4, 5)))
-        dx_out(1, (1,), second_product(2, 1, (1,)))
+            nc.vector.tensor_scalar_mul(dx[0][:, 5 * C + half * P : 5 * C + (half + 1) * P], acc[:], 2.0)
+        dx_out(1, (1,), second_product(4, 1, (1,)))
+        dx_out(1, (4, 5), second_product(2, 1, (4, 5)))
 
         sums = [tiles(TOP, [P, T], F32, "sums%d_" % kh) for kh in range(K // P)]
 

@@ -330,6 +330,7 @@ def tile_moe_bdx_mlp_relu2_kernel(
         mixed = at(at_mixed, [P, 2 * C, PACK], BF16, "mixed")
         interleave(5, mixed[:, :C, :])
         dh_out(1, 1)
+        relu(4)
         relu_by_halves(5, at_slope5)
 
         da16[0] = mixed[:, C:, :]
@@ -353,13 +354,12 @@ def tile_moe_bdx_mlp_relu2_kernel(
         da16[1] = at(at_da1, [P, C, PACK], BF16, "da16_1")[:]
         da_on_gpsimd(1)
         da16[4] = at(at_da4, [P, C, PACK], BF16, "da16_4")[:]
-        da_with_relu(4)
+        da_on_vector(4)
         da16[5] = tile([P, C, PACK], BF16, "da16_5")[:]
         da_on_vector(5)
         dx_out(0, (2, 3), second_product(5, 0, (2, 3)))
         dx_out(0, (0,), second_product(4, 0, (0,)))
-        dx_out(1, (0,), second_product(0, 1, (0,)))
-        dx_out(1, (2, 3), second_product(1, 1, (2, 3)))
+        late = [((0,), second_product(0, 1, (0,))), ((2, 3), second_product(1, 1, (2, 3)))]
         for x, e in enumerate((4, 1, 5)):
             da_codes[e] = at(at_slope5 + x * 4 * C, [P, C], U32, "da_codes%d" % e)[:]
         for x, e in enumerate((4, 1)):
@@ -379,8 +379,10 @@ def tile_moe_bdx_mlp_relu2_kernel(
                 scales_of[5][:, slots],
             )
             nc.vector.tensor_scalar_mul(dx[0][:, 5 * C + half * P : 5 * C + (half + 1) * P], acc[:], 2.0)
-        dx_out(1, (1,), second_product(4, 1, (1,)))
-        dx_out(1, (4, 5), second_product(2, 1, (4, 5)))
+        late.append(((1,), second_product(4, 1, (1,))))
+        late.append(((4, 5), second_product(2, 1, (4, 5))))
+        for experts, acc in late:
+            dx_out(1, experts, acc)
 
         sums = [tiles(TOP, [P, T], F32, "sums%d_" % kh) for kh in range(K // P)]
 
@@ -393,11 +395,7 @@ def tile_moe_bdx_mlp_relu2_kernel(
             if r == TOP - 1:
                 nc.sync.dma_start(out=out[kh * P : (kh + 1) * P, t0:t1], in_=sums[kh][r][:, t0:t1])
 
-        for r in range(TOP - 1):
-            fetch(0, r, 0, T // 2)
-            fetch(0, r, T // 2, T)
-        for r in range(TOP - 1):
-            fetch(1, r, 0, T)
-            fetch(0, TOP - 1, r * T // 2, (r + 1) * T // 2)
-        fetch(1, TOP - 1, 0, T - 192)
-        fetch(1, TOP - 1, T - 192, T)
+        for kh, cut in enumerate((T // 2, T - 192)):
+            for r in range(TOP):
+                fetch(kh, r, 0, cut)
+                fetch(kh, r, cut, T)

@@ -8,10 +8,16 @@ P = 128
 PACK = 4
 TOP = 3
 PER_COLUMN = 16
+BLOCKS = N // 32
 FLOPS = 2 * S * H * (N + K)
 BYTES = 4 * (N * T + H * S + S + K * T) + E * H * (N + K) // 2 + E * H * (N + K) // 32 + 2 * (S + TOP * T)
+
+WIDE = PACK * C * 4
+NARROW = PACK * C * 2
 LAP = 64
 SPARE = 32
+RUN = 4
+LAST_PIECE = 192
 
 F32 = mybir.dt.float32
 BF16 = mybir.dt.bfloat16
@@ -46,23 +52,19 @@ def tile_moe_bdx_mlp_relu2_kernel(
         def at(offset, shape, dtype, name):
             return placed.tile(shape, dtype, name=name, offset=offset, align_bytes=64)
 
-        WIDE = PACK * C * 4
-        NARROW = PACK * C * 2
-        at_dh1 = 0
-        at_a3 = at_dh1 + WIDE - LAP
-        at_mixed = at_a3 + WIDE
-        at_dy3 = at_mixed + WIDE - LAP
+        at_joint = 0
+        at_dy3 = at_joint + WIDE - LAP
         at_dh0 = at_dy3 + WIDE
         at_a1 = at_dh0 + WIDE - LAP
-        at_g23 = at_a1 + WIDE - LAP
-        at_g4 = at_g23 + LAP
-        at_da4 = at_g23 + WIDE
+        at_g16_2 = at_a1 + WIDE - LAP
+        at_g16_4 = at_g16_2 + LAP
+        at_da4 = at_g16_2 + WIDE
         at_da3 = at_da4 + NARROW - LAP
         at_da1 = at_da3 + NARROW - LAP
         at_da2 = at_da1 + NARROW
         at_g32 = {0: at_da3, 4: at_da2 - NARROW, 2: at_da3 + 2 * WIDE, 5: at_da3 + 2 * WIDE}
-        at_g01 = at_da3 + 4 * WIDE
-        at_raw4 = at_g01 + WIDE - LAP
+        at_g16_0 = at_da3 + 4 * WIDE
+        at_raw4 = at_g16_0 + WIDE - LAP
         at_slope3 = at_raw4 + NARROW
         at_slope5 = at_slope3 + WIDE
 
@@ -73,17 +75,15 @@ def tile_moe_bdx_mlp_relu2_kernel(
         gate_sb = tile([P, S], F32, "gate_sb")
         raw = {e: tile([P, 2, 2 * H], U8, "raw%d" % e) for e in (0, 2)}
         raw[4] = at(at_raw4, [P, 2, 2 * H], U8, "raw4")
-        w2 = {}
         w1 = tile([P, E, 2 * K], U8, "w1")
-        s2_raw = tile([P, 3 * H], U8, "s2_raw")
-        s2_rows = tile([P, 3 * H], U8, "s2_rows")
+        s2_raw = tile([P, E // 2 * H], U8, "s2_raw")
+        s2_rows = tile([P, E // 2 * H], U8, "s2_rows")
         s2 = tile([P, E, H], U8, "s2")
         s1 = tile([P, E, K], U8, "s1")
-        a_sb = {e: tile([P, PACK, C], F32, "a_sb%d" % e) for e in (0, 2, 4, 5)}
+        a_sb = {e: tile([P, PACK, C], F32, "a_sb%d" % e) for e in range(E) if e != 1}
         a_sb[1] = at(at_a1, [P, PACK, C], F32, "a_sb1")
-        a_sb[3] = at(at_a3, [P, PACK, C], F32, "a_sb3")
 
-        nc.vector.memset(s2_raw[32:64, :].bitcast(I32), 0)
+        nc.vector.memset(s2_raw[2 * BLOCKS : 64, :].bitcast(I32), 0)
         nc.vector.memset(s2_raw[64:P, :].bitcast(I32), 0)
         for d in range(PACK):
             nc.gpsimd.memset(dy[d][:, T:], 0.0)
@@ -97,7 +97,7 @@ def tile_moe_bdx_mlp_relu2_kernel(
             nc.sync.dma_start(out=gate_sb[:, e0 * C : e1 * C], in_=gate[0:P, e0 * C : e1 * C])
 
         def load_a(e):
-            nc.sync.dma_start(out=a_sb[e][:], in_=a_planes[:, :, e * C : e * C + a_sb[e].shape[2]])
+            nc.sync.dma_start(out=a_sb[e][:], in_=a_planes[:, :, e * C : (e + 1) * C])
 
         def load_words(dst, src, e0, e1):
             nc.sync.dma_start(
@@ -105,8 +105,16 @@ def tile_moe_bdx_mlp_relu2_kernel(
                 in_=src[e0:e1, 0].rearrange("e p n -> p e n").bitcast(I32),
             )
 
+        def spread_scales(x):
+            for q in range(BLOCKS // 4):
+                rows = s2_rows[BLOCKS * x + 4 * q : BLOCKS * x + 4 * q + 4, :]
+                nc.sync.dma_start(
+                    out=s2[32 * q : 32 * q + 4, x:E:2, :].bitcast(I32),
+                    in_=rows.rearrange("p (b n) -> p b n", n=H).bitcast(I32),
+                )
+
         nc.sync.dma_start(
-            out=s2_raw[0:32, :].rearrange("p (b n) -> p b n", b=3).bitcast(I32),
+            out=s2_raw[0 : 2 * BLOCKS, :].rearrange("p (b n) -> p b n", n=H).bitcast(I32),
             in_=w2_scales.rearrange("(b x) s f n -> (x s f) b n", x=2).bitcast(I32),
         )
         nc.sync.dma_start(offs_sb[:], offs)
@@ -118,24 +126,15 @@ def tile_moe_bdx_mlp_relu2_kernel(
             else:
                 load_words(raw[2 * d - 2], w2_words, 2 * d - 2, 2 * d)
         nc.vector.tensor_copy(
-            out=s2_rows[:].rearrange("p (b d m) -> p d b m", b=3, d=PACK),
-            in_=s2_raw[:].rearrange("p (b m d) -> p d b m", b=3, d=PACK),
+            out=s2_rows[:].rearrange("p (b d m) -> p d b m", d=PACK, m=P),
+            in_=s2_raw[:].rearrange("p (b m d) -> p d b m", d=PACK, m=P),
         )
         load_gate(2, 4)
-        def spread_scales(x):
-            for q in range(4):
-                nc.sync.dma_start(
-                    out=s2[32 * q : 32 * q + 4, x:E:2, :].bitcast(I32),
-                    in_=s2_rows[16 * x + 4 * q : 16 * x + 4 * q + 4, :].rearrange("p (b n) -> p b n", b=3).bitcast(I32),
-                )
-
-        load_a(0)
-        spread_scales(0)
-        load_a(1)
+        for e in range(2):
+            load_a(e)
+            spread_scales(e)
         load_gate(4, E)
-        load_a(3)
-        spread_scales(1)
-        for e in (2, 4, 5):
+        for e in (3, 2, 4, 5):
             load_a(e)
         load_words(w1, w1_words, 0, E)
         for r in range(4):
@@ -146,73 +145,83 @@ def tile_moe_bdx_mlp_relu2_kernel(
         for r, pos in enumerate((pos1, pos2, pos3)):
             nc.sync.dma_start(pos_sb[r][:], pos)
 
+        w2 = {}
         g32 = {}
         g16 = {}
         g_codes = {}
         g_scales = {}
         slope = {}
+        half_slope = {}
         dh_rows = {}
         dh_bank = {}
         da16 = {}
         da_codes = {}
-        da_scales = tile([P, S], U8, "da_scales")
-        scales_of = {e: da_scales[:, e * C : (e + 1) * C] for e in range(1, E)}
-        dx = tiles(2, [P, S], F32, "dx")
+        scale_bytes = tile([P, S], U8, "scale_bytes")
+        da_scales = {e: scale_bytes[:, e * C : (e + 1) * C] for e in range(1, E)}
+        dx = tiles(K // P, [P, S], F32, "dx")
 
-        def from_planes(ap, run):
-            return ap.rearrange("p d (c i) -> p c d i", i=run)
+        def half_of(half):
+            return slice(half * P, (half + 1) * P)
 
-        def side_by_side(ap, run):
-            return ap.rearrange("p (c i) d -> p c d i", i=run)
+        def from_planes(ap):
+            return ap.rearrange("p d (c i) -> p c d i", i=RUN)
+
+        def side_by_side(ap):
+            return ap.rearrange("p (c i) d -> p c d i", i=RUN)
+
+        def by_columns(ap):
+            return ap.rearrange("p d c -> p c d")
+
+        def flat(ap):
+            return ap.rearrange("p c d -> p (c d)")
 
         def quantize(codes, scales, values):
-            nc.vector.quantize_mx(out=codes.bitcast(FP8X4), scales=scales, in_=values.rearrange("p c d -> p (c d)"))
+            nc.vector.quantize_mx(out=codes.bitcast(FP8X4), scales=scales, in_=flat(values))
 
         def one_pass(acc, stationary, stationary_scales, moving, moving_scales):
             nc.tensor.matmul_mx(
                 out=acc,
-                lhsT=stationary,
+                lhsT=stationary.bitcast(FP4X4),
                 lhsT_scale=stationary_scales,
-                rhs=moving,
+                rhs=moving.bitcast(FP8X4),
                 rhs_scale=moving_scales,
                 start=True,
                 stop=True,
             )
 
         def regroup(first):
-            count = raw[first].shape[1]
-            words = tile([P, count, 2 * H], U8, "w2_%d" % first)
+            words = tile([P, 2, 2 * H], U8, "w2_%d" % first)
             nc.scalar.copy(
                 out=words[:].bitcast(U16).rearrange("p e (d m) -> p e d m", d=PACK),
                 in_=raw[first][:].bitcast(U16).rearrange("p e (m d) -> p e d m", d=PACK),
             )
-            for x in range(count):
+            for x in range(2):
                 w2[first + x] = words[:, x, :]
 
-        def gather(e, count):
-            g32[e] = at(at_g32[e], [P, PACK, count * C], F32, "g32_%d" % e)
+        def gather(first, count):
+            g32[first] = at(at_g32[first], [P, PACK, count * C], F32, "g32_%d" % first)
             for d in range(PACK):
-                step = 1 if (e, d) == (0, 0) else count
+                step = 1 if (first, d) == (0, 0) else count
                 for x in range(0, count, step):
-                    j0, j1 = (e + x) * C, (e + x + step) * C
+                    j0, j1 = (first + x) * C, (first + x + step) * C
                     nc.vector.tensor_tensor(
-                        g32[e][:, d, x * C : (x + step) * C],
+                        g32[first][:, d, x * C : (x + step) * C],
                         dy[d][:].indirect(offs_sb[:, j0 // PER_COLUMN : j1 // PER_COLUMN]),
                         gate_sb[:, j0:j1],
                         ALU.mult,
                     )
 
-        def interleave(e, values):
-            g16[e] = values
-            nc.scalar.copy(out=side_by_side(values, 4), in_=from_planes(g32[e][:], 4))
+        def interleave(first, values):
+            g16[first] = values
+            nc.scalar.copy(out=side_by_side(values), in_=from_planes(g32[first][:]))
 
-        def quantize_g(e, count):
-            codes = tile([P, count * C], U32, "g_codes%d" % e)
-            scales = tile([P, count * C], U8, "g_scales%d" % e)
-            quantize(codes[:], scales[:], g16[e])
+        def quantize_g(first, count):
+            codes = tile([P, count * C], U32, "g_codes%d" % first)
+            scales = tile([P, count * C], U8, "g_scales%d" % first)
+            quantize(codes[:], scales[:], g16[first])
             for x in range(count):
-                g_codes[e + x] = codes[:, x * C : (x + 1) * C]
-                g_scales[e + x] = scales[:, x * C : (x + 1) * C]
+                g_codes[first + x] = codes[:, x * C : (x + 1) * C]
+                g_scales[first + x] = scales[:, x * C : (x + 1) * C]
 
         def first_products(number, e):
             for half in range(2):
@@ -220,137 +229,125 @@ def tile_moe_bdx_mlp_relu2_kernel(
                 for d in range(PACK):
                     one_pass(
                         acc[:, d, :],
-                        w2[e][:, 2 * d * P : 2 * (d + 1) * P].bitcast(FP4X4),
+                        w2[e][:, 2 * d * P : 2 * (d + 1) * P],
                         s2[:, e, d * P : (d + 1) * P],
-                        g_codes[e][:, half * P : (half + 1) * P].bitcast(FP8X4),
-                        g_scales[e][:, half * P : (half + 1) * P],
+                        g_codes[e][:, half_of(half)],
+                        g_scales[e][:, half_of(half)],
                     )
                 dh_bank[e, half] = acc
 
-        def relu(e, offset=None):
-            slots = a_sb[e].shape[2]
-            if offset is None:
-                values = tile([P, slots, PACK], F32, "slope%d" % e)
-            else:
-                values = at(offset, [P, slots, PACK], F32, "slope%d" % e)
-            nc.scalar.activation(out=side_by_side(values[:], 4), in_=from_planes(a_sb[e][:], 4), func=ACT.Relu)
-            for x in range(slots // C):
-                slope[e + x] = values[:, x * C : (x + 1) * C, :]
+        def relu(values, planes):
+            nc.scalar.activation(out=side_by_side(values), in_=from_planes(planes), func=ACT.Relu)
 
-        def relu_by_halves(e, offset):
+        def make_slope(e):
+            slope[e] = tile([P, C, PACK], F32, "slope%d" % e)[:]
+            relu(slope[e], a_sb[e][:])
             for half in range(2):
-                values = at(offset + half * NARROW, [P, P, PACK], F32, "slope%d%d" % (e, half))
-                nc.scalar.activation(
-                    out=side_by_side(values[:], 4),
-                    in_=from_planes(a_sb[e][:, :, half * P : (half + 1) * P], 4),
-                    func=ACT.Relu,
-                )
-                slope[e, half] = values[:]
+                half_slope[e, half] = slope[e][:, half_of(half), :]
+
+        def make_slope_by_halves(e, offset):
+            for half in range(2):
+                half_slope[e, half] = at(offset + half * NARROW, [P, P, PACK], F32, "slope%d%d" % (e, half))[:]
+                relu(half_slope[e, half], a_sb[e][:, :, half_of(half)])
 
         def dh_out(e, half):
-            nc.scalar.copy(
-                out=dh_rows[e][:, half * P : (half + 1) * P, :], in_=dh_bank[e, half][:].rearrange("p d c -> p c d")
-            )
+            nc.scalar.copy(out=dh_rows[e][:, half_of(half), :], in_=by_columns(dh_bank[e, half][:]))
 
         def da_on_gpsimd(e):
-            nc.gpsimd.tensor_tensor(
-                da16[e].rearrange("p c d -> p (c d)"),
-                dh_rows[e][:].rearrange("p c d -> p (c d)"),
-                slope[e].rearrange("p c d -> p (c d)"),
-                ALU.mult,
-            )
+            nc.gpsimd.tensor_tensor(flat(da16[e]), flat(dh_rows[e][:]), flat(slope[e]), ALU.mult)
 
         def da_on_vector(e):
             for half in range(2):
                 nc.vector.tensor_tensor(
-                    da16[e][:, half * P : (half + 1) * P, :],
-                    slope[e, half] if (e, half) in slope else slope[e][:, half * P : (half + 1) * P, :],
-                    dh_bank[e, half][:].rearrange("p d c -> p c d"),
-                    ALU.mult,
+                    da16[e][:, half_of(half), :], half_slope[e, half], by_columns(dh_bank[e, half][:]), ALU.mult
                 )
 
         def da_with_relu(e):
             for half in range(2):
                 nc.vector.scalar_tensor_tensor(
-                    da16[e][:, half * P : (half + 1) * P, :],
-                    a_sb[e][:, :, half * P : (half + 1) * P].rearrange("p d c -> p c d"),
+                    da16[e][:, half_of(half), :],
+                    by_columns(a_sb[e][:, :, half_of(half)]),
                     0.0,
-                    dh_bank[e, half][:].rearrange("p d c -> p c d"),
+                    by_columns(dh_bank[e, half][:]),
                     ALU.max,
                     ALU.mult,
                 )
 
-        def quantize_da(e):
-            quantize(da_codes[e], scales_of[e], da16[e])
+        def quantize_da(e, slots=slice(0, C)):
+            quantize(da_codes[e][:, slots], da_scales[e][:, slots], da16[e][:, slots, :])
+
+        def second_pass(acc, kh, e, slots):
+            one_pass(
+                acc,
+                w1[:, e, 2 * kh * P : 2 * (kh + 1) * P],
+                s1[:, e, kh * P : (kh + 1) * P],
+                da_codes[e][:, slots],
+                da_scales[e][:, slots],
+            )
 
         def second_product(number, kh, experts):
             acc = bank(number, [P, len(experts), C], "dx%d_%d" % (kh, experts[0]))
             for x, e in enumerate(experts):
-                one_pass(
-                    acc[:, x, :],
-                    w1[:, e, 2 * kh * P : 2 * (kh + 1) * P].bitcast(FP4X4),
-                    s1[:, e, kh * P : (kh + 1) * P],
-                    da_codes[e].bitcast(FP8X4),
-                    scales_of[e],
-                )
+                second_pass(acc[:, x, :], kh, e, slice(0, C))
             return acc
 
-        def dx_out(kh, experts, acc, on_vector=False):
-            dst = dx[kh][:, experts[0] * C : (experts[-1] + 1) * C].rearrange("p (e c) -> p e c", c=C)
-            if on_vector:
-                nc.vector.tensor_scalar_mul(dst, acc[:], 2.0)
-            else:
-                nc.scalar.activation(out=dst, in_=acc[:], func=ACT.Copy, scale=2.0)
+        def dx_slots(kh, experts):
+            return dx[kh][:, experts[0] * C : (experts[-1] + 1) * C].rearrange("p (e c) -> p e c", c=C)
 
-        for e in (0, 2, 4):
-            regroup(e)
+        def dx_out(kh, experts, acc):
+            nc.scalar.activation(out=dx_slots(kh, experts), in_=acc[:], func=ACT.Copy, scale=2.0)
+
+        for first in (0, 2, 4):
+            regroup(first)
         gather(0, 2)
-        interleave(0, at(at_g01, [P, 2 * C, PACK], BF16, "g16_0")[:])
+        interleave(0, at(at_g16_0, [P, 2 * C, PACK], BF16, "g16_0")[:])
         gather(2, 2)
-        relu(0)
-        relu(1)
+        make_slope(0)
+        make_slope(1)
         quantize_g(0, 2)
         first_products(0, 0)
         first_products(2, 1)
-        interleave(2, at(at_g23, [P, 2 * C, PACK], BF16, "g16_2")[:])
+        interleave(2, at(at_g16_2, [P, 2 * C, PACK], BF16, "g16_2")[:])
         gather(4, 1)
         dh_rows[0] = at(at_dh0, [P, C, PACK], F32, "dh_rows0")
         dh_out(0, 0)
         dh_out(0, 1)
+        dh_rows[1] = tile([P, C, PACK], F32, "dh_rows1")
+        dh_out(1, 0)
         quantize_g(2, 2)
         first_products(4, 2)
         first_products(6, 3)
-        interleave(4, at(at_g4, [P, C, PACK], BF16, "g16_4")[:])
+        interleave(4, at(at_g16_4, [P, C, PACK], BF16, "g16_4")[:])
         gather(5, 1)
-        relu_by_halves(3, at_slope3)
-        dh_rows[1] = at(at_dh1, [P, C, PACK], F32, "dh_rows1")
-        dh_out(1, 0)
+        make_slope_by_halves(3, at_slope3)
         quantize_g(4, 1)
         first_products(0, 4)
-        mixed = at(at_mixed, [P, 2 * C, PACK], BF16, "mixed")
-        interleave(5, mixed[:, :C, :])
+        joint = at(at_joint, [P, 2 * C, PACK], BF16, "joint")
+        interleave(5, joint[:, :C, :])
         dh_out(1, 1)
-        relu(4)
-        relu_by_halves(5, at_slope5)
+        make_slope(4)
+        make_slope_by_halves(5, at_slope5)
 
-        da16[0] = mixed[:, C:, :]
+        da16[0] = joint[:, C:, :]
         da_on_gpsimd(0)
         da16[2] = at(at_da2, [P, C, PACK], BF16, "da16_2")[:]
         da16[3] = at(at_da3, [P, C, PACK], BF16, "da16_3")[:]
         da_with_relu(2)
         da_on_vector(3)
+
         da_codes[2] = at(at_slope3, [P, C], U32, "da_codes2")[:]
         da_codes[3] = tile([P, C], U32, "da_codes3")[:]
         quantize_da(2)
         quantize_da(3)
-        mixed_codes = at(at_slope3 + NARROW, [P, 2 * C], U32, "mixed_codes")
-        mixed_scales = tile([P, 2 * C], U8, "mixed_scales")
-        quantize(mixed_codes[:], mixed_scales[:], mixed[:])
-        g_codes[5] = mixed_codes[:, :C]
-        g_scales[5] = mixed_scales[:, :C]
-        da_codes[0] = mixed_codes[:, C:]
-        scales_of[0] = mixed_scales[:, C:]
+        joint_codes = at(at_slope3 + NARROW, [P, 2 * C], U32, "joint_codes")
+        joint_scales = tile([P, 2 * C], U8, "joint_scales")
+        quantize(joint_codes[:], joint_scales[:], joint[:])
+        g_codes[5] = joint_codes[:, :C]
+        g_scales[5] = joint_scales[:, :C]
+        da_codes[0] = joint_codes[:, C:]
+        da_scales[0] = joint_scales[:, C:]
         first_products(2, 5)
+
         da16[1] = at(at_da1, [P, C, PACK], BF16, "da16_1")[:]
         da_on_gpsimd(1)
         da16[4] = at(at_da4, [P, C, PACK], BF16, "da16_4")[:]
@@ -360,24 +357,18 @@ def tile_moe_bdx_mlp_relu2_kernel(
         dx_out(0, (2, 3), second_product(5, 0, (2, 3)))
         dx_out(0, (0,), second_product(4, 0, (0,)))
         late = [((0,), second_product(0, 1, (0,))), ((2, 3), second_product(1, 1, (2, 3)))]
+
         for x, e in enumerate((4, 1, 5)):
             da_codes[e] = at(at_slope5 + x * 4 * C, [P, C], U32, "da_codes%d" % e)[:]
-        for x, e in enumerate((4, 1)):
-            quantize_da(e)
-            dx_out(0, (e,), second_product(6 + x, 0, (e,)))
+        quantize_da(4)
+        nc.vector.tensor_scalar_mul(dx_slots(0, (4,)), second_product(6, 0, (4,))[:], 2.0)
+        quantize_da(1)
+        dx_out(0, (1,), second_product(7, 0, (1,)))
         for half in range(2):
-            slots = slice(half * P, (half + 1) * P)
-            quantize(da_codes[5][:, slots], scales_of[5][:, slots], da16[5][:, slots, :])
+            quantize_da(5, half_of(half))
         for half in range(2):
-            slots = slice(half * P, (half + 1) * P)
             acc = bank(2 + half, [P, P], "dx_last%d" % half)
-            one_pass(
-                acc[:],
-                w1[:, 5, 0 : 2 * P].bitcast(FP4X4),
-                s1[:, 5, 0:P],
-                da_codes[5][:, slots].bitcast(FP8X4),
-                scales_of[5][:, slots],
-            )
+            second_pass(acc[:], 0, 5, half_of(half))
             nc.vector.tensor_scalar_mul(dx[0][:, 5 * C + half * P : 5 * C + (half + 1) * P], acc[:], 2.0)
         late.append(((1,), second_product(4, 1, (1,))))
         late.append(((4, 5), second_product(2, 1, (4, 5))))
@@ -395,7 +386,7 @@ def tile_moe_bdx_mlp_relu2_kernel(
             if r == TOP - 1:
                 nc.sync.dma_start(out=out[kh * P : (kh + 1) * P, t0:t1], in_=sums[kh][r][:, t0:t1])
 
-        for kh, cut in enumerate((T // 2, T - 192)):
+        for kh, cut in enumerate((T // 2, T - LAST_PIECE)):
             for r in range(TOP):
                 fetch(kh, r, 0, cut)
                 fetch(kh, r, cut, T)

@@ -52,7 +52,9 @@ def tile_moe_bdx_mlp_relu2_kernel(
         def at(offset, shape, dtype, name):
             return placed.tile(shape, dtype, name=name, offset=offset, align_bytes=64)
 
-        at_joint = 0
+        at_dh1 = 0
+        at_a3 = at_dh1 + WIDE - LAP
+        at_joint = at_a3 + WIDE - LAP
         at_dy3 = at_joint + WIDE - LAP
         at_dh0 = at_dy3 + WIDE
         at_a1 = at_dh0 + WIDE - LAP
@@ -80,7 +82,8 @@ def tile_moe_bdx_mlp_relu2_kernel(
         s2_rows = tile([P, E // 2 * H], U8, "s2_rows")
         s2 = tile([P, E, H], U8, "s2")
         s1 = tile([P, E, K], U8, "s1")
-        a_sb = {e: tile([P, PACK, C], F32, "a_sb%d" % e) for e in range(E) if e != 1}
+        a_sb = {e: tile([P, PACK, C], F32, "a_sb%d" % e) for e in (0, 2, 4, 5)}
+        a_sb[3] = at(at_a3, [P, PACK, C], F32, "a_sb3")
         a_sb[1] = at(at_a1, [P, PACK, C], F32, "a_sb1")
 
         nc.vector.memset(s2_raw[2 * BLOCKS : 64, :].bitcast(I32), 0)
@@ -130,10 +133,11 @@ def tile_moe_bdx_mlp_relu2_kernel(
             in_=s2_raw[:].rearrange("p (b m d) -> p d b m", d=PACK, m=P),
         )
         load_gate(2, 4)
-        for e in range(2):
-            load_a(e)
-            spread_scales(e)
+        load_a(0)
         load_gate(4, E)
+        load_a(1)
+        for x in range(2):
+            spread_scales(x)
         for e in (3, 2, 4, 5):
             load_a(e)
         load_words(w1, w1_words, 0, E)
@@ -291,11 +295,9 @@ def tile_moe_bdx_mlp_relu2_kernel(
                 second_pass(acc[:, x, :], kh, e, slice(0, C))
             return acc
 
-        def dx_slots(kh, experts):
-            return dx[kh][:, experts[0] * C : (experts[-1] + 1) * C].rearrange("p (e c) -> p e c", c=C)
-
         def dx_out(kh, experts, acc):
-            nc.scalar.activation(out=dx_slots(kh, experts), in_=acc[:], func=ACT.Copy, scale=2.0)
+            dst = dx[kh][:, experts[0] * C : (experts[-1] + 1) * C].rearrange("p (e c) -> p e c", c=C)
+            nc.scalar.activation(out=dst, in_=acc[:], func=ACT.Copy, scale=2.0)
 
         for first in (0, 2, 4):
             regroup(first)
@@ -312,14 +314,14 @@ def tile_moe_bdx_mlp_relu2_kernel(
         dh_rows[0] = at(at_dh0, [P, C, PACK], F32, "dh_rows0")
         dh_out(0, 0)
         dh_out(0, 1)
-        dh_rows[1] = tile([P, C, PACK], F32, "dh_rows1")
-        dh_out(1, 0)
         quantize_g(2, 2)
         first_products(4, 2)
         first_products(6, 3)
         interleave(4, at(at_g16_4, [P, C, PACK], BF16, "g16_4")[:])
         gather(5, 1)
         make_slope_by_halves(3, at_slope3)
+        dh_rows[1] = at(at_dh1, [P, C, PACK], F32, "dh_rows1")
+        dh_out(1, 0)
         quantize_g(4, 1)
         first_products(0, 4)
         joint = at(at_joint, [P, 2 * C, PACK], BF16, "joint")
@@ -360,10 +362,9 @@ def tile_moe_bdx_mlp_relu2_kernel(
 
         for x, e in enumerate((4, 1, 5)):
             da_codes[e] = at(at_slope5 + x * 4 * C, [P, C], U32, "da_codes%d" % e)[:]
-        quantize_da(4)
-        nc.vector.tensor_scalar_mul(dx_slots(0, (4,)), second_product(6, 0, (4,))[:], 2.0)
-        quantize_da(1)
-        dx_out(0, (1,), second_product(7, 0, (1,)))
+        for x, e in enumerate((4, 1)):
+            quantize_da(e)
+            dx_out(0, (e,), second_product(6 + x, 0, (e,)))
         for half in range(2):
             quantize_da(5, half_of(half))
         for half in range(2):

@@ -13,11 +13,12 @@ FLOPS = 2 * S * H * (N + K)
 BYTES = 4 * (N * T + H * S + S + K * T) + E * H * (N + K) // 2 + E * H * (N + K) // 32 + 2 * (S + TOP * T)
 
 WIDE = PACK * C * 4
-NARROW = PACK * C * 2
 LAP = 64
-SPARE = 32
 RUN = 4
 LAST_PIECE = 192
+ORDER = (0, 2, 4, 1, 3, 5)
+WORDS_ON_VECTOR = (1, 2)
+FUSED = 4
 
 F32 = mybir.dt.float32
 BF16 = mybir.dt.bfloat16
@@ -52,117 +53,103 @@ def tile_moe_bdx_mlp_relu2_kernel(
         def at(offset, shape, dtype, name):
             return placed.tile(shape, dtype, name=name, offset=offset, align_bytes=64)
 
-        at_dh1 = 0
-        at_a3 = at_dh1 + WIDE - LAP
-        at_joint = at_a3 + WIDE - LAP
-        at_dy3 = at_joint + WIDE - LAP
-        at_dh0 = at_dy3 + WIDE
-        at_a1 = at_dh0 + WIDE - LAP
-        at_g16_2 = at_a1 + WIDE - LAP
-        at_g16_4 = at_g16_2 + LAP
-        at_da4 = at_g16_2 + WIDE
-        at_da3 = at_da4 + NARROW - LAP
-        at_da1 = at_da3 + NARROW - LAP
-        at_da2 = at_da1 + NARROW
-        at_g32 = {0: at_da3, 4: at_da2 - NARROW, 2: at_da3 + 2 * WIDE, 5: at_da3 + 2 * WIDE}
-        at_g16_0 = at_da3 + 4 * WIDE
-        at_raw4 = at_g16_0 + WIDE - LAP
-        at_slope3 = at_raw4 + NARROW
-        at_slope5 = at_slope3 + WIDE
+        at_rows = [k % 2 * WIDE for k in range(E)]
+        at_a3 = 2 * WIDE
+        at_dx = [3 * WIDE + kh * 4 * S for kh in range(K // P)]
 
         offs_sb = keep.tile([P, S // PER_COLUMN], U16, name="offs_sb")
         pos_sb = [keep.tile([P, T // PER_COLUMN], U16, name="pos_sb%d" % r) for r in range(TOP)]
-        dy = tiles(PACK - 1, [P, T + SPARE], F32, "dy")
-        dy.append(at(at_dy3, [P, T + SPARE], F32, "dy3"))
-        gate_sb = tile([P, S], F32, "gate_sb")
-        raw = {e: tile([P, 2, 2 * H], U8, "raw%d" % e) for e in (0, 2)}
-        raw[4] = at(at_raw4, [P, 2, 2 * H], U8, "raw4")
+        dy = tiles(PACK, [P, T], F32, "dy")
+        gate_sb = tile([P, E, C], F32, "gate_sb")
+        raw_sb = [tile([P, n, 2 * H], U8, "raw%d" % x) for x, n in enumerate((1, 2, 3))]
+        raw = [raw_sb[0][:, 0, :], raw_sb[1][:, 0, :], raw_sb[1][:, 1, :]] + [raw_sb[2][:, x, :] for x in range(3)]
         w1 = tile([P, E, 2 * K], U8, "w1")
         s2_raw = tile([P, E // 2 * H], U8, "s2_raw")
-        s2_rows = tile([P, E // 2 * H], U8, "s2_rows")
-        s2 = tile([P, E, H], U8, "s2")
-        s1 = tile([P, E, K], U8, "s1")
-        a_sb = {e: tile([P, PACK, C], F32, "a_sb%d" % e) for e in (0, 2, 4, 5)}
-        a_sb[3] = at(at_a3, [P, PACK, C], F32, "a_sb3")
-        a_sb[1] = at(at_a1, [P, PACK, C], F32, "a_sb1")
+        HALF = E // 2 * H
+        staged = tile([P, HALF + E * K], U8, "staged")
+        planes = [tile([P, HALF + x * E * K], U8, "planes%d" % x) for x in range(2)]
+        s2 = [planes[x][:, :HALF].rearrange("p (b n) -> p b n", n=H) for x in range(2)]
+        s1 = planes[1][:, HALF:].rearrange("p (e n) -> p e n", n=K)
+        a_sb = [tile([P, PACK, C], F32, "a_sb%d" % k) for k in range(FUSED - 1)]
+        a_sb.append(at(at_a3, [P, PACK, C], F32, "a_sb3"))
+        a_sb += [at(at_dx[kh], [P, PACK, C], F32, "a_sb%d" % (FUSED + kh)) for kh in range(K // P)]
 
         nc.vector.memset(s2_raw[2 * BLOCKS : 64, :].bitcast(I32), 0)
         nc.vector.memset(s2_raw[64:P, :].bitcast(I32), 0)
-        for d in range(PACK):
-            nc.gpsimd.memset(dy[d][:, T:], 0.0)
-        nc.gpsimd.memset(s2[:].bitcast(I32), 0)
-        nc.gpsimd.memset(s1[:].bitcast(I32), 0)
+        for x in range(2):
+            nc.gpsimd.memset(planes[x][:].bitcast(I32), 0)
 
         dy_planes = dyT.rearrange("(p d) c -> p d c", d=PACK)
         a_planes = a.rearrange("(p d) s -> p d s", d=PACK)
+        gate_rows = gate[0:P, :].rearrange("p (e c) -> p e c", c=C)
 
-        def load_gate(e0, e1):
-            nc.sync.dma_start(out=gate_sb[:, e0 * C : e1 * C], in_=gate[0:P, e0 * C : e1 * C])
+        def load_gate(experts):
+            nc.sync.dma_start(out=gate_sb[:, experts, :], in_=gate_rows[:, experts, :])
 
-        def load_a(e):
-            nc.sync.dma_start(out=a_sb[e][:], in_=a_planes[:, :, e * C : (e + 1) * C])
+        def load_a(k):
+            e = ORDER[k]
+            nc.sync.dma_start(out=a_sb[k][:], in_=a_planes[:, :, e * C : (e + 1) * C])
 
-        def load_words(dst, src, e0, e1):
+        def load_words(dst, src, experts):
             nc.sync.dma_start(
                 out=dst[:].bitcast(I32),
-                in_=src[e0:e1, 0].rearrange("e p n -> p e n").bitcast(I32),
+                in_=src[experts, 0].rearrange("e p n -> p e n").bitcast(I32),
             )
 
         def spread_scales(x):
             for q in range(BLOCKS // 4):
-                rows = s2_rows[BLOCKS * x + 4 * q : BLOCKS * x + 4 * q + 4, :]
-                nc.sync.dma_start(
-                    out=s2[32 * q : 32 * q + 4, x:E:2, :].bitcast(I32),
-                    in_=rows.rearrange("p (b n) -> p b n", n=H).bitcast(I32),
-                )
+                rows = staged[BLOCKS * x + 4 * q : BLOCKS * x + 4 * q + 4, : HALF + x * E * K]
+                nc.sync.dma_start(out=planes[x][32 * q : 32 * q + 4, :].bitcast(I32), in_=rows.bitcast(I32))
 
         nc.sync.dma_start(
             out=s2_raw[0 : 2 * BLOCKS, :].rearrange("p (b n) -> p b n", n=H).bitcast(I32),
             in_=w2_scales.rearrange("(b x) s f n -> (x s f) b n", x=2).bitcast(I32),
         )
+        load_words(raw_sb[0], w2_words, slice(0, 1))
         nc.sync.dma_start(offs_sb[:], offs)
-        load_gate(0, 1)
         for d in range(PACK):
-            nc.sync.dma_start(out=dy[d][:, :T], in_=dy_planes[:, d, :])
+            nc.sync.dma_start(out=dy[d][:], in_=dy_planes[:, d, :])
             if d == 0:
-                load_gate(1, 2)
-            else:
-                load_words(raw[2 * d - 2], w2_words, 2 * d - 2, 2 * d)
+                load_gate(slice(0, 1))
         nc.vector.tensor_copy(
-            out=s2_rows[:].rearrange("p (b d m) -> p d b m", d=PACK, m=P),
+            out=staged[:, :HALF].rearrange("p (b d m) -> p d b m", d=PACK, m=P),
             in_=s2_raw[:].rearrange("p (b m d) -> p d b m", d=PACK, m=P),
         )
-        load_gate(2, 4)
+        load_gate(slice(2, 3))
+        spread_scales(0)
+        load_words(raw_sb[1], w2_words, slice(2, 5, 2))
         load_a(0)
-        load_gate(4, E)
+        load_gate(slice(4, 5))
+        nc.sync.dma_start(
+            out=staged[BLOCKS : 2 * BLOCKS, HALF:].rearrange("p (e n) -> p e n", n=K).bitcast(I32),
+            in_=w1_scales[:, 0].rearrange("e f n -> f e n").bitcast(I32),
+        )
+        load_words(raw_sb[2], w2_words, slice(1, E, 2))
         load_a(1)
-        for x in range(2):
-            spread_scales(x)
-        for e in (3, 2, 4, 5):
-            load_a(e)
-        load_words(w1, w1_words, 0, E)
-        for r in range(4):
-            nc.sync.dma_start(
-                out=s1[r:P:32].bitcast(I32),
-                in_=w1_scales[:, 0, r:16:4, :].rearrange("e q n -> q e n").bitcast(I32),
-            )
+        load_gate(slice(1, 2))
+        load_words(w1, w1_words, slice(0, E))
+        spread_scales(1)
+        load_a(2)
+        load_gate(slice(3, 4))
+        load_a(4)
+        load_a(5)
+        load_a(3)
+        load_gate(slice(5, 6))
         for r, pos in enumerate((pos1, pos2, pos3)):
             nc.sync.dma_start(pos_sb[r][:], pos)
 
         w2 = {}
-        g32 = {}
+        rows32 = {}
         g16 = {}
-        g_codes = {}
-        g_scales = {}
-        slope = {}
-        half_slope = {}
-        dh_rows = {}
-        dh_bank = {}
+        g_codes = tiles(E, [P, C], U32, "g_codes")
+        g_scales = tiles(E, [P, C], U8, "g_scales")
         da16 = {}
-        da_codes = {}
-        scale_bytes = tile([P, S], U8, "scale_bytes")
-        da_scales = {e: scale_bytes[:, e * C : (e + 1) * C] for e in range(1, E)}
-        dx = tiles(K // P, [P, S], F32, "dx")
+        da_codes = tiles(E, [P, C], U32, "da_codes")
+        da_scales = tiles(E, [P, C], U8, "da_scales")
+        slope = {}
+        dh_bank = {}
+        dx_bank = {}
+        dx = [at(at_dx[kh], [P, S], F32, "dx%d" % kh) for kh in range(K // P)]
 
         def half_of(half):
             return slice(half * P, (half + 1) * P)
@@ -193,201 +180,163 @@ def tile_moe_bdx_mlp_relu2_kernel(
                 stop=True,
             )
 
-        def regroup(first):
-            words = tile([P, 2, 2 * H], U8, "w2_%d" % first)
-            nc.scalar.copy(
-                out=words[:].bitcast(U16).rearrange("p e (d m) -> p e d m", d=PACK),
-                in_=raw[first][:].bitcast(U16).rearrange("p e (m d) -> p e d m", d=PACK),
-            )
-            for x in range(2):
-                w2[first + x] = words[:, x, :]
+        def regroup(k):
+            w2[k] = tile([P, 2 * H], U8, "w2_%d" % k)
+            dst = w2[k][:].bitcast(U16).rearrange("p (d m) -> p d m", d=PACK)
+            src = raw[k].bitcast(U16).rearrange("p (m d) -> p d m", d=PACK)
+            if k in WORDS_ON_VECTOR:
+                nc.vector.tensor_copy(out=dst, in_=src)
+            else:
+                nc.scalar.copy(out=dst, in_=src)
 
-        def gather(first, count):
-            g32[first] = at(at_g32[first], [P, PACK, count * C], F32, "g32_%d" % first)
+        def gather(k):
+            e = ORDER[k]
+            rows32[k] = at(at_rows[k], [P, PACK, C], F32, "rows32_%d" % k)
+            entries = offs_sb[:, e * C // PER_COLUMN : (e + 1) * C // PER_COLUMN]
             for d in range(PACK):
-                step = 1 if (first, d) == (0, 0) else count
-                for x in range(0, count, step):
-                    j0, j1 = (first + x) * C, (first + x + step) * C
-                    nc.vector.tensor_tensor(
-                        g32[first][:, d, x * C : (x + step) * C],
-                        dy[d][:].indirect(offs_sb[:, j0 // PER_COLUMN : j1 // PER_COLUMN]),
-                        gate_sb[:, j0:j1],
-                        ALU.mult,
-                    )
+                if k == 0:
+                    nc.vector.tensor_tensor(rows32[k][:, d, :], dy[d][:].indirect(entries), gate_sb[:, e, :], ALU.mult)
+                else:
+                    nc.scalar.activation(rows32[k][:, d, :], dy[d][:].indirect(entries), ACT.Copy)
 
-        def interleave(first, values):
-            g16[first] = values
-            nc.scalar.copy(out=side_by_side(values), in_=from_planes(g32[first][:]))
+        def make_g(k):
+            g16[k] = tile([P, C, PACK], BF16, "g16_%d" % k)
+            if k == 0:
+                nc.scalar.copy(out=side_by_side(g16[k][:]), in_=from_planes(rows32[k][:]))
+            else:
+                weight = gate_sb[:, ORDER[k], :].unsqueeze(1).to_broadcast([P, PACK, C])
+                nc.vector.tensor_tensor(
+                    side_by_side(g16[k][:]), from_planes(rows32[k][:]), from_planes(weight), ALU.mult
+                )
 
-        def quantize_g(first, count):
-            codes = tile([P, count * C], U32, "g_codes%d" % first)
-            scales = tile([P, count * C], U8, "g_scales%d" % first)
-            quantize(codes[:], scales[:], g16[first])
-            for x in range(count):
-                g_codes[first + x] = codes[:, x * C : (x + 1) * C]
-                g_scales[first + x] = scales[:, x * C : (x + 1) * C]
-
-        def first_products(number, e):
+        def first_products(k):
+            quantize(g_codes[k][:], g_scales[k][:], g16[k][:])
             for half in range(2):
-                acc = bank(number + half, [P, PACK, P], "dh%d%d" % (e, half))
+                acc = bank(2 * (k % 2) + half, [P, PACK, P], "dh%d%d" % (k, half))
                 for d in range(PACK):
                     one_pass(
                         acc[:, d, :],
-                        w2[e][:, 2 * d * P : 2 * (d + 1) * P],
-                        s2[:, e, d * P : (d + 1) * P],
-                        g_codes[e][:, half_of(half)],
-                        g_scales[e][:, half_of(half)],
+                        w2[k][:, 2 * d * P : 2 * (d + 1) * P],
+                        s2[k // 3][:, k % 3, d * P : (d + 1) * P],
+                        g_codes[k][:, half_of(half)],
+                        g_scales[k][:, half_of(half)],
                     )
-                dh_bank[e, half] = acc
+                dh_bank[k, half] = acc
 
-        def relu(values, planes):
-            nc.scalar.activation(out=side_by_side(values), in_=from_planes(planes), func=ACT.Relu)
+        def make_slope(k):
+            slope[k] = tile([P, C, PACK], F32, "slope%d" % k)
+            nc.scalar.activation(out=side_by_side(slope[k][:]), in_=from_planes(a_sb[k][:]), func=ACT.Relu)
 
-        def make_slope(e):
-            slope[e] = tile([P, C, PACK], F32, "slope%d" % e)[:]
-            relu(slope[e], a_sb[e][:])
-            for half in range(2):
-                half_slope[e, half] = slope[e][:, half_of(half), :]
+        def make_da(k, halves=(0, 1)):
+            if k == FUSED:
+                da16[k] = at(at_a3, [P, C, PACK], BF16, "da16_placed")
+            elif k not in da16:
+                da16[k] = tile([P, C, PACK], BF16, "da16_%d" % k)
+            for half in halves:
+                dst = da16[k][:, half_of(half), :]
+                dh = by_columns(dh_bank[k, half][:])
+                if k < FUSED:
+                    saved = by_columns(a_sb[k][:, :, half_of(half)])
+                    nc.vector.scalar_tensor_tensor(dst, saved, 0.0, dh, ALU.max, ALU.mult)
+                else:
+                    nc.vector.tensor_tensor(dst, slope[k][:, half_of(half), :], dh, ALU.mult)
 
-        def make_slope_by_halves(e, offset):
-            for half in range(2):
-                half_slope[e, half] = at(offset + half * NARROW, [P, P, PACK], F32, "slope%d%d" % (e, half))[:]
-                relu(half_slope[e, half], a_sb[e][:, :, half_of(half)])
+        def quantize_da(k, slots):
+            quantize(da_codes[k][:, slots], da_scales[k][:, slots], da16[k][:, slots, :])
 
-        def dh_out(e, half):
-            nc.scalar.copy(out=dh_rows[e][:, half_of(half), :], in_=by_columns(dh_bank[e, half][:]))
-
-        def da_on_gpsimd(e):
-            nc.gpsimd.tensor_tensor(flat(da16[e]), flat(dh_rows[e][:]), flat(slope[e]), ALU.mult)
-
-        def da_on_vector(e):
-            for half in range(2):
-                nc.vector.tensor_tensor(
-                    da16[e][:, half_of(half), :], half_slope[e, half], by_columns(dh_bank[e, half][:]), ALU.mult
-                )
-
-        def da_with_relu(e):
-            for half in range(2):
-                nc.vector.scalar_tensor_tensor(
-                    da16[e][:, half_of(half), :],
-                    by_columns(a_sb[e][:, :, half_of(half)]),
-                    0.0,
-                    by_columns(dh_bank[e, half][:]),
-                    ALU.max,
-                    ALU.mult,
-                )
-
-        def quantize_da(e, slots=slice(0, C)):
-            quantize(da_codes[e][:, slots], da_scales[e][:, slots], da16[e][:, slots, :])
-
-        def second_pass(acc, kh, e, slots):
+        def second_pass(acc, kh, k, slots):
+            e = ORDER[k]
             one_pass(
                 acc,
                 w1[:, e, 2 * kh * P : 2 * (kh + 1) * P],
                 s1[:, e, kh * P : (kh + 1) * P],
-                da_codes[e][:, slots],
-                da_scales[e][:, slots],
+                da_codes[k][:, slots],
+                da_scales[k][:, slots],
             )
 
-        def second_product(number, kh, experts):
-            acc = bank(number, [P, len(experts), C], "dx%d_%d" % (kh, experts[0]))
-            for x, e in enumerate(experts):
-                second_pass(acc[:, x, :], kh, e, slice(0, C))
-            return acc
+        def dx_out(kh, column, acc):
+            dst = dx[kh][:, column : column + acc.shape[-1]]
+            nc.scalar.activation(out=dst, in_=acc, func=ACT.Copy, scale=2.0)
 
-        def dx_out(kh, experts, acc):
-            dst = dx[kh][:, experts[0] * C : (experts[-1] + 1) * C].rearrange("p (e c) -> p e c", c=C)
-            nc.scalar.activation(out=dst, in_=acc[:], func=ACT.Copy, scale=2.0)
+        def second_products(k):
+            quantize_da(k, slice(0, C))
+            dx_bank[k] = bank(4 + k, [P, K // P, C], "dx%d" % k)
+            for kh in range(K // P):
+                second_pass(dx_bank[k][:, kh, :], kh, k, slice(0, C))
 
-        for first in (0, 2, 4):
-            regroup(first)
-        gather(0, 2)
-        interleave(0, at(at_g16_0, [P, 2 * C, PACK], BF16, "g16_0")[:])
-        gather(2, 2)
-        make_slope(0)
-        make_slope(1)
-        quantize_g(0, 2)
-        first_products(0, 0)
-        first_products(2, 1)
-        interleave(2, at(at_g16_2, [P, 2 * C, PACK], BF16, "g16_2")[:])
-        gather(4, 1)
-        dh_rows[0] = at(at_dh0, [P, C, PACK], F32, "dh_rows0")
-        dh_out(0, 0)
-        dh_out(0, 1)
-        quantize_g(2, 2)
-        first_products(4, 2)
-        first_products(6, 3)
-        interleave(4, at(at_g16_4, [P, C, PACK], BF16, "g16_4")[:])
-        gather(5, 1)
-        make_slope_by_halves(3, at_slope3)
-        dh_rows[1] = at(at_dh1, [P, C, PACK], F32, "dh_rows1")
-        dh_out(1, 0)
-        quantize_g(4, 1)
-        first_products(0, 4)
-        joint = at(at_joint, [P, 2 * C, PACK], BF16, "joint")
-        interleave(5, joint[:, :C, :])
-        dh_out(1, 1)
-        make_slope(4)
-        make_slope_by_halves(5, at_slope5)
+        regroup(0)
+        gather(0)
+        gather(1)
+        make_g(0)
+        make_g(1)
+        first_products(0)
+        regroup(1)
+        gather(2)
+        first_products(1)
+        regroup(2)
+        gather(3)
+        regroup(3)
+        for k in range(E - 2):
+            make_da(k)
+            make_g(k + 2)
+            second_products(k)
+            first_products(k + 2)
+            if k + 4 < E:
+                gather(k + 4)
+                regroup(k + 4)
+        for k in range(FUSED, E):
+            make_slope(k)
+        for k in range(E - 2):
+            for kh in range(K // P):
+                dx_out(kh, ORDER[k] * C, dx_bank[k][:, kh, :])
 
-        da16[0] = joint[:, C:, :]
-        da_on_gpsimd(0)
-        da16[2] = at(at_da2, [P, C, PACK], BF16, "da16_2")[:]
-        da16[3] = at(at_da3, [P, C, PACK], BF16, "da16_3")[:]
-        da_with_relu(2)
-        da_on_vector(3)
-
-        da_codes[2] = at(at_slope3, [P, C], U32, "da_codes2")[:]
-        da_codes[3] = tile([P, C], U32, "da_codes3")[:]
-        quantize_da(2)
-        quantize_da(3)
-        joint_codes = at(at_slope3 + NARROW, [P, 2 * C], U32, "joint_codes")
-        joint_scales = tile([P, 2 * C], U8, "joint_scales")
-        quantize(joint_codes[:], joint_scales[:], joint[:])
-        g_codes[5] = joint_codes[:, :C]
-        g_scales[5] = joint_scales[:, :C]
-        da_codes[0] = joint_codes[:, C:]
-        da_scales[0] = joint_scales[:, C:]
-        first_products(2, 5)
-
-        da16[1] = at(at_da1, [P, C, PACK], BF16, "da16_1")[:]
-        da_on_gpsimd(1)
-        da16[4] = at(at_da4, [P, C, PACK], BF16, "da16_4")[:]
-        da_on_vector(4)
-        da16[5] = tile([P, C, PACK], BF16, "da16_5")[:]
-        da_on_vector(5)
-        dx_out(0, (2, 3), second_product(5, 0, (2, 3)))
-        dx_out(0, (0,), second_product(4, 0, (0,)))
-        late = [((0,), second_product(0, 1, (0,))), ((2, 3), second_product(1, 1, (2, 3)))]
-
-        for x, e in enumerate((4, 1, 5)):
-            da_codes[e] = at(at_slope5 + x * 4 * C, [P, C], U32, "da_codes%d" % e)[:]
-        for x, e in enumerate((4, 1)):
-            quantize_da(e)
-            dx_out(0, (e,), second_product(6 + x, 0, (e,)))
+        last = E - 1
+        make_da(last - 1)
+        make_da(last, (0,))
+        quantize_da(last - 1, slice(0, C))
+        early = bank(4, [P, C], "dx_early")
+        second_pass(early[:], 0, last - 1, slice(0, C))
+        dx_out(0, ORDER[last - 1] * C, early[:])
+        late = bank(5, [P, 2, C], "dx_late")
+        second_pass(late[:, 0, :], 1, last - 1, slice(0, C))
+        make_da(last, (1,))
         for half in range(2):
-            quantize_da(5, half_of(half))
+            quantize_da(last, half_of(half))
         for half in range(2):
-            acc = bank(2 + half, [P, P], "dx_last%d" % half)
-            second_pass(acc[:], 0, 5, half_of(half))
-            nc.vector.tensor_scalar_mul(dx[0][:, 5 * C + half * P : 5 * C + (half + 1) * P], acc[:], 2.0)
-        late.append(((1,), second_product(4, 1, (1,))))
-        late.append(((4, 5), second_product(2, 1, (4, 5))))
-        for experts, acc in late:
-            dx_out(1, experts, acc)
+            acc = bank(6 + half, [P, P], "dx_last%d" % half)
+            second_pass(acc[:], 0, last, half_of(half))
+            dx_out(0, ORDER[last] * C + half * P, acc[:])
+        second_pass(late[:, 1, :], 1, last, slice(0, C))
+        late_dst = dx[1][:].rearrange("p (e c) -> p e c", c=C)[:, ORDER[last - 1] : E : 2, :]
+        nc.vector.tensor_scalar_mul(late_dst, late[:], 2.0)
 
-        sums = [tiles(TOP, [P, T], F32, "sums%d_" % kh) for kh in range(K // P)]
+        sums = [tiles(TOP + 1, [P, T], F32, "sums%d_" % kh) for kh in range(K // P)]
 
-        def fetch(kh, r, t0, t1):
-            window = dx[kh][:].indirect(pos_sb[r][:, t0 // PER_COLUMN : t1 // PER_COLUMN])
-            if r == 0:
-                nc.vector.tensor_copy(sums[kh][r][:, t0:t1], window)
-            else:
-                nc.vector.tensor_tensor(sums[kh][r][:, t0:t1], window, sums[kh][r - 1][:, t0:t1], ALU.add)
-            if r == TOP - 1:
-                nc.sync.dma_start(out=out[kh * P : (kh + 1) * P, t0:t1], in_=sums[kh][r][:, t0:t1])
+        def window(kh, r, t):
+            return dx[kh][:].indirect(pos_sb[r][:, t.start // PER_COLUMN : t.stop // PER_COLUMN])
 
-        for kh, cut in enumerate((T // 2, T - LAST_PIECE)):
-            for r in range(TOP):
-                fetch(kh, r, 0, cut)
-                fetch(kh, r, cut, T)
+        def fetch(kh, r, t):
+            nc.scalar.activation(sums[kh][r][:, t], window(kh, r, t), ACT.Copy)
+
+        def fetch_add(kh, r, t, onto):
+            nc.vector.tensor_tensor(sums[kh][r][:, t], window(kh, r, t), sums[kh][onto][:, t], ALU.add)
+
+        def store(kh, r, t):
+            nc.sync.dma_start(out=out[kh * P : (kh + 1) * P, t], in_=sums[kh][r][:, t])
+
+        pieces = [(slice(0, cut), slice(cut, T)) for cut in (T // 2, T - LAST_PIECE)]
+        for kh in range(2):
+            for t in pieces[kh]:
+                fetch(kh, 0, t)
+        for t in pieces[1]:
+            fetch(1, 1, t)
+        for r in (1, 2):
+            for t in pieces[0]:
+                fetch_add(0, r, t, r - 1)
+                if r == 2:
+                    store(0, 2, t)
+        for t in pieces[1]:
+            fetch_add(1, 2, t, 0)
+        for t in pieces[1]:
+            nc.vector.tensor_tensor(sums[1][3][:, t], sums[1][2][:, t], sums[1][1][:, t], ALU.add)
+            store(1, 3, t)

@@ -15,10 +15,12 @@ BYTES = 4 * (N * T + H * S + S + K * T) + E * H * (N + K) // 2 + E * H * (N + K)
 WIDE = PACK * C * 4
 LAP = 64
 RUN = 4
-LAST_PIECE = 192
+LAST_PIECE = 160
+CHAINED = 288
 ORDER = (0, 2, 4, 1, 3, 5)
-WORDS_ON_VECTOR = (1, 2)
+WORDS_ON_VECTOR = (2, 3, 4)
 FUSED = 4
+SHARE = {2: 64, 3: 128, 4: 128, 5: 128}
 
 F32 = mybir.dt.float32
 BF16 = mybir.dt.bfloat16
@@ -55,13 +57,15 @@ def tile_moe_bdx_mlp_relu2_kernel(
 
         at_rows = [k % 2 * WIDE for k in range(E)]
         at_a3 = 2 * WIDE
+        at_g16 = {k: 3 * WIDE + 8 * S + k * WIDE // 2 for k in range(2, E)}
+        at_a = [6 * WIDE + 8 * S + k * WIDE for k in range(3)]
         at_dx = [3 * WIDE + kh * 4 * S for kh in range(K // P)]
 
         offs_sb = keep.tile([P, S // PER_COLUMN], U16, name="offs_sb")
         pos_sb = [keep.tile([P, T // PER_COLUMN], U16, name="pos_sb%d" % r) for r in range(TOP)]
         dy = tiles(PACK, [P, T], F32, "dy")
         gate_sb = tile([P, E, C], F32, "gate_sb")
-        raw_sb = [tile([P, n, 2 * H], U8, "raw%d" % x) for x, n in enumerate((1, 2, 3))]
+        raw_sb = [tile([P, 1, 2 * H], U8, "raw0"), at(at_g16[2], [P, 2, 2 * H], U8, "raw1"), tile([P, 3, 2 * H], U8, "raw2")]
         raw = [raw_sb[0][:, 0, :], raw_sb[1][:, 0, :], raw_sb[1][:, 1, :]] + [raw_sb[2][:, x, :] for x in range(3)]
         w1 = tile([P, E, 2 * K], U8, "w1")
         s2_raw = tile([P, E // 2 * H], U8, "s2_raw")
@@ -70,7 +74,7 @@ def tile_moe_bdx_mlp_relu2_kernel(
         planes = [tile([P, HALF + x * E * K], U8, "planes%d" % x) for x in range(2)]
         s2 = [planes[x][:, :HALF].rearrange("p (b n) -> p b n", n=H) for x in range(2)]
         s1 = planes[1][:, HALF:].rearrange("p (e n) -> p e n", n=K)
-        a_sb = [tile([P, PACK, C], F32, "a_sb%d" % k) for k in range(FUSED - 1)]
+        a_sb = [at(at_a[k], [P, PACK, C], F32, "a_sb%d" % k) for k in range(FUSED - 1)]
         a_sb.append(at(at_a3, [P, PACK, C], F32, "a_sb3"))
         a_sb += [at(at_dx[kh], [P, PACK, C], F32, "a_sb%d" % (FUSED + kh)) for kh in range(K // P)]
 
@@ -115,9 +119,9 @@ def tile_moe_bdx_mlp_relu2_kernel(
             out=staged[:, :HALF].rearrange("p (b d m) -> p d b m", d=PACK, m=P),
             in_=s2_raw[:].rearrange("p (b m d) -> p d b m", d=PACK, m=P),
         )
+        load_words(raw_sb[1], w2_words, slice(2, 5, 2))
         load_gate(slice(2, 3))
         spread_scales(0)
-        load_words(raw_sb[1], w2_words, slice(2, 5, 2))
         load_a(0)
         load_gate(slice(4, 5))
         nc.sync.dma_start(
@@ -181,7 +185,10 @@ def tile_moe_bdx_mlp_relu2_kernel(
             )
 
         def regroup(k):
-            w2[k] = tile([P, 2 * H], U8, "w2_%d" % k)
+            if k < 3:
+                w2[k] = tile([P, 2 * H], U8, "w2_%d" % k)
+            else:
+                w2[k] = at(at_a[k - 3], [P, 2 * H], U8, "w2_%d" % k)
             dst = w2[k][:].bitcast(U16).rearrange("p (d m) -> p d m", d=PACK)
             src = raw[k].bitcast(U16).rearrange("p (m d) -> p d m", d=PACK)
             if k in WORDS_ON_VECTOR:
@@ -195,22 +202,40 @@ def tile_moe_bdx_mlp_relu2_kernel(
             entries = offs_sb[:, e * C // PER_COLUMN : (e + 1) * C // PER_COLUMN]
             for d in range(PACK):
                 if k == 0:
-                    nc.vector.tensor_tensor(rows32[k][:, d, :], dy[d][:].indirect(entries), gate_sb[:, e, :], ALU.mult)
+                    step = P if d == PACK - 1 else C
+                    for j in range(0, C, step):
+                        nc.vector.tensor_tensor(
+                            rows32[k][:, d, j : j + step],
+                            dy[d][:].indirect(entries[:, j // PER_COLUMN : (j + step) // PER_COLUMN]),
+                            gate_sb[:, e, j : j + step],
+                            ALU.mult,
+                        )
                 else:
                     nc.scalar.activation(rows32[k][:, d, :], dy[d][:].indirect(entries), ACT.Copy)
 
         def make_g(k):
-            g16[k] = tile([P, C, PACK], BF16, "g16_%d" % k)
-            if k == 0:
-                nc.scalar.copy(out=side_by_side(g16[k][:]), in_=from_planes(rows32[k][:]))
+            if k < 2:
+                g16[k] = tile([P, C, PACK], BF16, "g16_%d" % k)
             else:
-                weight = gate_sb[:, ORDER[k], :].unsqueeze(1).to_broadcast([P, PACK, C])
+                g16[k] = at(at_g16[k], [P, C, PACK], BF16, "g16_%d" % k)
+            if k == 0:
+                for half in range(2):
+                    slots = half_of(half)
+                    nc.vector.tensor_copy(out=side_by_side(g16[k][:, slots, :]), in_=from_planes(rows32[k][:, :, slots]))
+            else:
+                cut = C - SHARE.get(k, 0)
+                if cut < C:
+                    weight = gate_sb[:, ORDER[k], cut:].unsqueeze(2).to_broadcast([P, C - cut, PACK])
+                    nc.gpsimd.tensor_tensor(g16[k][:, cut:, :], by_columns(rows32[k][:, :, cut:]), weight, ALU.mult)
+                weight = gate_sb[:, ORDER[k], :cut].unsqueeze(1).to_broadcast([P, PACK, cut])
                 nc.vector.tensor_tensor(
-                    side_by_side(g16[k][:]), from_planes(rows32[k][:]), from_planes(weight), ALU.mult
+                    side_by_side(g16[k][:, :cut, :]), from_planes(rows32[k][:, :, :cut]), from_planes(weight), ALU.mult
                 )
 
         def first_products(k):
-            quantize(g_codes[k][:], g_scales[k][:], g16[k][:])
+            step = P if k == 0 else C
+            for j in range(0, C, step):
+                quantize(g_codes[k][:, j : j + step], g_scales[k][:, j : j + step], g16[k][:, j : j + step, :])
             for half in range(2):
                 acc = bank(2 * (k % 2) + half, [P, PACK, P], "dh%d%d" % (k, half))
                 for d in range(PACK):
@@ -230,6 +255,8 @@ def tile_moe_bdx_mlp_relu2_kernel(
         def make_da(k, halves=(0, 1)):
             if k == FUSED:
                 da16[k] = at(at_a3, [P, C, PACK], BF16, "da16_placed")
+            elif k + 3 < E:
+                da16[k] = at(at_g16[k + 3], [P, C, PACK], BF16, "da16_%d" % k)
             elif k not in da16:
                 da16[k] = tile([P, C, PACK], BF16, "da16_%d" % k)
             for half in halves:
@@ -268,22 +295,22 @@ def tile_moe_bdx_mlp_relu2_kernel(
         gather(0)
         gather(1)
         make_g(0)
-        make_g(1)
         first_products(0)
+        make_g(1)
         regroup(1)
         gather(2)
-        first_products(1)
         regroup(2)
+        first_products(1)
         gather(3)
-        regroup(3)
         for k in range(E - 2):
             make_da(k)
             make_g(k + 2)
-            second_products(k)
-            first_products(k + 2)
             if k + 4 < E:
                 gather(k + 4)
-                regroup(k + 4)
+            if k + 3 < E:
+                regroup(k + 3)
+            second_products(k)
+            first_products(k + 2)
         for k in range(FUSED, E):
             make_slope(k)
         for k in range(E - 2):
@@ -297,18 +324,19 @@ def tile_moe_bdx_mlp_relu2_kernel(
         early = bank(4, [P, C], "dx_early")
         second_pass(early[:], 0, last - 1, slice(0, C))
         dx_out(0, ORDER[last - 1] * C, early[:])
-        late = bank(5, [P, 2, C], "dx_late")
-        second_pass(late[:, 0, :], 1, last - 1, slice(0, C))
         make_da(last, (1,))
+        late = [bank(3, [P, C], "dx_late0"), bank(0, [P, C], "dx_late1")]
+        second_pass(late[0][:], 1, last - 1, slice(0, C))
         for half in range(2):
             quantize_da(last, half_of(half))
         for half in range(2):
             acc = bank(6 + half, [P, P], "dx_last%d" % half)
             second_pass(acc[:], 0, last, half_of(half))
             dx_out(0, ORDER[last] * C + half * P, acc[:])
-        second_pass(late[:, 1, :], 1, last, slice(0, C))
-        late_dst = dx[1][:].rearrange("p (e c) -> p e c", c=C)[:, ORDER[last - 1] : E : 2, :]
-        nc.vector.tensor_scalar_mul(late_dst, late[:], 2.0)
+        second_pass(late[1][:], 1, last, slice(0, C))
+        for x in range(2):
+            e = ORDER[last - 1 + x]
+            nc.vector.tensor_scalar_mul(dx[1][:, e * C : (e + 1) * C], late[x][:], 2.0)
 
         sums = [tiles(TOP + 1, [P, T], F32, "sums%d_" % kh) for kh in range(K // P)]
 
@@ -324,19 +352,26 @@ def tile_moe_bdx_mlp_relu2_kernel(
         def store(kh, r, t):
             nc.sync.dma_start(out=out[kh * P : (kh + 1) * P, t], in_=sums[kh][r][:, t])
 
-        pieces = [(slice(0, cut), slice(cut, T)) for cut in (T // 2, T - LAST_PIECE)]
-        for kh in range(2):
-            for t in pieces[kh]:
-                fetch(kh, 0, t)
-        for t in pieces[1]:
-            fetch(1, 1, t)
+        chained = [slice(0, 128), slice(128, CHAINED)]
+        paired = [(0, slice(CHAINED, T)), (1, slice(0, T - LAST_PIECE)), (1, slice(T - LAST_PIECE, T))]
+
+        def add_pair(kh, t):
+            nc.vector.tensor_tensor(sums[kh][3][:, t], sums[kh][2][:, t], sums[kh][1][:, t], ALU.add)
+            store(kh, 3, t)
+
+        for t in chained:
+            fetch(0, 0, t)
+        for x in range(len(paired) + 1):
+            if x < len(paired):
+                fetch(paired[x][0], 0, paired[x][1])
+            if x > 0:
+                fetch(paired[x - 1][0], 1, paired[x - 1][1])
         for r in (1, 2):
-            for t in pieces[0]:
+            for t in chained:
                 fetch_add(0, r, t, r - 1)
-                if r == 2:
-                    store(0, 2, t)
-        for t in pieces[1]:
-            fetch_add(1, 2, t, 0)
-        for t in pieces[1]:
-            nc.vector.tensor_tensor(sums[1][3][:, t], sums[1][2][:, t], sums[1][1][:, t], ALU.add)
-            store(1, 3, t)
+        store(0, 2, slice(0, CHAINED))
+        for x in range(len(paired) + 1):
+            if x < len(paired):
+                fetch_add(paired[x][0], 2, paired[x][1], 0)
+            if x > 0:
+                add_pair(*paired[x - 1])

from contextlib import ExitStack

import concourse.mybir as mybir

K, T, E, C, H, N = 256, 512, 6, 256, 512, 512
S = E * C
P = 128
PACK = 4
TOP = 3
PER_COLUMN = 16
BLOCKS = N // 32
FLOPS = 2 * S * H * (N + K)
BYTES = 4 * (N * T + H * S + S + K * T) + E * H * (N + K) // 2 + E * H * (N + K) // 32 + 2 * (S + TOP * T)

WIDE = PACK * C * 4
LAP = 64
RUN = 4
LAST_PIECE = 160
CHAINED = 288
ORDER = (0, 2, 4, 1, 3, 5)
WORDS_ON_VECTOR = (2, 3, 4)
FUSED = 4
SHARE = {2: 64, 3: 128, 4: 128, 5: 128}

F32 = mybir.dt.float32
BF16 = mybir.dt.bfloat16
I32 = mybir.dt.int32
U32 = mybir.dt.uint32
U16 = mybir.dt.uint16
U8 = mybir.dt.uint8
FP8X4 = mybir.dt.float8_e4m3fn_x4
FP4X4 = mybir.dt.float4_e2m1fn_x4
ALU = mybir.AluOpType
ACT = mybir.ActivationFunctionType


def tile_moe_bdx_mlp_relu2_kernel(
    tc, dyT, a, w2_words, w2_scales, w1_words, w1_scales, gate, offs, pos1, pos2, pos3, out
):
    nc = tc.nc
    with ExitStack() as ctx:
        keep = ctx.enter_context(tc.tile_pool(name="keep", bufs=1))
        placed = ctx.enter_context(tc.tile_pool(name="placed", bufs=1))
        psum = ctx.enter_context(tc.psum_pool(name="psum", bufs=1))

        def bank(number, shape, name):
            return psum.tile(shape, F32, name=name, tag="bank%d" % number)

        def tile(shape, dtype, name):
            return keep.tile(shape, dtype, name=name, align_bytes=64)

        def tiles(count, shape, dtype, name):
            return [tile(shape, dtype, "%s%d" % (name, x)) for x in range(count)]

        def at(offset, shape, dtype, name):
            return placed.tile(shape, dtype, name=name, offset=offset, align_bytes=64)

        at_rows = [k % 2 * WIDE for k in range(E)]
        at_a3 = 2 * WIDE
        at_g16 = {k: 3 * WIDE + 8 * S + k * WIDE // 2 for k in range(2, E)}
        at_a = [6 * WIDE + 8 * S + k * WIDE for k in range(3)]
        at_dx = [3 * WIDE + kh * 4 * S for kh in range(K // P)]

        offs_sb = keep.tile([P, S // PER_COLUMN], U16, name="offs_sb")
        pos_sb = [keep.tile([P, T // PER_COLUMN], U16, name="pos_sb%d" % r) for r in range(TOP)]
        dy = tiles(PACK, [P, T], F32, "dy")
        gate_sb = tile([P, E, C], F32, "gate_sb")
        raw_sb = [tile([P, 1, 2 * H], U8, "raw0"), at(at_g16[2], [P, 2, 2 * H], U8, "raw1"), tile([P, 3, 2 * H], U8, "raw2")]
        raw = [raw_sb[0][:, 0, :], raw_sb[1][:, 0, :], raw_sb[1][:, 1, :]] + [raw_sb[2][:, x, :] for x in range(3)]
        w1 = tile([P, E, 2 * K], U8, "w1")
        s2_raw = tile([P, E // 2 * H], U8, "s2_raw")
        HALF = E // 2 * H
        staged = tile([P, HALF + E * K], U8, "staged")
        planes = [tile([P, HALF + x * E * K], U8, "planes%d" % x) for x in range(2)]
        s2 = [planes[x][:, :HALF].rearrange("p (b n) -> p b n", n=H) for x in range(2)]
        s1 = planes[1][:, HALF:].rearrange("p (e n) -> p e n", n=K)
        a_sb = [at(at_a[k], [P, PACK, C], F32, "a_sb%d" % k) for k in range(FUSED - 1)]
        a_sb.append(at(at_a3, [P, PACK, C], F32, "a_sb3"))
        a_sb += [at(at_dx[kh], [P, PACK, C], F32, "a_sb%d" % (FUSED + kh)) for kh in range(K // P)]

        nc.vector.memset(s2_raw[2 * BLOCKS : 64, :].bitcast(I32), 0)
        nc.vector.memset(s2_raw[64:P, :].bitcast(I32), 0)
        for x in range(2):
            nc.gpsimd.memset(planes[x][:].bitcast(I32), 0)

        dy_planes = dyT.rearrange("(p d) c -> p d c", d=PACK)
        a_planes = a.rearrange("(p d) s -> p d s", d=PACK)
        gate_rows = gate[0:P, :].rearrange("p (e c) -> p e c", c=C)

        def load_gate(experts):
            nc.sync.dma_start(out=gate_sb[:, experts, :], in_=gate_rows[:, experts, :])

        def load_a(k):
            e = ORDER[k]
            nc.sync.dma_start(out=a_sb[k][:], in_=a_planes[:, :, e * C : (e + 1) * C])

        def load_words(dst, src, experts):
            nc.sync.dma_start(
                out=dst[:].bitcast(I32),
                in_=src[experts, 0].rearrange("e p n -> p e n").bitcast(I32),
            )

        def spread_scales(x):
            for q in range(BLOCKS // 4):
                rows = staged[BLOCKS * x + 4 * q : BLOCKS * x + 4 * q + 4, : HALF + x * E * K]
                nc.sync.dma_start(out=planes[x][32 * q : 32 * q + 4, :].bitcast(I32), in_=rows.bitcast(I32))

        nc.sync.dma_start(
            out=s2_raw[0 : 2 * BLOCKS, :].rearrange("p (b n) -> p b n", n=H).bitcast(I32),
            in_=w2_scales.rearrange("(b x) s f n -> (x s f) b n", x=2).bitcast(I32),
        )
        load_words(raw_sb[0], w2_words, slice(0, 1))
        nc.sync.dma_start(offs_sb[:], offs)
        for d in range(PACK):
            nc.sync.dma_start(out=dy[d][:], in_=dy_planes[:, d, :])
            if d == 0:
                load_gate(slice(0, 1))
        nc.vector.tensor_copy(
            out=staged[:, :HALF].rearrange("p (b d m) -> p d b m", d=PACK, m=P),
            in_=s2_raw[:].rearrange("p (b m d) -> p d b m", d=PACK, m=P),
        )
        load_words(raw_sb[1], w2_words, slice(2, 5, 2))
        load_gate(slice(2, 3))
        spread_scales(0)
        load_a(0)
        load_gate(slice(4, 5))
        nc.sync.dma_start(
            out=staged[BLOCKS : 2 * BLOCKS, HALF:].rearrange("p (e n) -> p e n", n=K).bitcast(I32),
            in_=w1_scales[:, 0].rearrange("e f n -> f e n").bitcast(I32),
        )
        load_words(raw_sb[2], w2_words, slice(1, E, 2))
        load_a(1)
        load_gate(slice(1, 2))
        load_words(w1, w1_words, slice(0, E))
        spread_scales(1)
        load_a(2)
        load_gate(slice(3, 4))
        load_a(4)
        load_a(5)
        load_a(3)
        load_gate(slice(5, 6))
        for r, pos in enumerate((pos1, pos2, pos3)):
            nc.sync.dma_start(pos_sb[r][:], pos)

        w2 = {}
        rows32 = {}
        g16 = {}
        g_codes = tiles(E, [P, C], U32, "g_codes")
        g_scales = tiles(E, [P, C], U8, "g_scales")
        da16 = {}
        da_codes = tiles(E, [P, C], U32, "da_codes")
        da_scales = tiles(E, [P, C], U8, "da_scales")
        slope = {}
        dh_bank = {}
        dx_bank = {}
        dx = [at(at_dx[kh], [P, S], F32, "dx%d" % kh) for kh in range(K // P)]

        def half_of(half):
            return slice(half * P, (half + 1) * P)

        def from_planes(ap):
            return ap.rearrange("p d (c i) -> p c d i", i=RUN)

        def side_by_side(ap):
            return ap.rearrange("p (c i) d -> p c d i", i=RUN)

        def by_columns(ap):
            return ap.rearrange("p d c -> p c d")

        def flat(ap):
            return ap.rearrange("p c d -> p (c d)")

        def quantize(codes, scales, values):
            nc.vector.quantize_mx(out=codes.bitcast(FP8X4), scales=scales, in_=flat(values))

        def one_pass(acc, stationary, stationary_scales, moving, moving_scales):
            nc.tensor.matmul_mx(
                out=acc,
                lhsT=stationary.bitcast(FP4X4),
                lhsT_scale=stationary_scales,
                rhs=moving.bitcast(FP8X4),
                rhs_scale=moving_scales,
                start=True,
                stop=True,
            )

        def regroup(k):
            if k < 3:
                w2[k] = tile([P, 2 * H], U8, "w2_%d" % k)
            else:
                w2[k] = at(at_a[k - 3], [P, 2 * H], U8, "w2_%d" % k)
            dst = w2[k][:].bitcast(U16).rearrange("p (d m) -> p d m", d=PACK)
            src = raw[k].bitcast(U16).rearrange("p (m d) -> p d m", d=PACK)
            if k in WORDS_ON_VECTOR:
                nc.vector.tensor_copy(out=dst, in_=src)
            else:
                nc.scalar.copy(out=dst, in_=src)

        def gather(k):
            e = ORDER[k]
            rows32[k] = at(at_rows[k], [P, PACK, C], F32, "rows32_%d" % k)
            entries = offs_sb[:, e * C // PER_COLUMN : (e + 1) * C // PER_COLUMN]
            for d in range(PACK):
                if k == 0:
                    step = P if d == PACK - 1 else C
                    for j in range(0, C, step):
                        nc.vector.tensor_tensor(
                            rows32[k][:, d, j : j + step],
                            dy[d][:].indirect(entries[:, j // PER_COLUMN : (j + step) // PER_COLUMN]),
                            gate_sb[:, e, j : j + step],
                            ALU.mult,
                        )
                else:
                    nc.scalar.activation(rows32[k][:, d, :], dy[d][:].indirect(entries), ACT.Copy)

        def make_g(k):
            if k < 2:
                g16[k] = tile([P, C, PACK], BF16, "g16_%d" % k)
            else:
                g16[k] = at(at_g16[k], [P, C, PACK], BF16, "g16_%d" % k)
            if k == 0:
                for half in range(2):
                    slots = half_of(half)
                    nc.vector.tensor_copy(out=side_by_side(g16[k][:, slots, :]), in_=from_planes(rows32[k][:, :, slots]))
            else:
                cut = C - SHARE.get(k, 0)
                if cut < C:
                    weight = gate_sb[:, ORDER[k], cut:].unsqueeze(2).to_broadcast([P, C - cut, PACK])
                    nc.gpsimd.tensor_tensor(g16[k][:, cut:, :], by_columns(rows32[k][:, :, cut:]), weight, ALU.mult)
                weight = gate_sb[:, ORDER[k], :cut].unsqueeze(1).to_broadcast([P, PACK, cut])
                nc.vector.tensor_tensor(
                    side_by_side(g16[k][:, :cut, :]), from_planes(rows32[k][:, :, :cut]), from_planes(weight), ALU.mult
                )

        def first_products(k):
            step = P if k == 0 else C
            for j in range(0, C, step):
                quantize(g_codes[k][:, j : j + step], g_scales[k][:, j : j + step], g16[k][:, j : j + step, :])
            for half in range(2):
                acc = bank(2 * (k % 2) + half, [P, PACK, P], "dh%d%d" % (k, half))
                for d in range(PACK):
                    one_pass(
                        acc[:, d, :],
                        w2[k][:, 2 * d * P : 2 * (d + 1) * P],
                        s2[k // 3][:, k % 3, d * P : (d + 1) * P],
                        g_codes[k][:, half_of(half)],
                        g_scales[k][:, half_of(half)],
                    )
                dh_bank[k, half] = acc

        def make_slope(k):
            slope[k] = tile([P, C, PACK], F32, "slope%d" % k)
            nc.scalar.activation(out=side_by_side(slope[k][:]), in_=from_planes(a_sb[k][:]), func=ACT.Relu)

        def make_da(k, halves=(0, 1)):
            if k == FUSED:
                da16[k] = at(at_a3, [P, C, PACK], BF16, "da16_placed")
            elif k + 3 < E:
                da16[k] = at(at_g16[k + 3], [P, C, PACK], BF16, "da16_%d" % k)
            elif k not in da16:
                da16[k] = tile([P, C, PACK], BF16, "da16_%d" % k)
            for half in halves:
                dst = da16[k][:, half_of(half), :]
                dh = by_columns(dh_bank[k, half][:])
                if k < FUSED:
                    saved = by_columns(a_sb[k][:, :, half_of(half)])
                    nc.vector.scalar_tensor_tensor(dst, saved, 0.0, dh, ALU.max, ALU.mult)
                else:
                    nc.vector.tensor_tensor(dst, slope[k][:, half_of(half), :], dh, ALU.mult)

        def quantize_da(k, slots):
            quantize(da_codes[k][:, slots], da_scales[k][:, slots], da16[k][:, slots, :])

        def second_pass(acc, kh, k, slots):
            e = ORDER[k]
            one_pass(
                acc,
                w1[:, e, 2 * kh * P : 2 * (kh + 1) * P],
                s1[:, e, kh * P : (kh + 1) * P],
                da_codes[k][:, slots],
                da_scales[k][:, slots],
            )

        def dx_out(kh, column, acc):
            dst = dx[kh][:, column : column + acc.shape[-1]]
            nc.scalar.activation(out=dst, in_=acc, func=ACT.Copy, scale=2.0)

        def second_products(k):
            quantize_da(k, slice(0, C))
            dx_bank[k] = bank(4 + k, [P, K // P, C], "dx%d" % k)
            for kh in range(K // P):
                second_pass(dx_bank[k][:, kh, :], kh, k, slice(0, C))

        regroup(0)
        gather(0)
        gather(1)
        make_g(0)
        first_products(0)
        make_g(1)
        regroup(1)
        gather(2)
        regroup(2)
        first_products(1)
        gather(3)
        for k in range(E - 2):
            make_da(k)
            make_g(k + 2)
            if k + 4 < E:
                gather(k + 4)
            if k + 3 < E:
                regroup(k + 3)
            second_products(k)
            first_products(k + 2)
        for k in range(FUSED, E):
            make_slope(k)
        for k in range(E - 2):
            for kh in range(K // P):
                dx_out(kh, ORDER[k] * C, dx_bank[k][:, kh, :])

        last = E - 1
        make_da(last - 1)
        make_da(last, (0,))
        quantize_da(last - 1, slice(0, C))
        early = bank(4, [P, C], "dx_early")
        second_pass(early[:], 0, last - 1, slice(0, C))
        dx_out(0, ORDER[last - 1] * C, early[:])
        make_da(last, (1,))
        late = [bank(3, [P, C], "dx_late0"), bank(0, [P, C], "dx_late1")]
        second_pass(late[0][:], 1, last - 1, slice(0, C))
        for half in range(2):
            quantize_da(last, half_of(half))
        for half in range(2):
            acc = bank(6 + half, [P, P], "dx_last%d" % half)
            second_pass(acc[:], 0, last, half_of(half))
            dx_out(0, ORDER[last] * C + half * P, acc[:])
        second_pass(late[1][:], 1, last, slice(0, C))
        for x in range(2):
            e = ORDER[last - 1 + x]
            nc.vector.tensor_scalar_mul(dx[1][:, e * C : (e + 1) * C], late[x][:], 2.0)

        sums = [tiles(TOP + 1, [P, T], F32, "sums%d_" % kh) for kh in range(K // P)]

        def window(kh, r, t):
            return dx[kh][:].indirect(pos_sb[r][:, t.start // PER_COLUMN : t.stop // PER_COLUMN])

        def fetch(kh, r, t):
            nc.scalar.activation(sums[kh][r][:, t], window(kh, r, t), ACT.Copy)

        def fetch_add(kh, r, t, onto):
            nc.vector.tensor_tensor(sums[kh][r][:, t], window(kh, r, t), sums[kh][onto][:, t], ALU.add)

        def store(kh, r, t):
            nc.sync.dma_start(out=out[kh * P : (kh + 1) * P, t], in_=sums[kh][r][:, t])

        chained = [slice(0, 128), slice(128, CHAINED)]
        paired = [(0, slice(CHAINED, T)), (1, slice(0, T - LAST_PIECE)), (1, slice(T - LAST_PIECE, T))]

        def add_pair(kh, t):
            nc.vector.tensor_tensor(sums[kh][3][:, t], sums[kh][2][:, t], sums[kh][1][:, t], ALU.add)
            store(kh, 3, t)

        for t in chained:
            fetch(0, 0, t)
        for x in range(len(paired) + 1):
            if x < len(paired):
                fetch(paired[x][0], 0, paired[x][1])
            if x > 0:
                fetch(paired[x - 1][0], 1, paired[x - 1][1])
        for r in (1, 2):
            for t in chained:
                fetch_add(0, r, t, r - 1)
        store(0, 2, slice(0, CHAINED))
        for x in range(len(paired) + 1):
            if x < len(paired):
                fetch_add(paired[x][0], 2, paired[x][1], 0)
            if x > 0:
                add_pair(*paired[x - 1])
